import numpy as np
import ml_dtypes


def mxq(x, axis, fmt="e4m3"):
    dtype, down = {"e4m3": (ml_dtypes.float8_e4m3fn, 7), "e5m2": (ml_dtypes.float8_e5m2, 14)}[fmt]
    v = np.moveaxis(np.asarray(x, np.float32).astype(ml_dtypes.bfloat16).astype(np.float64), axis, -1)
    blocks = v.reshape(v.shape[:-1] + (-1, 32))
    amax = np.abs(blocks).max(-1, keepdims=True)
    byte = np.maximum(np.where(amax > 0, np.frexp(amax)[1] - 1 + 127, 0) - down, 1)
    scale = np.exp2(byte - 127.0)
    codes = (blocks / scale).astype(np.float32).astype(dtype).astype(np.float64)
    return np.moveaxis((codes * scale).reshape(v.shape), -1, axis)


WIDE = False


def mx_kscale(k):
    if not WIDE:
        return np.ones(k)
    levels = np.array([10, -10, 5, -5, 0])
    if k % 512:
        return np.exp2(np.random.permutation(np.resize(levels, k // 32))).repeat(32)
    a = np.empty((k // 512, 16))
    for p in range(k // 512):
        a[p, :8] = np.random.permutation(np.resize(levels, 8))
        for g in range(8):
            far = levels[np.abs(levels - a[p, g]) >= 10]
            a[p, g + 8] = far[np.random.randint(len(far))]
    return np.exp2(a.ravel()).repeat(32)


def f64(x):
    return np.asarray(x).astype(np.float64)


def striped(idx):
    return np.tile(idx.reshape(-1, 16).T, (8, 1)).astype(np.uint16)


def unstriped(offs):
    return offs[:16].T.reshape(-1).astype(np.int64)


E2M1 = np.array([0.0, 0.5, 1.0, 1.5, 2.0, 3.0, 4.0, 6.0, -0.0, -0.5, -1.0, -1.5, -2.0, -3.0, -4.0, -6.0])


def pack_weight(w, fmt):
    k, n = w.shape
    w = f64(np.asarray(w, np.float32).astype(ml_dtypes.bfloat16)).reshape(k // 32, 32, n)
    amax = np.abs(w).max(1)
    if fmt == "e4m3":
        byte = np.frexp(amax)[1] - 1 + 127 - 7
    else:
        mant, ex = np.frexp(amax / 6.0)
        byte = np.where(mant > 0.5, ex, ex - 1) + 127
    byte = np.clip(np.where(amax > 0, byte, 1), 1, 254)
    scaled = (w * np.exp2(127.0 - byte)[:, None, :]).reshape(k, n).astype(np.float32)
    by_word = np.ascontiguousarray(scaled.reshape(k // 512, 128, 4, n).transpose(0, 1, 3, 2))
    if fmt == "e4m3":
        words = by_word.astype(ml_dtypes.float8_e4m3fn).view(np.uint8)
    else:
        c = by_word.astype(ml_dtypes.float4_e2m1fn).view(np.uint8) & 0xF
        words = (c[..., 0::2] | (c[..., 1::2] << 4)).reshape(k // 512, 128, 2 * n)
    return np.ascontiguousarray(words), np.ascontiguousarray(byte.astype(np.uint8).reshape(k // 512, 16, n))


def unpack_weight(words, scales, fmt):
    g, _, n = scales.shape
    words = np.ascontiguousarray(words).reshape(g, 128, n, -1)
    if fmt == "e4m3":
        vals = words.view(ml_dtypes.float8_e4m3fn).astype(np.float64)
    else:
        nib = np.empty((g, 128, n, 4), np.uint8)
        nib[..., 0::2] = words & 0xF
        nib[..., 1::2] = words >> 4
        vals = E2M1[nib]
    vals = vals * np.repeat(np.exp2(scales.astype(np.float64) - 127.0), 8, axis=1)[..., None]
    return vals.transpose(0, 1, 3, 2).reshape(g * 512, n)


def gelu(v):
    return 0.5 * v * (1.0 + np.tanh(np.sqrt(2.0 / np.pi) * (v + 0.044715 * v**3)))


K, H, T, S = 1024, 512, 2048, 1024

def setup_inputs():
    n = np.random.standard_normal
    s = mx_kscale(K)[:, None]
    u = mx_kscale(H)[:, None]
    tab_words, tab_scales = pack_weight(n((K, T)) * s, "e4m3")
    offs = striped(np.random.permutation(T)[:S])
    w = (n((K, H)) / np.sqrt(K) / s / u.T).astype(np.float32)
    e = (np.random.uniform(0.7, 1.4, H) * u[:, 0]).astype(np.float32)
    w4_words, w4_scales = pack_weight(0.6 * n((K, K)) / np.sqrt(K) / s / s.T, "e2m1")
    gT = n((K, T)).astype(np.float32)
    d = (np.random.uniform(0.5, 1.5, K) * s[:, 0]).astype(np.float32)
    return {"tab_words": tab_words, "tab_scales": tab_scales, "offs": offs,
            "w": w, "e": e, "w4_words": w4_words, "w4_scales": w4_scales,
            "gT": gT, "d": d}

def reference(tab_words, tab_scales, offs, w, e, w4_words, w4_scales, gT, d):
    v = unpack_weight(tab_words, tab_scales, "e4m3")[:, unstriped(offs)]
    w4 = unpack_weight(w4_words, w4_scales, "e2m1")
    a = f64(e)[:, None] * (mxq(f64(w), 0, "e4m3").T @ v)
    act = 0.5 * a * (1.0 + np.tanh(np.sqrt(2.0 / np.pi) * (a + 0.044715 * a * a * a)))
    h = f64(e)[:, None] * act
    y = mxq(f64(w).T, 0, "e4m3").T @ mxq(h, 0, "e4m3") + w4.T @ v
    g = f64(gT)[:, unstriped(offs)]
    new = g - f64(d)[:, None] * y
    out = f64(gT).copy()
    out[:, unstriped(offs)] = new
    return out

@@ -1,0 +1,232 @@
+from contextlib import ExitStack
+
+import concourse.mybir as mybir
+from concourse.masks import make_identity
+
+K, H, T, S = 1024, 512, 2048, 1024
+FLOPS = 2 * S * (K * H + H * K + K * K)
+
+F32 = mybir.dt.float32
+BF16 = mybir.dt.bfloat16
+I32 = mybir.dt.int32
+U32 = mybir.dt.uint32
+U16 = mybir.dt.uint16
+U8 = mybir.dt.uint8
+FP8X4 = mybir.dt.float8_e4m3fn_x4
+FP4X4 = mybir.dt.float4_e2m1fn_x4
+ACT = mybir.ActivationFunctionType
+ADD = mybir.AluOpType.add
+
+P = 128
+PACK = 4
+K_PASS = P * PACK
+PASSES = K // K_PASS
+BANK = 512
+HALVES = S // BANK
+ROW_TILES = K // P
+QUADS = 4
+LEAD = 2
+
+
+def tile_list_tied_vessel_residual_kernel(tc, tab_words, tab_scales, offs, w, e, w4_words, w4_scales, gT, d, out):
+    nc = tc.nc
+    with ExitStack() as ctx:
+        keep = ctx.enter_context(tc.tile_pool(name="keep", bufs=1))
+        ring = ctx.enter_context(tc.tile_pool(name="ring", bufs=3))
+        psum = ctx.enter_context(tc.psum_pool(name="psum", bufs=1))
+
+        def held(name, shape, dtype):
+            return keep.tile(shape, dtype, name=name, align_bytes=64)
+
+        offsets = held("offsets", [P, S // 16], U16)
+        tab_s = held("tab_s", [P, T], U8)
+        tab_w = [held(f"tab_w{a}", [P, T], I32) for a in range(PASSES)]
+        w_raw = [held(f"w_raw{a}", [P, PACK * H], F32) for a in range(PASSES)]
+        state = [held(f"state{m}", [P, T], F32) for m in range(ROW_TILES)]
+        picked = [held(f"picked{m}", [P, S], F32) for m in range(ROW_TILES)]
+        w4_w = held("w4_w", [P, PASSES, 2 * K], U8)
+        w4_s = held("w4_s", [P, PASSES, K], U8)
+        vec_rows = held("vec_rows", [P, P], F32)
+        ident = held("ident", [P, P], F32)
+        v_w = [held(f"v_w{a}", [P, S], U32) for a in range(PASSES)]
+        v_s = held("v_s", [P, S], U8)
+        v_s1 = held("v_s1", [P, S], U8)
+        enc_in = [held(f"enc_in{a}", [P, H * PACK], BF16) for a in range(PASSES)]
+        enc_w = [held(f"enc_w{a}", [P, H], U32) for a in range(PASSES)]
+        enc_s = [held(f"enc_s{a}", [P, H], U8) for a in range(PASSES)]
+        dec_in = [held(f"dec_in{a}", [P, K_PASS * PACK], BF16) for a in range(PASSES)]
+        dec_w = [held(f"dec_w{a}", [P, K_PASS], U32) for a in range(PASSES)]
+        dec_s = [held(f"dec_s{a}", [P, K_PASS], U8) for a in range(PASSES)]
+        h_rows = [held(f"h_rows{b}", [P, PACK * BANK], BF16) for b in range(HALVES)]
+        h_in = [held(f"h_in{b}", [P, BANK * PACK], BF16) for b in range(HALVES)]
+        h_w = [held(f"h_w{b}", [P, BANK], U32) for b in range(HALVES)]
+        h_s = [held(f"h_s{b}", [P, BANK], U8) for b in range(HALVES)]
+        neg_d = held("neg_d", [P, ROW_TILES], F32)
+        e_cols = held("e_cols", [P, PACK], F32)
+        warm = held("warm", [P, 1], F32)
+
+        nc.vector.memset(tab_s[:].bitcast(I32), 0)
+        nc.gpsimd.memset(vec_rows[:], 0.0)
+        make_identity(nc, ident[:])
+        nc.gpsimd.memset(w4_s[:].rearrange("p a n -> p (a n)").bitcast(I32), 0)
+        nc.gpsimd.memset(v_s1[:].bitcast(I32), 0)
+
+        def load_table(a):
+            nc.sync.dma_start(out=tab_w[a][:], in_=tab_words[a].rearrange("p t i -> p (t i)").bitcast(I32))
+
+        def load_w(a):
+            rows = w[a * K_PASS : (a + 1) * K_PASS, :]
+            nc.sync.dma_start(out=w_raw[a][:], in_=rows.rearrange("(p i) r -> p (i r)", i=PACK))
+
+        def load_state(m):
+            nc.sync.dma_start(out=state[m][:], in_=gT[m * P : (m + 1) * P, :])
+
+        nc.sync.dma_start(offsets[:], offs)
+        load_table(0)
+        for q in range(QUADS):
+            nc.sync.dma_start(
+                out=tab_s[32 * q : 32 * q + 4 * PASSES, :].bitcast(I32),
+                in_=tab_scales[:, 4 * q : 4 * q + 4, :].bitcast(I32),
+            )
+        load_table(1)
+        load_w(0)
+        load_state(0)
+        load_w(1)
+        nc.sync.dma_start(out=vec_rows[0:ROW_TILES, :], in_=d.rearrange("(m p) -> m p", p=P))
+        nc.sync.dma_start(
+            out=vec_rows[ROW_TILES : ROW_TILES + PACK, :].rearrange("t (b s) -> t b s", s=8),
+            in_=e.rearrange("(b t s) -> t b s", t=PACK, s=8),
+        )
+        load_state(1)
+        load_state(2)
+        load_state(3)
+        nc.sync.dma_start(out=w4_w[:].bitcast(I32), in_=w4_words.rearrange("a p c -> p a c").bitcast(I32))
+        for q in range(QUADS):
+            nc.sync.dma_start(
+                out=w4_s[32 * q : 32 * q + 4, :, :].bitcast(I32),
+                in_=w4_scales[:, 4 * q : 4 * q + 4, :].rearrange("a r n -> r a n").bitcast(I32),
+            )
+        for m in range(4, ROW_TILES):
+            load_state(m)
+
+        nc.scalar.activation(out=warm[:], in_=ident[:, 0:1], func=ACT.Gelu_apprx_tanh)
+
+        def pick_words(a):
+            nc.vector.tensor_copy(v_w[a][:], tab_w[a][:].bitcast(U32).indirect(offsets[:]))
+
+        pick_words(0)
+        nc.vector.tensor_copy(v_s[:], tab_s[:].indirect(offsets[:]))
+        nc.gpsimd.dma_start(out=v_s1[0:112, :].bitcast(I32), in_=v_s[4:116, :].bitcast(I32))
+        pick_words(1)
+
+        def pick_state(m):
+            nc.vector.tensor_copy(picked[m][:], state[m][:].indirect(offsets[:]))
+
+        def quantize(codes, scales, grouped):
+            nc.vector.quantize_mx(out=codes[:].bitcast(FP8X4), scales=scales[:], in_=grouped[:])
+
+        def cast_w(a):
+            nc.scalar.copy(
+                out=enc_in[a][:].rearrange("p (t b s i) -> p b t s i", t=PACK, s=8, i=PACK),
+                in_=w_raw[a][:].rearrange("p (i b t s) -> p b t s i", i=PACK, t=PACK, s=8),
+            )
+
+        def turn_w(a):
+            words = enc_in[a][:].bitcast(F32).rearrange("p (t c u) -> p t c u", t=PACK, u=2)
+            for u in range(2):
+                turned = psum.tile([P, PACK, P], F32, name="turned", tag="turned", bufs=2)
+                for t in range(PACK):
+                    nc.tensor.transpose(turned[:, t, :], words[:, t, :, u], ident[:])
+                nc.scalar.copy(
+                    out=dec_in[a][:].rearrange("c (p u x t) -> c p u x t", u=2, x=2, t=PACK)[:, :, u, :, :],
+                    in_=turned[:].rearrange("c t p -> c (t p)").bitcast(BF16).rearrange("c (t p x) -> c p x t", t=PACK, x=2),
+                )
+
+        cast_w(0)
+        pick_state(0)
+        quantize(enc_w[0], enc_s[0], enc_in[0])
+        turn_w(0)
+        cast_w(1)
+
+        vec_cols = psum.tile([P, PACK, P], F32, name="vec_cols", tag="turned", bufs=2)
+        nc.tensor.transpose(vec_cols[:, 0, :], vec_rows[:], ident[:])
+        nc.scalar.copy(out=e_cols[:], in_=vec_cols[:, 0, ROW_TILES : ROW_TILES + PACK])
+        nc.scalar.activation(out=neg_d[:], in_=vec_cols[:, 0, 0:ROW_TILES], func=ACT.Copy, scale=-1.0)
+
+        pick_state(1)
+        quantize(dec_w[0], dec_s[0], dec_in[0])
+        quantize(enc_w[1], enc_s[1], enc_in[1])
+        turn_w(1)
+
+        def encode(b):
+            cols = slice(b * BANK, (b + 1) * BANK)
+            for t in range(PACK):
+                units = slice(t * P, (t + 1) * P)
+                acc = psum.tile([P, BANK], F32, name="acc", tag="acc", bufs=3)
+                for a in range(PASSES):
+                    nc.tensor.matmul_mx(
+                        out=acc[:],
+                        lhsT=enc_w[a][:, units].bitcast(FP8X4),
+                        lhsT_scale=enc_s[a][:, units],
+                        rhs=v_w[a][:, cols].bitcast(FP8X4),
+                        rhs_scale=v_s[4 * a : P, cols],
+                        start=(a == 0),
+                        stop=(a == PASSES - 1),
+                    )
+                act = ring.tile([P, BANK], F32, name="act", tag="act")
+                nc.scalar.activation(out=act[:], in_=acc[:], func=ACT.Gelu_apprx_tanh, scale=e_cols[:, t : t + 1])
+                nc.scalar.activation(
+                    out=h_rows[b][:, t * BANK : (t + 1) * BANK], in_=act[:], func=ACT.Copy, scale=e_cols[:, t : t + 1]
+                )
+            nc.scalar.copy(
+                out=h_in[b][:].rearrange("p (c x t) -> p c t x", x=4, t=PACK),
+                in_=h_rows[b][:].rearrange("p (t c x) -> p c t x", t=PACK, x=4),
+            )
+
+        def decode(m, b):
+            cols = slice(b * BANK, (b + 1) * BANK)
+            y = psum.tile([P, BANK], F32, name="y", tag="y", bufs=3)
+            for a in range(PASSES):
+                plane = v_s if a == 0 else v_s1
+                nc.tensor.matmul_mx(
+                    out=y[:],
+                    lhsT=w4_w[:, a, 2 * m * P : 2 * (m + 1) * P].bitcast(FP4X4),
+                    lhsT_scale=w4_s[:, a, m * P : (m + 1) * P],
+                    rhs=v_w[a][:, cols].bitcast(FP8X4),
+                    rhs_scale=plane[:, cols],
+                    start=(a == 0),
+                    stop=False,
+                )
+            a, first = divmod(m * P, K_PASS)
+            nc.tensor.matmul_mx(
+                out=y[:],
+                lhsT=dec_w[a][:, first : first + P].bitcast(FP8X4),
+                lhsT_scale=dec_s[a][:, first : first + P],
+                rhs=h_w[b][:].bitcast(FP8X4),
+                rhs_scale=h_s[b][:],
+                start=False,
+                stop=True,
+            )
+            step = ring.tile([P, BANK], F32, name="step", tag="step")
+            nc.scalar.activation(out=step[:], in_=y[:], func=ACT.Copy, scale=neg_d[:, m : m + 1])
+            window = state[m][:].indirect(offsets[:, b * BANK // 16 : (b + 1) * BANK // 16])
+            nc.vector.tensor_tensor(window, picked[m][:, cols], step[:], ADD)
+            if b == HALVES - 1:
+                nc.sync.dma_start(out=out[m * P : (m + 1) * P, :], in_=state[m][:])
+
+        encode(0)
+        pick_state(2)
+        quantize(dec_w[1], dec_s[1], dec_in[1])
+        pick_state(3)
+        pick_state(4)
+        quantize(h_w[0], h_s[0], h_in[0])
+        for m in range(LEAD):
+            decode(m, 0)
+        encode(1)
+        for m in range(5, ROW_TILES):
+            pick_state(m)
+        quantize(h_w[1], h_s[1], h_in[1])
+        for m in range(ROW_TILES):
+            if m + LEAD < ROW_TILES:
+                decode(m + LEAD, 0)
+            decode(m, 1)

@@ -24,8 +24,11 @@ PASSES = K // K_PASS
 BANK = 512
 HALVES = S // BANK
 ROW_TILES = K // P
+LAST = ROW_TILES - 1
 QUADS = 4
-LEAD = 2
+RUN = 8
+SHIFT_ROWS = 112
+D_AFTER = 6
 
 
 def tile_list_tied_vessel_residual_kernel(tc, tab_words, tab_scales, offs, w, e, w4_words, w4_scales, gT, d, out):
@@ -35,18 +38,19 @@ def tile_list_tied_vessel_residual_kernel(tc, tab_words, tab_scales, offs, w, e,
         ring = ctx.enter_context(tc.tile_pool(name="ring", bufs=3))
         psum = ctx.enter_context(tc.psum_pool(name="psum", bufs=1))
 
-        def held(name, shape, dtype):
-            return keep.tile(shape, dtype, name=name, align_bytes=64)
+        def held(name, shape, dtype, on=None):
+            return keep.tile(shape, dtype, name=name, tag=on or name, align_bytes=64)
 
         offsets = held("offsets", [P, S // 16], U16)
         tab_s = held("tab_s", [P, T], U8)
         tab_w = [held(f"tab_w{a}", [P, T], I32) for a in range(PASSES)]
         w_raw = [held(f"w_raw{a}", [P, PACK * H], F32) for a in range(PASSES)]
         state = [held(f"state{m}", [P, T], F32) for m in range(ROW_TILES)]
-        picked = [held(f"picked{m}", [P, S], F32) for m in range(ROW_TILES)]
+        picked = [held(f"picked{m}", [P, S], F32) for m in range(LAST)]
         w4_w = held("w4_w", [P, PASSES, 2 * K], U8)
         w4_s = held("w4_s", [P, PASSES, K], U8)
-        vec_rows = held("vec_rows", [P, P], F32)
+        e_rows = held("e_rows", [P, P], F32)
+        d_rows = held("d_rows", [P, P], F32)
         ident = held("ident", [P, P], F32)
         v_w = [held(f"v_w{a}", [P, S], U32) for a in range(PASSES)]
         v_s = held("v_s", [P, S], U8)
@@ -54,22 +58,22 @@ def tile_list_tied_vessel_residual_kernel(tc, tab_words, tab_scales, offs, w, e,
         enc_in = [held(f"enc_in{a}", [P, H * PACK], BF16) for a in range(PASSES)]
         enc_w = [held(f"enc_w{a}", [P, H], U32) for a in range(PASSES)]
         enc_s = [held(f"enc_s{a}", [P, H], U8) for a in range(PASSES)]
-        dec_in = [held(f"dec_in{a}", [P, K_PASS * PACK], BF16) for a in range(PASSES)]
-        dec_w = [held(f"dec_w{a}", [P, K_PASS], U32) for a in range(PASSES)]
-        dec_s = [held(f"dec_s{a}", [P, K_PASS], U8) for a in range(PASSES)]
+        dec_s = held("dec_s", [P, K], U8)
         h_rows = [held(f"h_rows{b}", [P, PACK * BANK], BF16) for b in range(HALVES)]
         h_in = [held(f"h_in{b}", [P, BANK * PACK], BF16) for b in range(HALVES)]
-        h_w = [held(f"h_w{b}", [P, BANK], U32) for b in range(HALVES)]
         h_s = [held(f"h_s{b}", [P, BANK], U8) for b in range(HALVES)]
         neg_d = held("neg_d", [P, ROW_TILES], F32)
         e_cols = held("e_cols", [P, PACK], F32)
         warm = held("warm", [P, 1], F32)
+        zero = held("zero", [P, 1], F32)
 
-        nc.vector.memset(tab_s[:].bitcast(I32), 0)
-        nc.gpsimd.memset(vec_rows[:], 0.0)
+        nc.gpsimd.memset(tab_s[:].bitcast(I32), 0)
+        nc.vector.memset(zero[:], 0.0)
+        nc.vector.memset(e_rows[:], 0.0)
+        nc.vector.memset(d_rows[:], 0.0)
+        nc.vector.memset(w4_s[:].rearrange("p a n -> p (a n)").bitcast(I32), 0)
+        nc.vector.memset(v_s1[:].bitcast(I32), 0)
         make_identity(nc, ident[:])
-        nc.gpsimd.memset(w4_s[:].rearrange("p a n -> p (a n)").bitcast(I32), 0)
-        nc.gpsimd.memset(v_s1[:].bitcast(I32), 0)
 
         def load_table(a):
             nc.sync.dma_start(out=tab_w[a][:], in_=tab_words[a].rearrange("p t i -> p (t i)").bitcast(I32))
@@ -88,36 +92,30 @@ def tile_list_tied_vessel_residual_kernel(tc, tab_words, tab_scales, offs, w, e,
                 out=tab_s[32 * q : 32 * q + 4 * PASSES, :].bitcast(I32),
                 in_=tab_scales[:, 4 * q : 4 * q + 4, :].bitcast(I32),
             )
-        load_table(1)
         load_w(0)
-        load_state(0)
-        load_w(1)
-        nc.sync.dma_start(out=vec_rows[0:ROW_TILES, :], in_=d.rearrange("(m p) -> m p", p=P))
+        load_table(1)
         nc.sync.dma_start(
-            out=vec_rows[ROW_TILES : ROW_TILES + PACK, :].rearrange("t (b s) -> t b s", s=8),
-            in_=e.rearrange("(b t s) -> t b s", t=PACK, s=8),
+            out=e_rows[0:PACK, :].rearrange("t (b s) -> t b s", s=RUN),
+            in_=e.rearrange("(b t s) -> t b s", t=PACK, s=RUN),
         )
-        load_state(1)
-        load_state(2)
-        load_state(3)
-        nc.sync.dma_start(out=w4_w[:].bitcast(I32), in_=w4_words.rearrange("a p c -> p a c").bitcast(I32))
+        load_w(1)
+        for m in range(D_AFTER):
+            load_state(m)
+        nc.sync.dma_start(out=d_rows[0:ROW_TILES, :], in_=d.rearrange("(m p) -> m p", p=P))
+        for m in range(D_AFTER, LAST):
+            load_state(m)
         for q in range(QUADS):
             nc.sync.dma_start(
                 out=w4_s[32 * q : 32 * q + 4, :, :].bitcast(I32),
                 in_=w4_scales[:, 4 * q : 4 * q + 4, :].rearrange("a r n -> r a n").bitcast(I32),
             )
-        for m in range(4, ROW_TILES):
-            load_state(m)
+        nc.sync.dma_start(out=w4_w[:].bitcast(I32), in_=w4_words.rearrange("a p c -> p a c").bitcast(I32))
+        load_state(LAST)
 
-        nc.scalar.activation(out=warm[:], in_=ident[:, 0:1], func=ACT.Gelu_apprx_tanh)
+        nc.scalar.activation(out=warm[:], in_=zero[:], func=ACT.Gelu_apprx_tanh)
 
         def pick_words(a):
             nc.vector.tensor_copy(v_w[a][:], tab_w[a][:].bitcast(U32).indirect(offsets[:]))
-
-        pick_words(0)
-        nc.vector.tensor_copy(v_s[:], tab_s[:].indirect(offsets[:]))
-        nc.gpsimd.dma_start(out=v_s1[0:112, :].bitcast(I32), in_=v_s[4:116, :].bitcast(I32))
-        pick_words(1)
 
         def pick_state(m):
             nc.vector.tensor_copy(picked[m][:], state[m][:].indirect(offsets[:]))
@@ -127,36 +125,24 @@ def tile_list_tied_vessel_residual_kernel(tc, tab_words, tab_scales, offs, w, e,
 
         def cast_w(a):
             nc.scalar.copy(
-                out=enc_in[a][:].rearrange("p (t b s i) -> p b t s i", t=PACK, s=8, i=PACK),
-                in_=w_raw[a][:].rearrange("p (i b t s) -> p b t s i", i=PACK, t=PACK, s=8),
+                out=enc_in[a][:].rearrange("p (t b s i) -> p b t s i", t=PACK, s=RUN, i=PACK),
+                in_=w_raw[a][:].rearrange("p (i b t s) -> p b t s i", i=PACK, t=PACK, s=RUN),
             )
 
-        def turn_w(a):
-            words = enc_in[a][:].bitcast(F32).rearrange("p (t c u) -> p t c u", t=PACK, u=2)
-            for u in range(2):
-                turned = psum.tile([P, PACK, P], F32, name="turned", tag="turned", bufs=2)
-                for t in range(PACK):
-                    nc.tensor.transpose(turned[:, t, :], words[:, t, :, u], ident[:])
-                nc.scalar.copy(
-                    out=dec_in[a][:].rearrange("c (p u x t) -> c p u x t", u=2, x=2, t=PACK)[:, :, u, :, :],
-                    in_=turned[:].rearrange("c t p -> c (t p)").bitcast(BF16).rearrange("c (t p x) -> c p x t", t=PACK, x=2),
-                )
+        def to_partitions(rows):
+            cols = psum.tile([P, BANK], F32, name="cols", tag="y", bufs=3)
+            nc.tensor.transpose(cols[:, 0:P], rows[:], ident[:])
+            return cols
 
+        pick_words(0)
+        nc.vector.tensor_copy(v_s[:], tab_s[:].indirect(offsets[:]))
+        nc.gpsimd.dma_start(out=v_s1[0:SHIFT_ROWS, :].bitcast(I32), in_=v_s[4 : 4 + SHIFT_ROWS, :].bitcast(I32))
         cast_w(0)
-        pick_state(0)
         quantize(enc_w[0], enc_s[0], enc_in[0])
-        turn_w(0)
+        pick_words(1)
+        nc.scalar.copy(out=e_cols[:], in_=to_partitions(e_rows)[:, 0:PACK])
         cast_w(1)
-
-        vec_cols = psum.tile([P, PACK, P], F32, name="vec_cols", tag="turned", bufs=2)
-        nc.tensor.transpose(vec_cols[:, 0, :], vec_rows[:], ident[:])
-        nc.scalar.copy(out=e_cols[:], in_=vec_cols[:, 0, ROW_TILES : ROW_TILES + PACK])
-        nc.scalar.activation(out=neg_d[:], in_=vec_cols[:, 0, 0:ROW_TILES], func=ACT.Copy, scale=-1.0)
-
-        pick_state(1)
-        quantize(dec_w[0], dec_s[0], dec_in[0])
         quantize(enc_w[1], enc_s[1], enc_in[1])
-        turn_w(1)
 
         def encode(b):
             cols = slice(b * BANK, (b + 1) * BANK)
@@ -183,50 +169,81 @@ def tile_list_tied_vessel_residual_kernel(tc, tab_words, tab_scales, offs, w, e,
                 in_=h_rows[b][:].rearrange("p (t c x) -> p c t x", t=PACK, x=4),
             )
 
-        def decode(m, b):
+        encode(0)
+
+        dec_in = held("dec_in", [P, K * PACK], BF16, on="w_raw1")
+        for a in range(PASSES):
+            words = enc_in[a][:].bitcast(F32).rearrange("p (t c u) -> p t c u", t=PACK, u=2)
+            target = dec_in[:].rearrange("c (a p u x t) -> c a p u x t", a=PASSES, u=2, x=2, t=PACK)
+            for u in range(2):
+                turned = psum.tile([P, PACK, P], F32, name="turned", tag="turned", bufs=2)
+                for t in range(PACK):
+                    nc.tensor.transpose(turned[:, t, :], words[:, t, :, u], ident[:])
+                halves = turned[:].rearrange("c t p -> c (t p)").bitcast(BF16)
+                nc.scalar.copy(out=target[:, a, :, u, :, :], in_=halves.rearrange("c (t p x) -> c p x t", t=PACK, x=2))
+
+        encode(1)
+        for m in range(D_AFTER):
+            pick_state(m)
+
+        nc.scalar.activation(out=neg_d[:], in_=to_partitions(d_rows)[:, 0:ROW_TILES], func=ACT.Copy, scale=-1.0)
+        dec_w = held("dec_w", [P, K], U32, on="d_rows")
+        quantize(dec_w, dec_s, dec_in)
+        h_w = [held("h_w0", [P, BANK], U32, on="w_raw1")]
+        quantize(h_w[0], h_s[0], h_in[0])
+        for m in range(D_AFTER, LAST):
+            pick_state(m)
+
+        def decode(m, b, step):
             cols = slice(b * BANK, (b + 1) * BANK)
+            rows = slice(m * P, (m + 1) * P)
             y = psum.tile([P, BANK], F32, name="y", tag="y", bufs=3)
             for a in range(PASSES):
                 plane = v_s if a == 0 else v_s1
                 nc.tensor.matmul_mx(
                     out=y[:],
                     lhsT=w4_w[:, a, 2 * m * P : 2 * (m + 1) * P].bitcast(FP4X4),
-                    lhsT_scale=w4_s[:, a, m * P : (m + 1) * P],
+                    lhsT_scale=w4_s[:, a, rows],
                     rhs=v_w[a][:, cols].bitcast(FP8X4),
                     rhs_scale=plane[:, cols],
                     start=(a == 0),
                     stop=False,
                 )
-            a, first = divmod(m * P, K_PASS)
             nc.tensor.matmul_mx(
                 out=y[:],
-                lhsT=dec_w[a][:, first : first + P].bitcast(FP8X4),
-                lhsT_scale=dec_s[a][:, first : first + P],
+                lhsT=dec_w[:, rows].bitcast(FP8X4),
+                lhsT_scale=dec_s[:, rows],
                 rhs=h_w[b][:].bitcast(FP8X4),
                 rhs_scale=h_s[b][:],
                 start=False,
                 stop=True,
             )
-            step = ring.tile([P, BANK], F32, name="step", tag="step")
-            nc.scalar.activation(out=step[:], in_=y[:], func=ACT.Copy, scale=neg_d[:, m : m + 1])
-            window = state[m][:].indirect(offsets[:, b * BANK // 16 : (b + 1) * BANK // 16])
-            nc.vector.tensor_tensor(window, picked[m][:, cols], step[:], ADD)
-            if b == HALVES - 1:
-                nc.sync.dma_start(out=out[m * P : (m + 1) * P, :], in_=state[m][:])
+            nc.scalar.activation(out=step, in_=y[:], func=ACT.Copy, scale=neg_d[:, m : m + 1])
 
-        encode(0)
-        pick_state(2)
-        quantize(dec_w[1], dec_s[1], dec_in[1])
-        pick_state(3)
-        pick_state(4)
-        quantize(h_w[0], h_s[0], h_in[0])
-        for m in range(LEAD):
-            decode(m, 0)
-        encode(1)
-        for m in range(5, ROW_TILES):
-            pick_state(m)
+        def put_back(m, first, count, step):
+            window = state[m][:].indirect(offsets[:, first // 16 : (first + count) // 16])
+            nc.vector.tensor_tensor(window, picked[m][:, first : first + count], step, ADD)
+
+        def update_half(m, b, step):
+            decode(m, b, step[:])
+            put_back(m, b * BANK, BANK, step[:])
+
+        def update_whole(m):
+            step = ring.tile([P, S], F32, name="step", tag="step")
+            for b in range(HALVES):
+                decode(m, b, step[:, b * BANK : (b + 1) * BANK])
+            put_back(m, 0, S, step[:])
+
+        lead = 2
+        for m in range(lead):
+            update_half(m, 0, held(f"lead_step{m}", [P, BANK], F32))
+        h_w.append(held("h_w1", [P, BANK], U32, on=f"lead_step{lead - 1}"))
         quantize(h_w[1], h_s[1], h_in[1])
+        picked.append(held("picked_last", [P, S], F32, on="h_in1"))
+        pick_state(LAST)
         for m in range(ROW_TILES):
-            if m + LEAD < ROW_TILES:
-                decode(m + LEAD, 0)
-            decode(m, 1)
+            if m < lead:
+                update_half(m, 1, ring.tile([P, BANK], F32, name="step", tag="step"))
+            else:
+                update_whole(m)
+            nc.sync.dma_start(out=out[m * P : (m + 1) * P, :], in_=state[m][:])

@@ -27,8 +27,8 @@ ROW_TILES = K // P
 LAST = ROW_TILES - 1
 QUADS = 4
 RUN = 8
-SHIFT_ROWS = 112
-D_AFTER = 6
+SHIFT_ROWS = 100
+D_AFTER = 5
 
 
 def tile_list_tied_vessel_residual_kernel(tc, tab_words, tab_scales, offs, w, e, w4_words, w4_scales, gT, d, out):
@@ -46,8 +46,8 @@ def tile_list_tied_vessel_residual_kernel(tc, tab_words, tab_scales, offs, w, e,
         tab_w = [held(f"tab_w{a}", [P, T], I32) for a in range(PASSES)]
         w_raw = [held(f"w_raw{a}", [P, PACK * H], F32) for a in range(PASSES)]
         state = [held(f"state{m}", [P, T], F32) for m in range(ROW_TILES)]
-        picked = [held(f"picked{m}", [P, S], F32) for m in range(LAST)]
-        w4_w = held("w4_w", [P, PASSES, 2 * K], U8)
+        picked = [held(f"picked{m}", [P, S], F32) for m in range(ROW_TILES)]
+        w4_w = [held(f"w4_w{a}", [P, 2 * K], U8) for a in range(PASSES)]
         w4_s = held("w4_s", [P, PASSES, K], U8)
         e_rows = held("e_rows", [P, P], F32)
         d_rows = held("d_rows", [P, P], F32)
@@ -56,24 +56,22 @@ def tile_list_tied_vessel_residual_kernel(tc, tab_words, tab_scales, offs, w, e,
         v_s = held("v_s", [P, S], U8)
         v_s1 = held("v_s1", [P, S], U8)
         enc_in = [held(f"enc_in{a}", [P, H * PACK], BF16) for a in range(PASSES)]
-        enc_w = [held(f"enc_w{a}", [P, H], U32) for a in range(PASSES)]
         enc_s = [held(f"enc_s{a}", [P, H], U8) for a in range(PASSES)]
-        dec_s = held("dec_s", [P, K], U8)
+        dec_in = [held("dec_in0", [P, K_PASS * PACK], BF16)]
+        dec_s = [held(f"dec_s{a}", [P, K_PASS], U8) for a in range(PASSES)]
         h_rows = [held(f"h_rows{b}", [P, PACK * BANK], BF16) for b in range(HALVES)]
         h_in = [held(f"h_in{b}", [P, BANK * PACK], BF16) for b in range(HALVES)]
         h_s = [held(f"h_s{b}", [P, BANK], U8) for b in range(HALVES)]
         neg_d = held("neg_d", [P, ROW_TILES], F32)
         e_cols = held("e_cols", [P, PACK], F32)
         warm = held("warm", [P, 1], F32)
-        zero = held("zero", [P, 1], F32)
 
         nc.gpsimd.memset(tab_s[:].bitcast(I32), 0)
-        nc.vector.memset(zero[:], 0.0)
         nc.vector.memset(e_rows[:], 0.0)
         nc.vector.memset(d_rows[:], 0.0)
-        nc.vector.memset(w4_s[:].rearrange("p a n -> p (a n)").bitcast(I32), 0)
-        nc.vector.memset(v_s1[:].bitcast(I32), 0)
         make_identity(nc, ident[:])
+
+        nc.scalar.activation(out=warm[:], in_=d_rows[:, 0:1], func=ACT.Gelu_apprx_tanh)
 
         def load_table(a):
             nc.sync.dma_start(out=tab_w[a][:], in_=tab_words[a].rearrange("p t i -> p (t i)").bitcast(I32))
@@ -94,12 +92,13 @@ def tile_list_tied_vessel_residual_kernel(tc, tab_words, tab_scales, offs, w, e,
             )
         load_w(0)
         load_table(1)
+        load_w(1)
+        load_state(0)
         nc.sync.dma_start(
             out=e_rows[0:PACK, :].rearrange("t (b s) -> t b s", s=RUN),
             in_=e.rearrange("(b t s) -> t b s", t=PACK, s=RUN),
         )
-        load_w(1)
-        for m in range(D_AFTER):
+        for m in range(1, D_AFTER):
             load_state(m)
         nc.sync.dma_start(out=d_rows[0:ROW_TILES, :], in_=d.rearrange("(m p) -> m p", p=P))
         for m in range(D_AFTER, LAST):
@@ -109,10 +108,9 @@ def tile_list_tied_vessel_residual_kernel(tc, tab_words, tab_scales, offs, w, e,
                 out=w4_s[32 * q : 32 * q + 4, :, :].bitcast(I32),
                 in_=w4_scales[:, 4 * q : 4 * q + 4, :].rearrange("a r n -> r a n").bitcast(I32),
             )
-        nc.sync.dma_start(out=w4_w[:].bitcast(I32), in_=w4_words.rearrange("a p c -> p a c").bitcast(I32))
+        nc.sync.dma_start(out=w4_w[0][:].bitcast(I32), in_=w4_words[0].bitcast(I32))
         load_state(LAST)
-
-        nc.scalar.activation(out=warm[:], in_=zero[:], func=ACT.Gelu_apprx_tanh)
+        nc.sync.dma_start(out=w4_w[1][:].bitcast(I32), in_=w4_words[1].bitcast(I32))
 
         def pick_words(a):
             nc.vector.tensor_copy(v_w[a][:], tab_w[a][:].bitcast(U32).indirect(offsets[:]))
@@ -124,10 +122,20 @@ def tile_list_tied_vessel_residual_kernel(tc, tab_words, tab_scales, offs, w, e,
             nc.vector.quantize_mx(out=codes[:].bitcast(FP8X4), scales=scales[:], in_=grouped[:])
 
         def cast_w(a):
-            nc.scalar.copy(
-                out=enc_in[a][:].rearrange("p (t b s i) -> p b t s i", t=PACK, s=RUN, i=PACK),
-                in_=w_raw[a][:].rearrange("p (i b t s) -> p b t s i", i=PACK, t=PACK, s=RUN),
-            )
+            target = enc_in[a][:].rearrange("p (t b s x i) -> p s b t i x", t=PACK, s=2, x=4, i=PACK)
+            source = w_raw[a][:].rearrange("p (i b t s x) -> p s b t i x", i=PACK, t=PACK, s=2, x=4)
+            for s in range(2):
+                nc.scalar.copy(out=target[:, s], in_=source[:, s])
+
+        def turn_w(a):
+            words = enc_in[a][:].bitcast(F32).rearrange("p (t c u) -> p t c u", t=PACK, u=2)
+            target = dec_in[a][:].rearrange("c (p u x t) -> c p u x t", u=2, x=2, t=PACK)
+            for u in range(2):
+                turned = psum.tile([P, PACK, P], F32, name="turned", tag="turned", bufs=2)
+                for t in range(PACK):
+                    nc.tensor.transpose(turned[:, t, :], words[:, t, :, u], ident[:])
+                halves = turned[:].rearrange("c t p -> c (t p)").bitcast(BF16)
+                nc.scalar.copy(out=target[:, :, u, :, :], in_=halves.rearrange("c (t p x) -> c p x t", t=PACK, x=2))
 
         def to_partitions(rows):
             cols = psum.tile([P, BANK], F32, name="cols", tag="y", bufs=3)
@@ -138,14 +146,27 @@ def tile_list_tied_vessel_residual_kernel(tc, tab_words, tab_scales, offs, w, e,
         nc.vector.tensor_copy(v_s[:], tab_s[:].indirect(offsets[:]))
         nc.gpsimd.dma_start(out=v_s1[0:SHIFT_ROWS, :].bitcast(I32), in_=v_s[4 : 4 + SHIFT_ROWS, :].bitcast(I32))
         cast_w(0)
-        quantize(enc_w[0], enc_s[0], enc_in[0])
         pick_words(1)
-        nc.scalar.copy(out=e_cols[:], in_=to_partitions(e_rows)[:, 0:PACK])
+        enc_w = [held("enc_w0", [P, H], U32)]
+        quantize(enc_w[0], enc_s[0], enc_in[0])
+        turn_w(0)
+        dec_w = [held("dec_w0", [P, K_PASS], U32)]
+        quantize(dec_w[0], dec_s[0], dec_in[0])
         cast_w(1)
+        pick_state(0)
+        nc.scalar.copy(out=e_cols[:], in_=to_partitions(e_rows)[:, 0:PACK])
+        enc_w.append(held("enc_w1", [P, H], U32, on="e_rows"))
         quantize(enc_w[1], enc_s[1], enc_in[1])
 
         def encode(b):
             cols = slice(b * BANK, (b + 1) * BANK)
+            acts = []
+
+            def scale_units(t):
+                nc.scalar.activation(
+                    out=h_rows[b][:, t * BANK : (t + 1) * BANK], in_=acts[t][:], func=ACT.Copy, scale=e_cols[:, t : t + 1]
+                )
+
             for t in range(PACK):
                 units = slice(t * P, (t + 1) * P)
                 acc = psum.tile([P, BANK], F32, name="acc", tag="acc", bufs=3)
@@ -161,63 +182,51 @@ def tile_list_tied_vessel_residual_kernel(tc, tab_words, tab_scales, offs, w, e,
                     )
                 act = ring.tile([P, BANK], F32, name="act", tag="act")
                 nc.scalar.activation(out=act[:], in_=acc[:], func=ACT.Gelu_apprx_tanh, scale=e_cols[:, t : t + 1])
-                nc.scalar.activation(
-                    out=h_rows[b][:, t * BANK : (t + 1) * BANK], in_=act[:], func=ACT.Copy, scale=e_cols[:, t : t + 1]
-                )
+                acts.append(act)
+                if t > 0:
+                    scale_units(t - 1)
+            scale_units(PACK - 1)
             nc.scalar.copy(
                 out=h_in[b][:].rearrange("p (c x t) -> p c t x", x=4, t=PACK),
                 in_=h_rows[b][:].rearrange("p (t c x) -> p c t x", t=PACK, x=4),
             )
 
         encode(0)
-
-        dec_in = held("dec_in", [P, K * PACK], BF16, on="w_raw1")
-        for a in range(PASSES):
-            words = enc_in[a][:].bitcast(F32).rearrange("p (t c u) -> p t c u", t=PACK, u=2)
-            target = dec_in[:].rearrange("c (a p u x t) -> c a p u x t", a=PASSES, u=2, x=2, t=PACK)
-            for u in range(2):
-                turned = psum.tile([P, PACK, P], F32, name="turned", tag="turned", bufs=2)
-                for t in range(PACK):
-                    nc.tensor.transpose(turned[:, t, :], words[:, t, :, u], ident[:])
-                halves = turned[:].rearrange("c t p -> c (t p)").bitcast(BF16)
-                nc.scalar.copy(out=target[:, a, :, u, :, :], in_=halves.rearrange("c (t p x) -> c p x t", t=PACK, x=2))
-
         encode(1)
-        for m in range(D_AFTER):
+        for m in range(1, D_AFTER):
             pick_state(m)
 
         nc.scalar.activation(out=neg_d[:], in_=to_partitions(d_rows)[:, 0:ROW_TILES], func=ACT.Copy, scale=-1.0)
-        dec_w = held("dec_w", [P, K], U32, on="d_rows")
-        quantize(dec_w, dec_s, dec_in)
-        h_w = [held("h_w0", [P, BANK], U32, on="w_raw1")]
+        h_w = [held("h_w0", [P, BANK], U32, on="d_rows")]
         quantize(h_w[0], h_s[0], h_in[0])
-        for m in range(D_AFTER, LAST):
+        for m in range(D_AFTER, ROW_TILES):
             pick_state(m)
 
         def decode(m, b, step):
             cols = slice(b * BANK, (b + 1) * BANK)
             rows = slice(m * P, (m + 1) * P)
             y = psum.tile([P, BANK], F32, name="y", tag="y", bufs=3)
+            own = slice(m % PACK * P, (m % PACK + 1) * P)
+            nc.tensor.matmul_mx(
+                out=y[:],
+                lhsT=dec_w[m // PACK][:, own].bitcast(FP8X4),
+                lhsT_scale=dec_s[m // PACK][:, own],
+                rhs=h_w[b][:].bitcast(FP8X4),
+                rhs_scale=h_s[b][:],
+                start=True,
+                stop=False,
+            )
             for a in range(PASSES):
                 plane = v_s if a == 0 else v_s1
                 nc.tensor.matmul_mx(
                     out=y[:],
-                    lhsT=w4_w[:, a, 2 * m * P : 2 * (m + 1) * P].bitcast(FP4X4),
+                    lhsT=w4_w[a][:, 2 * m * P : 2 * (m + 1) * P].bitcast(FP4X4),
                     lhsT_scale=w4_s[:, a, rows],
                     rhs=v_w[a][:, cols].bitcast(FP8X4),
                     rhs_scale=plane[:, cols],
-                    start=(a == 0),
-                    stop=False,
+                    start=False,
+                    stop=(a == PASSES - 1),
                 )
-            nc.tensor.matmul_mx(
-                out=y[:],
-                lhsT=dec_w[:, rows].bitcast(FP8X4),
-                lhsT_scale=dec_s[:, rows],
-                rhs=h_w[b][:].bitcast(FP8X4),
-                rhs_scale=h_s[b][:],
-                start=False,
-                stop=True,
-            )
             nc.scalar.activation(out=step, in_=y[:], func=ACT.Copy, scale=neg_d[:, m : m + 1])
 
         def put_back(m, first, count, step):
@@ -234,14 +243,18 @@ def tile_list_tied_vessel_residual_kernel(tc, tab_words, tab_scales, offs, w, e,
                 decode(m, b, step[:, b * BANK : (b + 1) * BANK])
             put_back(m, 0, S, step[:])
 
-        lead = 2
-        for m in range(lead):
-            update_half(m, 0, held(f"lead_step{m}", [P, BANK], F32))
-        h_w.append(held("h_w1", [P, BANK], U32, on=f"lead_step{lead - 1}"))
+        lead = 3
+        update_half(0, 0, held("lead_step0", [P, BANK], F32))
+        h_w.append(held("h_w1", [P, BANK], U32, on="lead_step0"))
         quantize(h_w[1], h_s[1], h_in[1])
-        picked.append(held("picked_last", [P, S], F32, on="h_in1"))
-        pick_state(LAST)
+        for m in range(1, lead):
+            update_half(m, 0, held(f"lead_step{m}", [P, BANK], F32))
         for m in range(ROW_TILES):
+            if m == PACK - 1:
+                dec_in.append(held("dec_in1", [P, K_PASS * PACK], BF16, on="picked0"))
+                turn_w(1)
+                dec_w.append(held("dec_w1", [P, K_PASS], U32, on=f"picked{m - 1}"))
+                quantize(dec_w[1], dec_s[1], dec_in[1])
             if m < lead:
                 update_half(m, 1, ring.tile([P, BANK], F32, name="step", tag="step"))
             else:

@@ -27,8 +27,7 @@ ROW_TILES = K // P
 LAST = ROW_TILES - 1
 QUADS = 4
 RUN = 8
-SHIFT_ROWS = 100
-D_AFTER = 5
+D_AFTER = 6
 
 
 def tile_list_tied_vessel_residual_kernel(tc, tab_words, tab_scales, offs, w, e, w4_words, w4_scales, gT, d, out):
@@ -50,28 +49,29 @@ def tile_list_tied_vessel_residual_kernel(tc, tab_words, tab_scales, offs, w, e,
         w4_w = [held(f"w4_w{a}", [P, 2 * K], U8) for a in range(PASSES)]
         w4_s = held("w4_s", [P, PASSES, K], U8)
         e_rows = held("e_rows", [P, P], F32)
-        d_rows = held("d_rows", [P, P], F32)
+        d_rows = [held(f"d_rows{a}", [P, P], F32) for a in range(PASSES)]
         ident = held("ident", [P, P], F32)
         v_w = [held(f"v_w{a}", [P, S], U32) for a in range(PASSES)]
         v_s = held("v_s", [P, S], U8)
         v_s1 = held("v_s1", [P, S], U8)
         enc_in = [held(f"enc_in{a}", [P, H * PACK], BF16) for a in range(PASSES)]
         enc_s = [held(f"enc_s{a}", [P, H], U8) for a in range(PASSES)]
-        dec_in = [held("dec_in0", [P, K_PASS * PACK], BF16)]
+        dec_in = [held(f"dec_in{a}", [P, K_PASS * PACK], BF16) for a in range(PASSES)]
         dec_s = [held(f"dec_s{a}", [P, K_PASS], U8) for a in range(PASSES)]
         h_rows = [held(f"h_rows{b}", [P, PACK * BANK], BF16) for b in range(HALVES)]
         h_in = [held(f"h_in{b}", [P, BANK * PACK], BF16) for b in range(HALVES)]
         h_s = [held(f"h_s{b}", [P, BANK], U8) for b in range(HALVES)]
-        neg_d = held("neg_d", [P, ROW_TILES], F32)
+        neg_d = [held(f"neg_d{a}", [P, PACK], F32) for a in range(PASSES)]
         e_cols = held("e_cols", [P, PACK], F32)
         warm = held("warm", [P, 1], F32)
 
         nc.gpsimd.memset(tab_s[:].bitcast(I32), 0)
         nc.vector.memset(e_rows[:], 0.0)
-        nc.vector.memset(d_rows[:], 0.0)
+        for a in range(PASSES):
+            nc.vector.memset(d_rows[a][:], 0.0)
         make_identity(nc, ident[:])
 
-        nc.scalar.activation(out=warm[:], in_=d_rows[:, 0:1], func=ACT.Gelu_apprx_tanh)
+        nc.scalar.activation(out=warm[:], in_=d_rows[0][:, 0:1], func=ACT.Gelu_apprx_tanh)
 
         def load_table(a):
             nc.sync.dma_start(out=tab_w[a][:], in_=tab_words[a].rearrange("p t i -> p (t i)").bitcast(I32))
@@ -80,37 +80,23 @@ def tile_list_tied_vessel_residual_kernel(tc, tab_words, tab_scales, offs, w, e,
             rows = w[a * K_PASS : (a + 1) * K_PASS, :]
             nc.sync.dma_start(out=w_raw[a][:], in_=rows.rearrange("(p i) r -> p (i r)", i=PACK))
 
+        def load_d(a):
+            rows = d[a * K_PASS : (a + 1) * K_PASS]
+            nc.sync.dma_start(out=d_rows[a][0:PACK, :], in_=rows.rearrange("(m p) -> m p", p=P))
+
         def load_state(m):
             nc.sync.dma_start(out=state[m][:], in_=gT[m * P : (m + 1) * P, :])
 
         nc.sync.dma_start(offsets[:], offs)
         load_table(0)
-        for q in range(QUADS):
+        for r in range(4):
             nc.sync.dma_start(
-                out=tab_s[32 * q : 32 * q + 4 * PASSES, :].bitcast(I32),
-                in_=tab_scales[:, 4 * q : 4 * q + 4, :].bitcast(I32),
+                out=tab_s[r:P:16, :].bitcast(I32),
+                in_=tab_scales.rearrange("a (q r) t -> r q a t", r=4)[r].bitcast(I32),
             )
         load_w(0)
         load_table(1)
         load_w(1)
-        load_state(0)
-        nc.sync.dma_start(
-            out=e_rows[0:PACK, :].rearrange("t (b s) -> t b s", s=RUN),
-            in_=e.rearrange("(b t s) -> t b s", t=PACK, s=RUN),
-        )
-        for m in range(1, D_AFTER):
-            load_state(m)
-        nc.sync.dma_start(out=d_rows[0:ROW_TILES, :], in_=d.rearrange("(m p) -> m p", p=P))
-        for m in range(D_AFTER, LAST):
-            load_state(m)
-        for q in range(QUADS):
-            nc.sync.dma_start(
-                out=w4_s[32 * q : 32 * q + 4, :, :].bitcast(I32),
-                in_=w4_scales[:, 4 * q : 4 * q + 4, :].rearrange("a r n -> r a n").bitcast(I32),
-            )
-        nc.sync.dma_start(out=w4_w[0][:].bitcast(I32), in_=w4_words[0].bitcast(I32))
-        load_state(LAST)
-        nc.sync.dma_start(out=w4_w[1][:].bitcast(I32), in_=w4_words[1].bitcast(I32))
 
         def pick_words(a):
             nc.vector.tensor_copy(v_w[a][:], tab_w[a][:].bitcast(U32).indirect(offsets[:]))
@@ -144,7 +130,27 @@ def tile_list_tied_vessel_residual_kernel(tc, tab_words, tab_scales, offs, w, e,
 
         pick_words(0)
         nc.vector.tensor_copy(v_s[:], tab_s[:].indirect(offsets[:]))
-        nc.gpsimd.dma_start(out=v_s1[0:SHIFT_ROWS, :].bitcast(I32), in_=v_s[4 : 4 + SHIFT_ROWS, :].bitcast(I32))
+        for r in range(4):
+            nc.sync.dma_start(out=v_s1[r:P:32, :].bitcast(I32), in_=v_s[16 + r : P : 32, :].bitcast(I32))
+        load_state(0)
+        nc.sync.dma_start(
+            out=e_rows[0:PACK, :].rearrange("t (b s) -> t b s", s=RUN),
+            in_=e.rearrange("(b t s) -> t b s", t=PACK, s=RUN),
+        )
+        for m in range(1, D_AFTER):
+            load_state(m)
+        load_d(1)
+        for m in range(D_AFTER, LAST):
+            load_state(m)
+        for q in range(QUADS):
+            nc.sync.dma_start(
+                out=w4_s[32 * q : 32 * q + 4, :, :].bitcast(I32),
+                in_=w4_scales[:, 4 * q : 4 * q + 4, :].rearrange("a r n -> r a n").bitcast(I32),
+            )
+        nc.sync.dma_start(out=w4_w[0][:].bitcast(I32), in_=w4_words[0].bitcast(I32))
+        load_state(LAST)
+        load_d(0)
+        nc.sync.dma_start(out=w4_w[1][:].bitcast(I32), in_=w4_words[1].bitcast(I32))
         cast_w(0)
         pick_words(1)
         enc_w = [held("enc_w0", [P, H], U32)]
@@ -157,6 +163,7 @@ def tile_list_tied_vessel_residual_kernel(tc, tab_words, tab_scales, offs, w, e,
         nc.scalar.copy(out=e_cols[:], in_=to_partitions(e_rows)[:, 0:PACK])
         enc_w.append(held("enc_w1", [P, H], U32, on="e_rows"))
         quantize(enc_w[1], enc_s[1], enc_in[1])
+        turn_w(1)
 
         def encode(b):
             cols = slice(b * BANK, (b + 1) * BANK)
@@ -176,7 +183,7 @@ def tile_list_tied_vessel_residual_kernel(tc, tab_words, tab_scales, offs, w, e,
                         lhsT=enc_w[a][:, units].bitcast(FP8X4),
                         lhsT_scale=enc_s[a][:, units],
                         rhs=v_w[a][:, cols].bitcast(FP8X4),
-                        rhs_scale=v_s[4 * a : P, cols],
+                        rhs_scale=(v_s if a == 0 else v_s1)[:, cols],
                         start=(a == 0),
                         stop=(a == PASSES - 1),
                     )
@@ -196,8 +203,13 @@ def tile_list_tied_vessel_residual_kernel(tc, tab_words, tab_scales, offs, w, e,
         for m in range(1, D_AFTER):
             pick_state(m)
 
-        nc.scalar.activation(out=neg_d[:], in_=to_partitions(d_rows)[:, 0:ROW_TILES], func=ACT.Copy, scale=-1.0)
-        h_w = [held("h_w0", [P, BANK], U32, on="d_rows")]
+        def negate_d(a):
+            nc.scalar.activation(out=neg_d[a][:], in_=to_partitions(d_rows[a])[:, 0:PACK], func=ACT.Copy, scale=-1.0)
+
+        negate_d(1)
+        dec_w.append(held("dec_w1", [P, K_PASS], U32, on="d_rows1"))
+        quantize(dec_w[1], dec_s[1], dec_in[1])
+        h_w = [held("h_w0", [P, BANK], U32, on="dec_in1")]
         quantize(h_w[0], h_s[0], h_in[0])
         for m in range(D_AFTER, ROW_TILES):
             pick_state(m)
@@ -227,7 +239,7 @@ def tile_list_tied_vessel_residual_kernel(tc, tab_words, tab_scales, offs, w, e,
                     start=False,
                     stop=(a == PASSES - 1),
                 )
-            nc.scalar.activation(out=step, in_=y[:], func=ACT.Copy, scale=neg_d[:, m : m + 1])
+            nc.scalar.activation(out=step, in_=y[:], func=ACT.Copy, scale=neg_d[m // PACK][:, m % PACK : m % PACK + 1])
 
         def put_back(m, first, count, step):
             window = state[m][:].indirect(offsets[:, first // 16 : (first + count) // 16])
@@ -243,18 +255,13 @@ def tile_list_tied_vessel_residual_kernel(tc, tab_words, tab_scales, offs, w, e,
                 decode(m, b, step[:, b * BANK : (b + 1) * BANK])
             put_back(m, 0, S, step[:])
 
-        lead = 3
-        update_half(0, 0, held("lead_step0", [P, BANK], F32))
-        h_w.append(held("h_w1", [P, BANK], U32, on="lead_step0"))
+        lead = 2
+        negate_d(0)
+        h_w.append(held("h_w1", [P, BANK], U32, on="d_rows0"))
         quantize(h_w[1], h_s[1], h_in[1])
-        for m in range(1, lead):
+        for m in range(lead):
             update_half(m, 0, held(f"lead_step{m}", [P, BANK], F32))
         for m in range(ROW_TILES):
-            if m == PACK - 1:
-                dec_in.append(held("dec_in1", [P, K_PASS * PACK], BF16, on="picked0"))
-                turn_w(1)
-                dec_w.append(held("dec_w1", [P, K_PASS], U32, on=f"picked{m - 1}"))
-                quantize(dec_w[1], dec_s[1], dec_in[1])
             if m < lead:
                 update_half(m, 1, ring.tile([P, BANK], F32, name="step", tag="step"))
             else:

@@ -28,6 +28,7 @@ LAST = ROW_TILES - 1
 QUADS = 4
 RUN = 8
 D_AFTER = 6
+LEAD = 2
 
 
 def tile_list_tied_vessel_residual_kernel(tc, tab_words, tab_scales, offs, w, e, w4_words, w4_scales, gT, d, out):
@@ -46,7 +47,8 @@ def tile_list_tied_vessel_residual_kernel(tc, tab_words, tab_scales, offs, w, e,
         w_raw = [held(f"w_raw{a}", [P, PACK * H], F32) for a in range(PASSES)]
         state = [held(f"state{m}", [P, T], F32) for m in range(ROW_TILES)]
         picked = [held(f"picked{m}", [P, S], F32) for m in range(ROW_TILES)]
-        w4_w = [held(f"w4_w{a}", [P, 2 * K], U8) for a in range(PASSES)]
+        w4_lead = held("w4_lead", [P, PASSES, 2 * LEAD * P], U8)
+        w4_rest = held("w4_rest", [P, PASSES, 2 * (K - LEAD * P)], U8)
         w4_s = held("w4_s", [P, PASSES, K], U8)
         e_rows = held("e_rows", [P, P], F32)
         d_rows = [held(f"d_rows{a}", [P, P], F32) for a in range(PASSES)]
@@ -87,8 +89,8 @@ def tile_list_tied_vessel_residual_kernel(tc, tab_words, tab_scales, offs, w, e,
         def load_state(m):
             nc.sync.dma_start(out=state[m][:], in_=gT[m * P : (m + 1) * P, :])
 
-        nc.sync.dma_start(offsets[:], offs)
         load_table(0)
+        nc.sync.dma_start(offsets[:], offs)
         for r in range(4):
             nc.sync.dma_start(
                 out=tab_s[r:P:16, :].bitcast(I32),
@@ -130,27 +132,27 @@ def tile_list_tied_vessel_residual_kernel(tc, tab_words, tab_scales, offs, w, e,
 
         pick_words(0)
         nc.vector.tensor_copy(v_s[:], tab_s[:].indirect(offsets[:]))
-        for r in range(4):
-            nc.sync.dma_start(out=v_s1[r:P:32, :].bitcast(I32), in_=v_s[16 + r : P : 32, :].bitcast(I32))
         load_state(0)
         nc.sync.dma_start(
             out=e_rows[0:PACK, :].rearrange("t (b s) -> t b s", s=RUN),
             in_=e.rearrange("(b t s) -> t b s", t=PACK, s=RUN),
         )
+        for r in range(4):
+            nc.sync.dma_start(out=v_s1[r:P:32, :].bitcast(I32), in_=v_s[16 + r : P : 32, :].bitcast(I32))
         for m in range(1, D_AFTER):
             load_state(m)
         load_d(1)
-        for m in range(D_AFTER, LAST):
+        for m in range(D_AFTER, ROW_TILES):
             load_state(m)
+        load_d(0)
         for q in range(QUADS):
             nc.sync.dma_start(
                 out=w4_s[32 * q : 32 * q + 4, :, :].bitcast(I32),
                 in_=w4_scales[:, 4 * q : 4 * q + 4, :].rearrange("a r n -> r a n").bitcast(I32),
             )
-        nc.sync.dma_start(out=w4_w[0][:].bitcast(I32), in_=w4_words[0].bitcast(I32))
-        load_state(LAST)
-        load_d(0)
-        nc.sync.dma_start(out=w4_w[1][:].bitcast(I32), in_=w4_words[1].bitcast(I32))
+        w4_rows = w4_words.rearrange("a p c -> p a c")
+        nc.sync.dma_start(out=w4_lead[:].bitcast(I32), in_=w4_rows[:, :, 0 : 2 * LEAD * P].bitcast(I32))
+        nc.sync.dma_start(out=w4_rest[:].bitcast(I32), in_=w4_rows[:, :, 2 * LEAD * P : 2 * K].bitcast(I32))
         cast_w(0)
         pick_words(1)
         enc_w = [held("enc_w0", [P, H], U32)]
@@ -219,25 +221,27 @@ def tile_list_tied_vessel_residual_kernel(tc, tab_words, tab_scales, offs, w, e,
             rows = slice(m * P, (m + 1) * P)
             y = psum.tile([P, BANK], F32, name="y", tag="y", bufs=3)
             own = slice(m % PACK * P, (m % PACK + 1) * P)
-            nc.tensor.matmul_mx(
-                out=y[:],
-                lhsT=dec_w[m // PACK][:, own].bitcast(FP8X4),
-                lhsT_scale=dec_s[m // PACK][:, own],
-                rhs=h_w[b][:].bitcast(FP8X4),
-                rhs_scale=h_s[b][:],
-                start=True,
-                stop=False,
-            )
-            for a in range(PASSES):
-                plane = v_s if a == 0 else v_s1
+            short, first = (w4_lead, m) if m < LEAD else (w4_rest, m - LEAD)
+            passes = [
+                (
+                    short[:, a, 2 * first * P : 2 * (first + 1) * P].bitcast(FP4X4),
+                    w4_s[:, a, rows],
+                    v_w[a][:, cols].bitcast(FP8X4),
+                    (v_s if a == 0 else v_s1)[:, cols],
+                )
+                for a in range(PASSES)
+            ]
+            tied = (dec_w[m // PACK][:, own].bitcast(FP8X4), dec_s[m // PACK][:, own], h_w[b][:].bitcast(FP8X4), h_s[b][:])
+            passes = [tied] + passes if b == 0 else passes + [tied]
+            for number, (lhsT, lhsT_scale, rhs, rhs_scale) in enumerate(passes):
                 nc.tensor.matmul_mx(
                     out=y[:],
-                    lhsT=w4_w[a][:, 2 * m * P : 2 * (m + 1) * P].bitcast(FP4X4),
-                    lhsT_scale=w4_s[:, a, rows],
-                    rhs=v_w[a][:, cols].bitcast(FP8X4),
-                    rhs_scale=plane[:, cols],
-                    start=False,
-                    stop=(a == PASSES - 1),
+                    lhsT=lhsT,
+                    lhsT_scale=lhsT_scale,
+                    rhs=rhs,
+                    rhs_scale=rhs_scale,
+                    start=(number == 0),
+                    stop=(number == len(passes) - 1),
                 )
             nc.scalar.activation(out=step, in_=y[:], func=ACT.Copy, scale=neg_d[m // PACK][:, m % PACK : m % PACK + 1])
 
@@ -255,7 +259,7 @@ def tile_list_tied_vessel_residual_kernel(tc, tab_words, tab_scales, offs, w, e,
                 decode(m, b, step[:, b * BANK : (b + 1) * BANK])
             put_back(m, 0, S, step[:])
 
-        lead = 2
+        lead = LEAD
         negate_d(0)
         h_w.append(held("h_w1", [P, BANK], U32, on="d_rows0"))
         quantize(h_w[1], h_s[1], h_in[1])

@@ -24,9 +24,14 @@ PASSES = K // K_PASS
 BANK = 512
 HALVES = S // BANK
 ROW_TILES = K // P
-LAST = ROW_TILES - 1
+TILES_A_PASS = K_PASS // P
+GROUP = 16
 QUADS = 4
+QUAD = P // QUADS
+LIVE = 4
+SPREAD = P // (PASSES * QUADS * LIVE)
 RUN = 8
+LINE = 4
 D_AFTER = 6
 LEAD = 2
 
@@ -41,7 +46,7 @@ def tile_list_tied_vessel_residual_kernel(tc, tab_words, tab_scales, offs, w, e,
         def held(name, shape, dtype, on=None):
             return keep.tile(shape, dtype, name=name, tag=on or name, align_bytes=64)
 
-        offsets = held("offsets", [P, S // 16], U16)
+        offsets = held("offsets", [P, S // GROUP], U16)
         tab_s = held("tab_s", [P, T], U8)
         tab_w = [held(f"tab_w{a}", [P, T], I32) for a in range(PASSES)]
         w_raw = [held(f"w_raw{a}", [P, PACK * H], F32) for a in range(PASSES)]
@@ -54,8 +59,8 @@ def tile_list_tied_vessel_residual_kernel(tc, tab_words, tab_scales, offs, w, e,
         d_rows = [held(f"d_rows{a}", [P, P], F32) for a in range(PASSES)]
         ident = held("ident", [P, P], F32)
         v_w = [held(f"v_w{a}", [P, S], U32) for a in range(PASSES)]
-        v_s = held("v_s", [P, S], U8)
-        v_s1 = held("v_s1", [P, S], U8)
+        v_rows = held("v_rows", [P, S], U8)
+        v_s = [held(f"v_s{a}", [P, S], U8) for a in range(PASSES)]
         enc_in = [held(f"enc_in{a}", [P, H * PACK], BF16) for a in range(PASSES)]
         enc_s = [held(f"enc_s{a}", [P, H], U8) for a in range(PASSES)]
         dec_in = [held(f"dec_in{a}", [P, K_PASS * PACK], BF16) for a in range(PASSES)]
@@ -63,7 +68,7 @@ def tile_list_tied_vessel_residual_kernel(tc, tab_words, tab_scales, offs, w, e,
         h_rows = [held(f"h_rows{b}", [P, PACK * BANK], BF16) for b in range(HALVES)]
         h_in = [held(f"h_in{b}", [P, BANK * PACK], BF16) for b in range(HALVES)]
         h_s = [held(f"h_s{b}", [P, BANK], U8) for b in range(HALVES)]
-        neg_d = [held(f"neg_d{a}", [P, PACK], F32) for a in range(PASSES)]
+        neg_d = [held(f"neg_d{a}", [P, TILES_A_PASS], F32) for a in range(PASSES)]
         e_cols = held("e_cols", [P, PACK], F32)
         warm = held("warm", [P, 1], F32)
 
@@ -84,21 +89,10 @@ def tile_list_tied_vessel_residual_kernel(tc, tab_words, tab_scales, offs, w, e,
 
         def load_d(a):
             rows = d[a * K_PASS : (a + 1) * K_PASS]
-            nc.sync.dma_start(out=d_rows[a][0:PACK, :], in_=rows.rearrange("(m p) -> m p", p=P))
+            nc.sync.dma_start(out=d_rows[a][0:TILES_A_PASS, :], in_=rows.rearrange("(m p) -> m p", p=P))
 
         def load_state(m):
             nc.sync.dma_start(out=state[m][:], in_=gT[m * P : (m + 1) * P, :])
-
-        load_table(0)
-        nc.sync.dma_start(offsets[:], offs)
-        for r in range(4):
-            nc.sync.dma_start(
-                out=tab_s[r:P:16, :].bitcast(I32),
-                in_=tab_scales.rearrange("a (q r) t -> r q a t", r=4)[r].bitcast(I32),
-            )
-        load_w(0)
-        load_table(1)
-        load_w(1)
 
         def pick_words(a):
             nc.vector.tensor_copy(v_w[a][:], tab_w[a][:].bitcast(U32).indirect(offsets[:]))
@@ -110,10 +104,10 @@ def tile_list_tied_vessel_residual_kernel(tc, tab_words, tab_scales, offs, w, e,
             nc.vector.quantize_mx(out=codes[:].bitcast(FP8X4), scales=scales[:], in_=grouped[:])
 
         def cast_w(a):
-            target = enc_in[a][:].rearrange("p (t b s x i) -> p s b t i x", t=PACK, s=2, x=4, i=PACK)
-            source = w_raw[a][:].rearrange("p (i b t s x) -> p s b t i x", i=PACK, t=PACK, s=2, x=4)
-            for s in range(2):
-                nc.scalar.copy(out=target[:, s], in_=source[:, s])
+            target = enc_in[a][:].rearrange("p (t g z x i) -> p z g t i x", t=PACK, z=RUN // LINE, x=LINE, i=PACK)
+            source = w_raw[a][:].rearrange("p (i g t z x) -> p z g t i x", i=PACK, t=PACK, z=RUN // LINE, x=LINE)
+            for z in range(RUN // LINE):
+                nc.scalar.copy(out=target[:, z], in_=source[:, z])
 
         def turn_w(a):
             words = enc_in[a][:].bitcast(F32).rearrange("p (t c u) -> p t c u", t=PACK, u=2)
@@ -122,24 +116,36 @@ def tile_list_tied_vessel_residual_kernel(tc, tab_words, tab_scales, offs, w, e,
                 turned = psum.tile([P, PACK, P], F32, name="turned", tag="turned", bufs=2)
                 for t in range(PACK):
                     nc.tensor.transpose(turned[:, t, :], words[:, t, :, u], ident[:])
-                halves = turned[:].rearrange("c t p -> c (t p)").bitcast(BF16)
-                nc.scalar.copy(out=target[:, :, u, :, :], in_=halves.rearrange("c (t p x) -> c p x t", t=PACK, x=2))
+                pairs = turned[:].rearrange("c t p -> c (t p)").bitcast(BF16)
+                nc.scalar.copy(out=target[:, :, u, :, :], in_=pairs.rearrange("c (t p x) -> c p x t", t=PACK, x=2))
 
         def to_partitions(rows):
-            cols = psum.tile([P, BANK], F32, name="cols", tag="y", bufs=3)
-            nc.tensor.transpose(cols[:, 0:P], rows[:], ident[:])
-            return cols
+            columns = psum.tile([P, BANK], F32, name="columns", tag="y", bufs=3)
+            nc.tensor.transpose(columns[:, 0:P], rows[:], ident[:])
+            return columns
 
+        load_table(0)
+        nc.sync.dma_start(offsets[:], offs)
+        nc.sync.dma_start(out=tab_s[0:P:SPREAD, :].bitcast(I32), in_=tab_scales.rearrange("a j t -> (a j) t").bitcast(I32))
+        load_w(0)
+        load_table(1)
+        load_w(1)
         pick_words(0)
-        nc.vector.tensor_copy(v_s[:], tab_s[:].indirect(offsets[:]))
+        nc.vector.tensor_copy(v_rows[:], tab_s[:].indirect(offsets[:]))
         load_state(0)
         nc.sync.dma_start(
-            out=e_rows[0:PACK, :].rearrange("t (b s) -> t b s", s=RUN),
-            in_=e.rearrange("(b t s) -> t b s", t=PACK, s=RUN),
+            out=e_rows[0:PACK, :].rearrange("t (g s) -> t g s", s=RUN),
+            in_=e.rearrange("(g t s) -> t g s", t=PACK, s=RUN),
         )
-        for r in range(4):
-            nc.sync.dma_start(out=v_s1[r:P:32, :].bitcast(I32), in_=v_s[16 + r : P : 32, :].bitcast(I32))
-        for m in range(1, D_AFTER):
+        for a in range(PASSES):
+            for q in range(QUADS):
+                row = SPREAD * LIVE * (QUADS * a + q)
+                nc.sync.dma_start(
+                    out=v_s[a][QUAD * q : QUAD * q + LIVE, :].bitcast(I32),
+                    in_=v_rows[row : row + SPREAD * LIVE : SPREAD, :].bitcast(I32),
+                )
+            load_state(1 + a)
+        for m in range(1 + PASSES, D_AFTER):
             load_state(m)
         load_d(1)
         for m in range(D_AFTER, ROW_TILES):
@@ -147,12 +153,13 @@ def tile_list_tied_vessel_residual_kernel(tc, tab_words, tab_scales, offs, w, e,
         load_d(0)
         for q in range(QUADS):
             nc.sync.dma_start(
-                out=w4_s[32 * q : 32 * q + 4, :, :].bitcast(I32),
-                in_=w4_scales[:, 4 * q : 4 * q + 4, :].rearrange("a r n -> r a n").bitcast(I32),
+                out=w4_s[QUAD * q : QUAD * q + LIVE, :, :].bitcast(I32),
+                in_=w4_scales[:, LIVE * q : LIVE * (q + 1), :].rearrange("a j n -> j a n").bitcast(I32),
             )
         w4_rows = w4_words.rearrange("a p c -> p a c")
         nc.sync.dma_start(out=w4_lead[:].bitcast(I32), in_=w4_rows[:, :, 0 : 2 * LEAD * P].bitcast(I32))
         nc.sync.dma_start(out=w4_rest[:].bitcast(I32), in_=w4_rows[:, :, 2 * LEAD * P : 2 * K].bitcast(I32))
+
         cast_w(0)
         pick_words(1)
         enc_w = [held("enc_w0", [P, H], U32)]
@@ -168,7 +175,7 @@ def tile_list_tied_vessel_residual_kernel(tc, tab_words, tab_scales, offs, w, e,
         turn_w(1)
 
         def encode(b):
-            cols = slice(b * BANK, (b + 1) * BANK)
+            entries = slice(b * BANK, (b + 1) * BANK)
             acts = []
 
             def scale_units(t):
@@ -184,8 +191,8 @@ def tile_list_tied_vessel_residual_kernel(tc, tab_words, tab_scales, offs, w, e,
                         out=acc[:],
                         lhsT=enc_w[a][:, units].bitcast(FP8X4),
                         lhsT_scale=enc_s[a][:, units],
-                        rhs=v_w[a][:, cols].bitcast(FP8X4),
-                        rhs_scale=(v_s if a == 0 else v_s1)[:, cols],
+                        rhs=v_w[a][:, entries].bitcast(FP8X4),
+                        rhs_scale=v_s[a][:, entries],
                         start=(a == 0),
                         stop=(a == PASSES - 1),
                     )
@@ -196,18 +203,17 @@ def tile_list_tied_vessel_residual_kernel(tc, tab_words, tab_scales, offs, w, e,
                     scale_units(t - 1)
             scale_units(PACK - 1)
             nc.scalar.copy(
-                out=h_in[b][:].rearrange("p (c x t) -> p c t x", x=4, t=PACK),
-                in_=h_rows[b][:].rearrange("p (t c x) -> p c t x", t=PACK, x=4),
+                out=h_in[b][:].rearrange("p (c x t) -> p c t x", x=LINE, t=PACK),
+                in_=h_rows[b][:].rearrange("p (t c x) -> p c t x", t=PACK, x=LINE),
             )
 
-        encode(0)
-        encode(1)
+        def negate_d(a):
+            nc.scalar.activation(out=neg_d[a][:], in_=to_partitions(d_rows[a])[:, 0:TILES_A_PASS], func=ACT.Copy, scale=-1.0)
+
+        for b in range(HALVES):
+            encode(b)
         for m in range(1, D_AFTER):
             pick_state(m)
-
-        def negate_d(a):
-            nc.scalar.activation(out=neg_d[a][:], in_=to_partitions(d_rows[a])[:, 0:PACK], func=ACT.Copy, scale=-1.0)
-
         negate_d(1)
         dec_w.append(held("dec_w1", [P, K_PASS], U32, on="d_rows1"))
         quantize(dec_w[1], dec_s[1], dec_in[1])
@@ -215,25 +221,28 @@ def tile_list_tied_vessel_residual_kernel(tc, tab_words, tab_scales, offs, w, e,
         quantize(h_w[0], h_s[0], h_in[0])
         for m in range(D_AFTER, ROW_TILES):
             pick_state(m)
+        negate_d(0)
+        h_w.append(held("h_w1", [P, BANK], U32, on="d_rows0"))
+        quantize(h_w[1], h_s[1], h_in[1])
 
         def decode(m, b, step):
-            cols = slice(b * BANK, (b + 1) * BANK)
-            rows = slice(m * P, (m + 1) * P)
+            entries = slice(b * BANK, (b + 1) * BANK)
+            half, place = divmod(m, TILES_A_PASS)
+            own = slice(place * P, (place + 1) * P)
+            w4_part, tile_in_part = (w4_lead, m) if m < LEAD else (w4_rest, m - LEAD)
             y = psum.tile([P, BANK], F32, name="y", tag="y", bufs=3)
-            own = slice(m % PACK * P, (m % PACK + 1) * P)
-            short, first = (w4_lead, m) if m < LEAD else (w4_rest, m - LEAD)
-            passes = [
+            short_cut = [
                 (
-                    short[:, a, 2 * first * P : 2 * (first + 1) * P].bitcast(FP4X4),
-                    w4_s[:, a, rows],
-                    v_w[a][:, cols].bitcast(FP8X4),
-                    (v_s if a == 0 else v_s1)[:, cols],
+                    w4_part[:, a, 2 * tile_in_part * P : 2 * (tile_in_part + 1) * P].bitcast(FP4X4),
+                    w4_s[:, a, m * P : (m + 1) * P],
+                    v_w[a][:, entries].bitcast(FP8X4),
+                    v_s[a][:, entries],
                 )
                 for a in range(PASSES)
             ]
-            tied = (dec_w[m // PACK][:, own].bitcast(FP8X4), dec_s[m // PACK][:, own], h_w[b][:].bitcast(FP8X4), h_s[b][:])
-            passes = [tied] + passes if b == 0 else passes + [tied]
-            for number, (lhsT, lhsT_scale, rhs, rhs_scale) in enumerate(passes):
+            tied = [(dec_w[half][:, own].bitcast(FP8X4), dec_s[half][:, own], h_w[b][:].bitcast(FP8X4), h_s[b][:])]
+            terms = tied + short_cut if b == 0 else short_cut + tied
+            for number, (lhsT, lhsT_scale, rhs, rhs_scale) in enumerate(terms):
                 nc.tensor.matmul_mx(
                     out=y[:],
                     lhsT=lhsT,
@@ -241,12 +250,12 @@ def tile_list_tied_vessel_residual_kernel(tc, tab_words, tab_scales, offs, w, e,
                     rhs=rhs,
                     rhs_scale=rhs_scale,
                     start=(number == 0),
-                    stop=(number == len(passes) - 1),
+                    stop=(number == len(terms) - 1),
                 )
-            nc.scalar.activation(out=step, in_=y[:], func=ACT.Copy, scale=neg_d[m // PACK][:, m % PACK : m % PACK + 1])
+            nc.scalar.activation(out=step, in_=y[:], func=ACT.Copy, scale=neg_d[half][:, place : place + 1])
 
         def put_back(m, first, count, step):
-            window = state[m][:].indirect(offsets[:, first // 16 : (first + count) // 16])
+            window = state[m][:].indirect(offsets[:, first // GROUP : (first + count) // GROUP])
             nc.vector.tensor_tensor(window, picked[m][:, first : first + count], step, ADD)
 
         def update_half(m, b, step):
@@ -259,14 +268,10 @@ def tile_list_tied_vessel_residual_kernel(tc, tab_words, tab_scales, offs, w, e,
                 decode(m, b, step[:, b * BANK : (b + 1) * BANK])
             put_back(m, 0, S, step[:])
 
-        lead = LEAD
-        negate_d(0)
-        h_w.append(held("h_w1", [P, BANK], U32, on="d_rows0"))
-        quantize(h_w[1], h_s[1], h_in[1])
-        for m in range(lead):
+        for m in range(LEAD):
             update_half(m, 0, held(f"lead_step{m}", [P, BANK], F32))
         for m in range(ROW_TILES):
-            if m < lead:
+            if m < LEAD:
                 update_half(m, 1, ring.tile([P, BANK], F32, name="step", tag="step"))
             else:
                 update_whole(m)

@@ -29,11 +29,11 @@ GROUP = 16
 QUADS = 4
 QUAD = P // QUADS
 LIVE = 4
-SPREAD = P // (PASSES * QUADS * LIVE)
 RUN = 8
 LINE = 4
-D_AFTER = 6
+D_AFTER = 4
 LEAD = 2
+SHARE = 2
 
 
 def tile_list_tied_vessel_residual_kernel(tc, tab_words, tab_scales, offs, w, e, w4_words, w4_scales, gT, d, out):
@@ -72,7 +72,8 @@ def tile_list_tied_vessel_residual_kernel(tc, tab_words, tab_scales, offs, w, e,
         e_cols = held("e_cols", [P, PACK], F32)
         warm = held("warm", [P, 1], F32)
 
-        nc.gpsimd.memset(tab_s[:].bitcast(I32), 0)
+        nc.gpsimd.memset(tab_s[QUAD : 2 * QUAD, :].bitcast(I32), 0)
+        nc.gpsimd.memset(tab_s[2 * QUAD : P, :].bitcast(I32), 0)
         nc.vector.memset(e_rows[:], 0.0)
         for a in range(PASSES):
             nc.vector.memset(d_rows[a][:], 0.0)
@@ -104,10 +105,11 @@ def tile_list_tied_vessel_residual_kernel(tc, tab_words, tab_scales, offs, w, e,
             nc.vector.quantize_mx(out=codes[:].bitcast(FP8X4), scales=scales[:], in_=grouped[:])
 
         def cast_w(a):
-            target = enc_in[a][:].rearrange("p (t g z x i) -> p z g t i x", t=PACK, z=RUN // LINE, x=LINE, i=PACK)
-            source = w_raw[a][:].rearrange("p (i g t z x) -> p z g t i x", i=PACK, t=PACK, z=RUN // LINE, x=LINE)
+            target = enc_in[a][:].rearrange("p (t g z x i) -> p z t g i x", t=PACK, z=RUN // LINE, x=LINE, i=PACK)
+            source = w_raw[a][:].rearrange("p (i g t z x) -> p z t g i x", i=PACK, t=PACK, z=RUN // LINE, x=LINE)
             for z in range(RUN // LINE):
-                nc.scalar.copy(out=target[:, z], in_=source[:, z])
+                nc.vector.tensor_copy(target[:, z, 0:SHARE], source[:, z, 0:SHARE])
+                nc.scalar.copy(out=target[:, z, SHARE:PACK], in_=source[:, z, SHARE:PACK])
 
         def turn_w(a):
             words = enc_in[a][:].bitcast(F32).rearrange("p (t c u) -> p t c u", t=PACK, u=2)
@@ -124,33 +126,35 @@ def tile_list_tied_vessel_residual_kernel(tc, tab_words, tab_scales, offs, w, e,
             nc.tensor.transpose(columns[:, 0:P], rows[:], ident[:])
             return columns
 
-        load_table(0)
         nc.sync.dma_start(offsets[:], offs)
-        nc.sync.dma_start(out=tab_s[0:P:SPREAD, :].bitcast(I32), in_=tab_scales.rearrange("a j t -> (a j) t").bitcast(I32))
-        load_w(0)
-        load_table(1)
-        load_w(1)
-        pick_words(0)
+        nc.sync.dma_start(out=tab_s[0:QUAD, :].bitcast(I32), in_=tab_scales.rearrange("a j t -> (a j) t").bitcast(I32))
+        for a in range(PASSES):
+            load_w(a)
+            load_table(a)
         nc.vector.tensor_copy(v_rows[:], tab_s[:].indirect(offsets[:]))
+
+        def move_plane(a):
+            for q in range(QUADS):
+                row = LIVE * (QUADS * a + q)
+                nc.sync.dma_start(
+                    out=v_s[a][QUAD * q : QUAD * q + LIVE, :].bitcast(I32),
+                    in_=v_rows[row : row + LIVE, :].bitcast(I32),
+                )
+
+        move_plane(0)
         load_state(0)
         nc.sync.dma_start(
             out=e_rows[0:PACK, :].rearrange("t (g s) -> t g s", s=RUN),
             in_=e.rearrange("(g t s) -> t g s", t=PACK, s=RUN),
         )
-        for a in range(PASSES):
-            for q in range(QUADS):
-                row = SPREAD * LIVE * (QUADS * a + q)
-                nc.sync.dma_start(
-                    out=v_s[a][QUAD * q : QUAD * q + LIVE, :].bitcast(I32),
-                    in_=v_rows[row : row + SPREAD * LIVE : SPREAD, :].bitcast(I32),
-                )
-            load_state(1 + a)
-        for m in range(1 + PASSES, D_AFTER):
+        move_plane(1)
+        for m in range(1, D_AFTER):
             load_state(m)
         load_d(1)
-        for m in range(D_AFTER, ROW_TILES):
+        for m in range(D_AFTER, ROW_TILES - 1):
             load_state(m)
         load_d(0)
+        load_state(ROW_TILES - 1)
         for q in range(QUADS):
             nc.sync.dma_start(
                 out=w4_s[QUAD * q : QUAD * q + LIVE, :, :].bitcast(I32),
@@ -160,19 +164,16 @@ def tile_list_tied_vessel_residual_kernel(tc, tab_words, tab_scales, offs, w, e,
         nc.sync.dma_start(out=w4_lead[:].bitcast(I32), in_=w4_rows[:, :, 0 : 2 * LEAD * P].bitcast(I32))
         nc.sync.dma_start(out=w4_rest[:].bitcast(I32), in_=w4_rows[:, :, 2 * LEAD * P : 2 * K].bitcast(I32))
 
-        cast_w(0)
-        pick_words(1)
-        enc_w = [held("enc_w0", [P, H], U32)]
-        quantize(enc_w[0], enc_s[0], enc_in[0])
-        turn_w(0)
-        dec_w = [held("dec_w0", [P, K_PASS], U32)]
-        quantize(dec_w[0], dec_s[0], dec_in[0])
-        cast_w(1)
-        pick_state(0)
+        enc_w, dec_w = [], []
+        for a in range(PASSES):
+            cast_w(a)
+            enc_w.append(held(f"enc_w{a}", [P, H], U32))
+            quantize(enc_w[a], enc_s[a], enc_in[a])
+            turn_w(a)
+            pick_words(a)
+            dec_w.append(held(f"dec_w{a}", [P, K_PASS], U32, on=f"tab_w{a}"))
+            quantize(dec_w[a], dec_s[a], dec_in[a])
         nc.scalar.copy(out=e_cols[:], in_=to_partitions(e_rows)[:, 0:PACK])
-        enc_w.append(held("enc_w1", [P, H], U32, on="e_rows"))
-        quantize(enc_w[1], enc_s[1], enc_in[1])
-        turn_w(1)
 
         def encode(b):
             entries = slice(b * BANK, (b + 1) * BANK)
@@ -186,15 +187,15 @@ def tile_list_tied_vessel_residual_kernel(tc, tab_words, tab_scales, offs, w, e,
             for t in range(PACK):
                 units = slice(t * P, (t + 1) * P)
                 acc = psum.tile([P, BANK], F32, name="acc", tag="acc", bufs=3)
-                for a in range(PASSES):
+                for a in reversed(range(PASSES)):
                     nc.tensor.matmul_mx(
                         out=acc[:],
                         lhsT=enc_w[a][:, units].bitcast(FP8X4),
                         lhsT_scale=enc_s[a][:, units],
                         rhs=v_w[a][:, entries].bitcast(FP8X4),
                         rhs_scale=v_s[a][:, entries],
-                        start=(a == 0),
-                        stop=(a == PASSES - 1),
+                        start=(a == PASSES - 1),
+                        stop=(a == 0),
                     )
                 act = ring.tile([P, BANK], F32, name="act", tag="act")
                 nc.scalar.activation(out=act[:], in_=acc[:], func=ACT.Gelu_apprx_tanh, scale=e_cols[:, t : t + 1])
@@ -212,18 +213,17 @@ def tile_list_tied_vessel_residual_kernel(tc, tab_words, tab_scales, offs, w, e,
 
         for b in range(HALVES):
             encode(b)
-        for m in range(1, D_AFTER):
+        for m in range(D_AFTER):
             pick_state(m)
         negate_d(1)
-        dec_w.append(held("dec_w1", [P, K_PASS], U32, on="d_rows1"))
-        quantize(dec_w[1], dec_s[1], dec_in[1])
-        h_w = [held("h_w0", [P, BANK], U32, on="dec_in1")]
+        h_w = [held("h_w0", [P, BANK], U32, on="d_rows1")]
         quantize(h_w[0], h_s[0], h_in[0])
-        for m in range(D_AFTER, ROW_TILES):
+        for m in range(D_AFTER, ROW_TILES - 1):
             pick_state(m)
         negate_d(0)
         h_w.append(held("h_w1", [P, BANK], U32, on="d_rows0"))
         quantize(h_w[1], h_s[1], h_in[1])
+        pick_state(ROW_TILES - 1)
 
         def decode(m, b, step):
             entries = slice(b * BANK, (b + 1) * BANK)

@@ -33,7 +33,7 @@ RUN = 8
 LINE = 4
 D_AFTER = 4
 LEAD = 2
-SHARE = 2
+SHARE = 3
 
 
 def tile_list_tied_vessel_residual_kernel(tc, tab_words, tab_scales, offs, w, e, w4_words, w4_scales, gT, d, out):
@@ -105,11 +105,14 @@ def tile_list_tied_vessel_residual_kernel(tc, tab_words, tab_scales, offs, w, e,
             nc.vector.quantize_mx(out=codes[:].bitcast(FP8X4), scales=scales[:], in_=grouped[:])
 
         def cast_w(a):
-            target = enc_in[a][:].rearrange("p (t g z x i) -> p z t g i x", t=PACK, z=RUN // LINE, x=LINE, i=PACK)
-            source = w_raw[a][:].rearrange("p (i g t z x) -> p z t g i x", i=PACK, t=PACK, z=RUN // LINE, x=LINE)
-            for z in range(RUN // LINE):
-                nc.vector.tensor_copy(target[:, z, 0:SHARE], source[:, z, 0:SHARE])
-                nc.scalar.copy(out=target[:, z, SHARE:PACK], in_=source[:, z, SHARE:PACK])
+            nc.vector.tensor_copy(
+                enc_in[a][:].rearrange("p (t g s i) -> p g t s i", t=PACK, s=RUN, i=PACK)[:, :, 0:SHARE],
+                w_raw[a][:].rearrange("p (i g t s) -> p g t s i", i=PACK, t=PACK, s=RUN)[:, :, 0:SHARE],
+            )
+            target = enc_in[a][:].rearrange("p (t g z x i) -> p t g z i x", t=PACK, z=RUN // LINE, x=LINE, i=PACK)
+            source = w_raw[a][:].rearrange("p (i g t z x) -> p t g z i x", i=PACK, t=PACK, z=RUN // LINE, x=LINE)
+            for t in range(SHARE, PACK):
+                nc.scalar.copy(out=target[:, t], in_=source[:, t])
 
         def turn_w(a):
             words = enc_in[a][:].bitcast(F32).rearrange("p (t c u) -> p t c u", t=PACK, u=2)
@@ -171,9 +174,13 @@ def tile_list_tied_vessel_residual_kernel(tc, tab_words, tab_scales, offs, w, e,
             quantize(enc_w[a], enc_s[a], enc_in[a])
             turn_w(a)
             pick_words(a)
-            dec_w.append(held(f"dec_w{a}", [P, K_PASS], U32, on=f"tab_w{a}"))
-            quantize(dec_w[a], dec_s[a], dec_in[a])
+            if a == 0:
+                dec_w.append(held("dec_w0", [P, K_PASS], U32, on="tab_w0"))
+                quantize(dec_w[0], dec_s[0], dec_in[0])
+        pick_state(0)
         nc.scalar.copy(out=e_cols[:], in_=to_partitions(e_rows)[:, 0:PACK])
+        dec_w.append(held("dec_w1", [P, K_PASS], U32, on="e_rows"))
+        quantize(dec_w[1], dec_s[1], dec_in[1])
 
         def encode(b):
             entries = slice(b * BANK, (b + 1) * BANK)
@@ -213,7 +220,7 @@ def tile_list_tied_vessel_residual_kernel(tc, tab_words, tab_scales, offs, w, e,
 
         for b in range(HALVES):
             encode(b)
-        for m in range(D_AFTER):
+        for m in range(1, D_AFTER):
             pick_state(m)
         negate_d(1)
         h_w = [held("h_w0", [P, BANK], U32, on="d_rows1")]

@@ -31,7 +31,7 @@ QUAD = P // QUADS
 LIVE = 4
 RUN = 8
 LINE = 4
-D_AFTER = 4
+D_AFTER = 5
 LEAD = 2
 SHARE = 3
 
@@ -54,7 +54,8 @@ def tile_list_tied_vessel_residual_kernel(tc, tab_words, tab_scales, offs, w, e,
         picked = [held(f"picked{m}", [P, S], F32) for m in range(ROW_TILES)]
         w4_lead = held("w4_lead", [P, PASSES, 2 * LEAD * P], U8)
         w4_rest = held("w4_rest", [P, PASSES, 2 * (K - LEAD * P)], U8)
-        w4_s = held("w4_s", [P, PASSES, K], U8)
+        w4_lead_s = held("w4_lead_s", [P, PASSES, LEAD * P], U8)
+        w4_rest_s = held("w4_rest_s", [P, PASSES, K - LEAD * P], U8)
         e_rows = held("e_rows", [P, P], F32)
         d_rows = [held(f"d_rows{a}", [P, P], F32) for a in range(PASSES)]
         ident = held("ident", [P, P], F32)
@@ -157,15 +158,19 @@ def tile_list_tied_vessel_residual_kernel(tc, tab_words, tab_scales, offs, w, e,
         for m in range(D_AFTER, ROW_TILES - 1):
             load_state(m)
         load_d(0)
+
+        def load_w4(words, scales, first, last):
+            for q in range(QUADS):
+                nc.sync.dma_start(
+                    out=scales[QUAD * q : QUAD * q + LIVE, :, :].bitcast(I32),
+                    in_=w4_scales[:, LIVE * q : LIVE * (q + 1), first:last].rearrange("a j n -> j a n").bitcast(I32),
+                )
+            rows = w4_words.rearrange("a p c -> p a c")
+            nc.sync.dma_start(out=words[:].bitcast(I32), in_=rows[:, :, 2 * first : 2 * last].bitcast(I32))
+
+        load_w4(w4_lead, w4_lead_s, 0, LEAD * P)
         load_state(ROW_TILES - 1)
-        for q in range(QUADS):
-            nc.sync.dma_start(
-                out=w4_s[QUAD * q : QUAD * q + LIVE, :, :].bitcast(I32),
-                in_=w4_scales[:, LIVE * q : LIVE * (q + 1), :].rearrange("a j n -> j a n").bitcast(I32),
-            )
-        w4_rows = w4_words.rearrange("a p c -> p a c")
-        nc.sync.dma_start(out=w4_lead[:].bitcast(I32), in_=w4_rows[:, :, 0 : 2 * LEAD * P].bitcast(I32))
-        nc.sync.dma_start(out=w4_rest[:].bitcast(I32), in_=w4_rows[:, :, 2 * LEAD * P : 2 * K].bitcast(I32))
+        load_w4(w4_rest, w4_rest_s, LEAD * P, K)
 
         enc_w, dec_w = [], []
         for a in range(PASSES):
@@ -236,12 +241,12 @@ def tile_list_tied_vessel_residual_kernel(tc, tab_words, tab_scales, offs, w, e,
             entries = slice(b * BANK, (b + 1) * BANK)
             half, place = divmod(m, TILES_A_PASS)
             own = slice(place * P, (place + 1) * P)
-            w4_part, tile_in_part = (w4_lead, m) if m < LEAD else (w4_rest, m - LEAD)
+            w4_part, w4_s, tile_in_part = (w4_lead, w4_lead_s, m) if m < LEAD else (w4_rest, w4_rest_s, m - LEAD)
             y = psum.tile([P, BANK], F32, name="y", tag="y", bufs=3)
             short_cut = [
                 (
                     w4_part[:, a, 2 * tile_in_part * P : 2 * (tile_in_part + 1) * P].bitcast(FP4X4),
-                    w4_s[:, a, m * P : (m + 1) * P],
+                    w4_s[:, a, tile_in_part * P : (tile_in_part + 1) * P],
                     v_w[a][:, entries].bitcast(FP8X4),
                     v_s[a][:, entries],
                 )

@@ -31,8 +31,10 @@ QUAD = P // QUADS
 LIVE = 4
 RUN = 8
 LINE = 4
-D_AFTER = 5
-LEAD = 2
+EARLY = 5
+PIECE = 256
+PIECES = S // PIECE
+LEAD = 3
 SHARE = 3
 
 
@@ -40,7 +42,6 @@ def tile_list_tied_vessel_residual_kernel(tc, tab_words, tab_scales, offs, w, e,
     nc = tc.nc
     with ExitStack() as ctx:
         keep = ctx.enter_context(tc.tile_pool(name="keep", bufs=1))
-        ring = ctx.enter_context(tc.tile_pool(name="ring", bufs=3))
         psum = ctx.enter_context(tc.psum_pool(name="psum", bufs=1))
 
         def held(name, shape, dtype, on=None):
@@ -51,36 +52,38 @@ def tile_list_tied_vessel_residual_kernel(tc, tab_words, tab_scales, offs, w, e,
         tab_w = [held(f"tab_w{a}", [P, T], I32) for a in range(PASSES)]
         w_raw = [held(f"w_raw{a}", [P, PACK * H], F32) for a in range(PASSES)]
         state = [held(f"state{m}", [P, T], F32) for m in range(ROW_TILES)]
-        picked = [held(f"picked{m}", [P, S], F32) for m in range(ROW_TILES)]
+        picked = [held(f"picked{m}", [P, S], F32)[:] for m in range(EARLY)]
+        late = held("late", [P, (ROW_TILES - EARLY) * S], F32)
+        picked = picked + [late[:, j * S : (j + 1) * S] for j in range(ROW_TILES - EARLY)]
         w4_lead = held("w4_lead", [P, PASSES, 2 * LEAD * P], U8)
         w4_rest = held("w4_rest", [P, PASSES, 2 * (K - LEAD * P)], U8)
         w4_lead_s = held("w4_lead_s", [P, PASSES, LEAD * P], U8)
         w4_rest_s = held("w4_rest_s", [P, PASSES, K - LEAD * P], U8)
         e_rows = held("e_rows", [P, P], F32)
-        d_rows = [held(f"d_rows{a}", [P, P], F32) for a in range(PASSES)]
+        d_rows = held("d_rows", [P, P], F32)
         ident = held("ident", [P, P], F32)
         v_w = [held(f"v_w{a}", [P, S], U32) for a in range(PASSES)]
         v_rows = held("v_rows", [P, S], U8)
         v_s = [held(f"v_s{a}", [P, S], U8) for a in range(PASSES)]
         enc_in = [held(f"enc_in{a}", [P, H * PACK], BF16) for a in range(PASSES)]
         enc_s = [held(f"enc_s{a}", [P, H], U8) for a in range(PASSES)]
-        dec_in = [held(f"dec_in{a}", [P, K_PASS * PACK], BF16) for a in range(PASSES)]
         dec_s = [held(f"dec_s{a}", [P, K_PASS], U8) for a in range(PASSES)]
         h_rows = [held(f"h_rows{b}", [P, PACK * BANK], BF16) for b in range(HALVES)]
-        h_in = [held(f"h_in{b}", [P, BANK * PACK], BF16) for b in range(HALVES)]
+        lead_d = held("lead_d", [P, LEAD - 1], F32)
+        h_in = [held("h_in0", [P, BANK * PACK], BF16), held("h_in1", [P, BANK * PACK], BF16)]
+        dec_in = [held("dec_in0", [P, K_PASS * PACK], BF16), held("dec_in1", [P, K_PASS * PACK], BF16, on="h_in1")]
         h_s = [held(f"h_s{b}", [P, BANK], U8) for b in range(HALVES)]
-        neg_d = [held(f"neg_d{a}", [P, TILES_A_PASS], F32) for a in range(PASSES)]
+        neg_d = held("neg_d", [P, 1], F32)
         e_cols = held("e_cols", [P, PACK], F32)
         warm = held("warm", [P, 1], F32)
 
         nc.gpsimd.memset(tab_s[QUAD : 2 * QUAD, :].bitcast(I32), 0)
         nc.gpsimd.memset(tab_s[2 * QUAD : P, :].bitcast(I32), 0)
         nc.vector.memset(e_rows[:], 0.0)
-        for a in range(PASSES):
-            nc.vector.memset(d_rows[a][:], 0.0)
+        nc.vector.memset(d_rows[:], 0.0)
         make_identity(nc, ident[:])
 
-        nc.scalar.activation(out=warm[:], in_=d_rows[0][:, 0:1], func=ACT.Gelu_apprx_tanh)
+        nc.scalar.activation(out=warm[:], in_=e_rows[:, 0:1], func=ACT.Gelu_apprx_tanh)
 
         def load_table(a):
             nc.sync.dma_start(out=tab_w[a][:], in_=tab_words[a].rearrange("p t i -> p (t i)").bitcast(I32))
@@ -89,18 +92,22 @@ def tile_list_tied_vessel_residual_kernel(tc, tab_words, tab_scales, offs, w, e,
             rows = w[a * K_PASS : (a + 1) * K_PASS, :]
             nc.sync.dma_start(out=w_raw[a][:], in_=rows.rearrange("(p i) r -> p (i r)", i=PACK))
 
-        def load_d(a):
-            rows = d[a * K_PASS : (a + 1) * K_PASS]
-            nc.sync.dma_start(out=d_rows[a][0:TILES_A_PASS, :], in_=rows.rearrange("(m p) -> m p", p=P))
+        def load_d(rows, first, last):
+            nc.sync.dma_start(out=rows, in_=d[first * P : last * P].rearrange("(m p) -> m p", p=P))
 
         def load_state(m):
             nc.sync.dma_start(out=state[m][:], in_=gT[m * P : (m + 1) * P, :])
 
         def pick_words(a):
-            nc.vector.tensor_copy(v_w[a][:], tab_w[a][:].bitcast(U32).indirect(offsets[:]))
+            if a < PASSES - 1:
+                nc.vector.tensor_copy(v_w[a][:], tab_w[a][:].bitcast(U32).indirect(offsets[:]))
+                return
+            for b in range(HALVES):
+                window = tab_w[a][:].bitcast(U32).indirect(offsets[:, b * BANK // GROUP : (b + 1) * BANK // GROUP])
+                nc.vector.tensor_copy(v_w[a][:, b * BANK : (b + 1) * BANK], window)
 
         def pick_state(m):
-            nc.vector.tensor_copy(picked[m][:], state[m][:].indirect(offsets[:]))
+            nc.vector.tensor_copy(picked[m], state[m][:].indirect(offsets[:]))
 
         def quantize(codes, scales, grouped):
             nc.vector.quantize_mx(out=codes[:].bitcast(FP8X4), scales=scales[:], in_=grouped[:])
@@ -125,16 +132,13 @@ def tile_list_tied_vessel_residual_kernel(tc, tab_words, tab_scales, offs, w, e,
                 pairs = turned[:].rearrange("c t p -> c (t p)").bitcast(BF16)
                 nc.scalar.copy(out=target[:, :, u, :, :], in_=pairs.rearrange("c (t p x) -> c p x t", t=PACK, x=2))
 
-        def to_partitions(rows):
-            columns = psum.tile([P, BANK], F32, name="columns", tag="y", bufs=3)
+        def to_partitions(rows, bank):
+            columns = psum.tile([P, BANK], F32, name="columns", tag=bank, bufs=1)
             nc.tensor.transpose(columns[:, 0:P], rows[:], ident[:])
             return columns
 
         nc.sync.dma_start(offsets[:], offs)
         nc.sync.dma_start(out=tab_s[0:QUAD, :].bitcast(I32), in_=tab_scales.rearrange("a j t -> (a j) t").bitcast(I32))
-        for a in range(PASSES):
-            load_w(a)
-            load_table(a)
         nc.vector.tensor_copy(v_rows[:], tab_s[:].indirect(offsets[:]))
 
         def move_plane(a):
@@ -145,60 +149,87 @@ def tile_list_tied_vessel_residual_kernel(tc, tab_words, tab_scales, offs, w, e,
                     in_=v_rows[row : row + LIVE, :].bitcast(I32),
                 )
 
-        move_plane(0)
+        for a in range(PASSES):
+            load_w(a)
+            if a == PASSES - 1:
+                nc.sync.dma_start(
+                    out=e_rows[0:PACK, :].rearrange("t (g s) -> t g s", s=RUN),
+                    in_=e.rearrange("(g t s) -> t g s", t=PACK, s=RUN),
+                )
+                load_d(e_rows[PACK : 2 * PACK, :], 0, TILES_A_PASS)
+            load_table(a)
+            move_plane(a)
         load_state(0)
-        nc.sync.dma_start(
-            out=e_rows[0:PACK, :].rearrange("t (g s) -> t g s", s=RUN),
-            in_=e.rearrange("(g t s) -> t g s", t=PACK, s=RUN),
-        )
-        move_plane(1)
-        for m in range(1, D_AFTER):
-            load_state(m)
-        load_d(1)
-        for m in range(D_AFTER, ROW_TILES - 1):
-            load_state(m)
-        load_d(0)
 
-        def load_w4(words, scales, first, last):
+        def load_w4_scales(scales, first, last):
             for q in range(QUADS):
                 nc.sync.dma_start(
                     out=scales[QUAD * q : QUAD * q + LIVE, :, :].bitcast(I32),
                     in_=w4_scales[:, LIVE * q : LIVE * (q + 1), first:last].rearrange("a j n -> j a n").bitcast(I32),
                 )
+
+        def load_w4_words(words, first, last):
             rows = w4_words.rearrange("a p c -> p a c")
             nc.sync.dma_start(out=words[:].bitcast(I32), in_=rows[:, :, 2 * first : 2 * last].bitcast(I32))
 
-        load_w4(w4_lead, w4_lead_s, 0, LEAD * P)
-        load_state(ROW_TILES - 1)
-        load_w4(w4_rest, w4_rest_s, LEAD * P, K)
+        for m in range(1, EARLY - 1):
+            load_state(m)
+        load_d(d_rows[0:TILES_A_PASS, :], TILES_A_PASS, ROW_TILES)
+        load_w4_scales(w4_lead_s, 0, LEAD * P)
+        load_state(EARLY - 1)
+        load_w4_words(w4_lead, 0, LEAD * P)
+        load_state(EARLY)
+        load_w4_scales(w4_rest_s, LEAD * P, K)
+        load_w4_words(w4_rest, LEAD * P, K)
+        for m in range(EARLY + 1, ROW_TILES):
+            load_state(m)
 
         enc_w, dec_w = [], []
         for a in range(PASSES):
             cast_w(a)
             enc_w.append(held(f"enc_w{a}", [P, H], U32))
             quantize(enc_w[a], enc_s[a], enc_in[a])
-            turn_w(a)
+            if a == 0:
+                turn_w(a)
             pick_words(a)
             if a == 0:
                 dec_w.append(held("dec_w0", [P, K_PASS], U32, on="tab_w0"))
                 quantize(dec_w[0], dec_s[0], dec_in[0])
         pick_state(0)
-        nc.scalar.copy(out=e_cols[:], in_=to_partitions(e_rows)[:, 0:PACK])
-        dec_w.append(held("dec_w1", [P, K_PASS], U32, on="e_rows"))
-        quantize(dec_w[1], dec_s[1], dec_in[1])
+        columns = to_partitions(e_rows, "y2")
+        nc.scalar.copy(out=e_cols[:], in_=columns[:, 0:PACK])
+        d_cols = columns[:, PACK : 2 * PACK]
+
+        def negate(target, source):
+            nc.scalar.activation(out=target, in_=source, func=ACT.Copy, scale=-1.0)
+
+        woven = (ROW_TILES - EARLY) * PIECES
+        first_woven = LEAD - 1
+        slots = late[:].rearrange("p (k c) -> p k c", c=PIECE)
+        negate(lead_d[:], d_cols[:, 0:first_woven])
+        negate(slots[:, 0, 0:1], d_cols[:, first_woven:LEAD])
+        negate(slots[:, 1 : 2 + LEAD, 0], d_cols)
+        negate(slots[:, 2 + LEAD, 0:1], d_cols[:, LEAD : LEAD + 1])
 
         def encode(b):
             entries = slice(b * BANK, (b + 1) * BANK)
             acts = []
+            if b == 0:
+                pairs = [held("acts0", [P, 2, BANK], F32)] * 2
+            else:
+                pairs = [held(f"acts_{home}", [P, 2, BANK], F32, on=home) for home in ("h_rows0", "lead_d")]
 
             def scale_units(t):
                 nc.scalar.activation(
-                    out=h_rows[b][:, t * BANK : (t + 1) * BANK], in_=acts[t][:], func=ACT.Copy, scale=e_cols[:, t : t + 1]
+                    out=h_rows[b][:, t * BANK : (t + 1) * BANK], in_=acts[t], func=ACT.Copy, scale=e_cols[:, t : t + 1]
                 )
 
             for t in range(PACK):
                 units = slice(t * P, (t + 1) * P)
-                acc = psum.tile([P, BANK], F32, name="acc", tag="acc", bufs=3)
+                if b and t == PACK - 1:
+                    acc = psum.tile([P, BANK], F32, name="acc", tag="y0", bufs=1)
+                else:
+                    acc = psum.tile([P, BANK], F32, name="acc", tag="acc", bufs=3)
                 for a in reversed(range(PASSES)):
                     nc.tensor.matmul_mx(
                         out=acc[:],
@@ -209,8 +240,8 @@ def tile_list_tied_vessel_residual_kernel(tc, tab_words, tab_scales, offs, w, e,
                         start=(a == PASSES - 1),
                         stop=(a == 0),
                     )
-                act = ring.tile([P, BANK], F32, name="act", tag="act")
-                nc.scalar.activation(out=act[:], in_=acc[:], func=ACT.Gelu_apprx_tanh, scale=e_cols[:, t : t + 1])
+                act = pairs[t // 2][:, t % 2, :]
+                nc.scalar.activation(out=act, in_=acc[:], func=ACT.Gelu_apprx_tanh, scale=e_cols[:, t : t + 1])
                 acts.append(act)
                 if t > 0:
                     scale_units(t - 1)
@@ -220,29 +251,29 @@ def tile_list_tied_vessel_residual_kernel(tc, tab_words, tab_scales, offs, w, e,
                 in_=h_rows[b][:].rearrange("p (t c x) -> p c t x", t=PACK, x=LINE),
             )
 
-        def negate_d(a):
-            nc.scalar.activation(out=neg_d[a][:], in_=to_partitions(d_rows[a])[:, 0:TILES_A_PASS], func=ACT.Copy, scale=-1.0)
-
-        for b in range(HALVES):
-            encode(b)
-        for m in range(1, D_AFTER):
+        encode(0)
+        for m in range(1, EARLY - 1):
             pick_state(m)
-        negate_d(1)
-        h_w = [held("h_w0", [P, BANK], U32, on="d_rows1")]
+        late_cols = to_partitions(d_rows, "y2")
+        h_w = [held("h_w0", [P, BANK], U32, on="d_rows")]
         quantize(h_w[0], h_s[0], h_in[0])
-        for m in range(D_AFTER, ROW_TILES - 1):
-            pick_state(m)
-        negate_d(0)
-        h_w.append(held("h_w1", [P, BANK], U32, on="d_rows0"))
-        quantize(h_w[1], h_s[1], h_in[1])
-        pick_state(ROW_TILES - 1)
+        pick_state(EARLY - 1)
+        pairs_left = (woven - 3 - LEAD) // HALVES
+        negate(
+            slots[:, 3 + LEAD : woven, 0].rearrange("p (m b) -> p m b", b=HALVES),
+            late_cols[:, 0:pairs_left].unsqueeze(2).to_broadcast([P, pairs_left, HALVES]),
+        )
+        negate(neg_d[:], late_cols[:, TILES_A_PASS - 1 : TILES_A_PASS])
 
-        def decode(m, b, step):
+        order = [(m, b) for b in range(HALVES) for m in range(LEAD)]
+        order = order + [(m, b) for m in range(LEAD, ROW_TILES) for b in range(HALVES)]
+
+        def decode(m, b, step, scale, bank):
             entries = slice(b * BANK, (b + 1) * BANK)
             half, place = divmod(m, TILES_A_PASS)
             own = slice(place * P, (place + 1) * P)
             w4_part, w4_s, tile_in_part = (w4_lead, w4_lead_s, m) if m < LEAD else (w4_rest, w4_rest_s, m - LEAD)
-            y = psum.tile([P, BANK], F32, name="y", tag="y", bufs=3)
+            y = psum.tile([P, BANK], F32, name="y", tag=bank, bufs=1)
             short_cut = [
                 (
                     w4_part[:, a, 2 * tile_in_part * P : 2 * (tile_in_part + 1) * P].bitcast(FP4X4),
@@ -253,7 +284,7 @@ def tile_list_tied_vessel_residual_kernel(tc, tab_words, tab_scales, offs, w, e,
                 for a in range(PASSES)
             ]
             tied = [(dec_w[half][:, own].bitcast(FP8X4), dec_s[half][:, own], h_w[b][:].bitcast(FP8X4), h_s[b][:])]
-            terms = tied + short_cut if b == 0 else short_cut + tied
+            terms = short_cut + tied
             for number, (lhsT, lhsT_scale, rhs, rhs_scale) in enumerate(terms):
                 nc.tensor.matmul_mx(
                     out=y[:],
@@ -264,27 +295,36 @@ def tile_list_tied_vessel_residual_kernel(tc, tab_words, tab_scales, offs, w, e,
                     start=(number == 0),
                     stop=(number == len(terms) - 1),
                 )
-            nc.scalar.activation(out=step, in_=y[:], func=ACT.Copy, scale=neg_d[half][:, place : place + 1])
+            nc.scalar.activation(out=step, in_=y[:], func=ACT.Copy, scale=scale)
 
         def put_back(m, first, count, step):
             window = state[m][:].indirect(offsets[:, first // GROUP : (first + count) // GROUP])
             nc.vector.tensor_tensor(window, picked[m][:, first : first + count], step, ADD)
 
-        def update_half(m, b, step):
-            decode(m, b, step[:])
-            put_back(m, b * BANK, BANK, step[:])
-
-        def update_whole(m):
-            step = ring.tile([P, S], F32, name="step", tag="step")
-            for b in range(HALVES):
-                decode(m, b, step[:, b * BANK : (b + 1) * BANK])
-            put_back(m, 0, S, step[:])
-
-        for m in range(LEAD):
-            update_half(m, 0, held(f"lead_step{m}", [P, BANK], F32))
-        for m in range(ROW_TILES):
-            if m < LEAD:
-                update_half(m, 1, ring.tile([P, BANK], F32, name="step", tag="step"))
+        for i, (m, b) in enumerate(order):
+            k = i - first_woven
+            if i < first_woven:
+                home = f"step{i}"
             else:
-                update_whole(m)
-            nc.sync.dma_start(out=out[m * P : (m + 1) * P, :], in_=state[m][:])
+                home = "step0" if k % 2 else "h_rows1"
+            step = held(f"step{i}", [P, BANK], F32, on=home)
+            if k < 0:
+                scale = lead_d[:, i : i + 1]
+            else:
+                scale = slots[:, k, 0:1] if k < woven else neg_d[:]
+            decode(m, b, step[:], scale, f"y{i % 3}")
+            put_back(m, b * BANK, BANK, step[:])
+            if 0 <= k < woven:
+                target, part = divmod(k, PIECES)
+                window = state[EARLY + target][:].indirect(offsets[:, part * PIECE // GROUP : (part + 1) * PIECE // GROUP])
+                nc.vector.tensor_copy(slots[:, k, :], window)
+            if i == first_woven - 1:
+                encode(1)
+                h_w.append(held("h_w1", [P, BANK], U32))
+                quantize(h_w[1], h_s[1], h_in[1])
+            if i == LEAD:
+                turn_w(1)
+                dec_w.append(held("dec_w1", [P, K_PASS], U32))
+                quantize(dec_w[1], dec_s[1], dec_in[1])
+            if b == HALVES - 1:
+                nc.sync.dma_start(out=out[m * P : (m + 1) * P, :], in_=state[m][:])

@@ -33,7 +33,7 @@ RUN = 8
 LINE = 4
 EARLY = 5
 PIECE = 256
-PIECES = S // PIECE
+BIT = 128
 LEAD = 3
 SHARE = 3
 
@@ -69,11 +69,12 @@ def tile_list_tied_vessel_residual_kernel(tc, tab_words, tab_scales, offs, w, e,
         enc_s = [held(f"enc_s{a}", [P, H], U8) for a in range(PASSES)]
         dec_s = [held(f"dec_s{a}", [P, K_PASS], U8) for a in range(PASSES)]
         h_rows = [held(f"h_rows{b}", [P, PACK * BANK], BF16) for b in range(HALVES)]
-        lead_d = held("lead_d", [P, LEAD - 1], F32)
+        lead_d = held("lead_d", [P, 1], F32)
         h_in = [held("h_in0", [P, BANK * PACK], BF16), held("h_in1", [P, BANK * PACK], BF16)]
         dec_in = [held("dec_in0", [P, K_PASS * PACK], BF16), held("dec_in1", [P, K_PASS * PACK], BF16, on="h_in1")]
         h_s = [held(f"h_s{b}", [P, BANK], U8) for b in range(HALVES)]
-        neg_d = held("neg_d", [P, 1], F32)
+        neg_d = held("neg_d", [P, 2], F32)
+        zeros = held("zeros", [P, BIT], F32)
         e_cols = held("e_cols", [P, PACK], F32)
         warm = held("warm", [P, 1], F32)
 
@@ -81,6 +82,7 @@ def tile_list_tied_vessel_residual_kernel(tc, tab_words, tab_scales, offs, w, e,
         nc.gpsimd.memset(tab_s[2 * QUAD : P, :].bitcast(I32), 0)
         nc.vector.memset(e_rows[:], 0.0)
         nc.vector.memset(d_rows[:], 0.0)
+        nc.vector.memset(zeros[:], 0.0)
         make_identity(nc, ident[:])
 
         nc.scalar.activation(out=warm[:], in_=e_rows[:, 0:1], func=ACT.Gelu_apprx_tanh)
@@ -126,7 +128,7 @@ def tile_list_tied_vessel_residual_kernel(tc, tab_words, tab_scales, offs, w, e,
             words = enc_in[a][:].bitcast(F32).rearrange("p (t c u) -> p t c u", t=PACK, u=2)
             target = dec_in[a][:].rearrange("c (p u x t) -> c p u x t", u=2, x=2, t=PACK)
             for u in range(2):
-                turned = psum.tile([P, PACK, P], F32, name="turned", tag="turned", bufs=2)
+                turned = psum.tile([P, PACK, P], F32, name="turned", tag="t1" if a else f"t{u}", bufs=1)
                 for t in range(PACK):
                     nc.tensor.transpose(turned[:, t, :], words[:, t, :, u], ident[:])
                 pairs = turned[:].rearrange("c t p -> c (t p)").bitcast(BF16)
@@ -203,13 +205,18 @@ def tile_list_tied_vessel_residual_kernel(tc, tab_words, tab_scales, offs, w, e,
         def negate(target, source):
             nc.scalar.activation(out=target, in_=source, func=ACT.Copy, scale=-1.0)
 
-        woven = (ROW_TILES - EARLY) * PIECES
-        first_woven = LEAD - 1
-        slots = late[:].rearrange("p (k c) -> p k c", c=PIECE)
-        negate(lead_d[:], d_cols[:, 0:first_woven])
-        negate(slots[:, 0, 0:1], d_cols[:, first_woven:LEAD])
-        negate(slots[:, 1 : 2 + LEAD, 0], d_cols)
-        negate(slots[:, 2 + LEAD, 0:1], d_cols[:, LEAD : LEAD + 1])
+        pairs_of = [((1, 1), (0, 1))] + [((m + 1, 0), (m, 1)) for m in range(LEAD - 1, ROW_TILES - 2)]
+        bits = late[:, 2 * PIECE :].rearrange("p (g q s c) -> p g q s c", q=2, s=2, c=BIT)
+
+        def spread_d(columns, first, last):
+            for g, pair in enumerate(pairs_of):
+                for s, (m, half) in enumerate(pair):
+                    if first <= m < last:
+                        negate(bits[:, g, :, s, 0], columns[:, m - first : m - first + 1].to_broadcast([P, 2]))
+
+        negate(lead_d[:], d_cols[:, 0:1])
+        negate(late[:, 0 : 2 * PIECE : PIECE], d_cols[:, 1:LEAD])
+        spread_d(d_cols, 0, TILES_A_PASS)
 
         def encode(b):
             entries = slice(b * BANK, (b + 1) * BANK)
@@ -226,10 +233,8 @@ def tile_list_tied_vessel_residual_kernel(tc, tab_words, tab_scales, offs, w, e,
 
             for t in range(PACK):
                 units = slice(t * P, (t + 1) * P)
-                if b and t == PACK - 1:
-                    acc = psum.tile([P, BANK], F32, name="acc", tag="y0", bufs=1)
-                else:
-                    acc = psum.tile([P, BANK], F32, name="acc", tag="acc", bufs=3)
+                bank = "t1" if b and t == PACK - 1 else f"a{(PACK * b + t) % 3}"
+                acc = psum.tile([P, BANK], F32, name="acc", tag=bank, bufs=1)
                 for a in reversed(range(PASSES)):
                     nc.tensor.matmul_mx(
                         out=acc[:],
@@ -254,26 +259,21 @@ def tile_list_tied_vessel_residual_kernel(tc, tab_words, tab_scales, offs, w, e,
         encode(0)
         for m in range(1, EARLY - 1):
             pick_state(m)
-        late_cols = to_partitions(d_rows, "y2")
+        late_cols = to_partitions(d_rows, "t0")
         h_w = [held("h_w0", [P, BANK], U32, on="d_rows")]
         quantize(h_w[0], h_s[0], h_in[0])
         pick_state(EARLY - 1)
-        pairs_left = (woven - 3 - LEAD) // HALVES
-        negate(
-            slots[:, 3 + LEAD : woven, 0].rearrange("p (m b) -> p m b", b=HALVES),
-            late_cols[:, 0:pairs_left].unsqueeze(2).to_broadcast([P, pairs_left, HALVES]),
-        )
-        negate(neg_d[:], late_cols[:, TILES_A_PASS - 1 : TILES_A_PASS])
 
-        order = [(m, b) for b in range(HALVES) for m in range(LEAD)]
-        order = order + [(m, b) for m in range(LEAD, ROW_TILES) for b in range(HALVES)]
+        banks = ["y0", "y1", "y2", "a1"]
+        sums = {}
 
-        def decode(m, b, step, scale, bank):
+        def decode(m, b):
             entries = slice(b * BANK, (b + 1) * BANK)
             half, place = divmod(m, TILES_A_PASS)
             own = slice(place * P, (place + 1) * P)
             w4_part, w4_s, tile_in_part = (w4_lead, w4_lead_s, m) if m < LEAD else (w4_rest, w4_rest_s, m - LEAD)
-            y = psum.tile([P, BANK], F32, name="y", tag=bank, bufs=1)
+            y = psum.tile([P, BANK], F32, name="y", tag=banks[len(sums) % len(banks)], bufs=1)
+            sums.setdefault((m, b), y)
             short_cut = [
                 (
                     w4_part[:, a, 2 * tile_in_part * P : 2 * (tile_in_part + 1) * P].bitcast(FP4X4),
@@ -295,36 +295,52 @@ def tile_list_tied_vessel_residual_kernel(tc, tab_words, tab_scales, offs, w, e,
                     start=(number == 0),
                     stop=(number == len(terms) - 1),
                 )
-            nc.scalar.activation(out=step, in_=y[:], func=ACT.Copy, scale=scale)
 
         def put_back(m, first, count, step):
             window = state[m][:].indirect(offsets[:, first // GROUP : (first + count) // GROUP])
             nc.vector.tensor_tensor(window, picked[m][:, first : first + count], step, ADD)
 
-        for i, (m, b) in enumerate(order):
-            k = i - first_woven
-            if i < first_woven:
-                home = f"step{i}"
-            else:
-                home = "step0" if k % 2 else "h_rows1"
-            step = held(f"step{i}", [P, BANK], F32, on=home)
-            if k < 0:
-                scale = lead_d[:, i : i + 1]
-            else:
-                scale = slots[:, k, 0:1] if k < woven else neg_d[:]
-            decode(m, b, step[:], scale, f"y{i % 3}")
-            put_back(m, b * BANK, BANK, step[:])
-            if 0 <= k < woven:
-                target, part = divmod(k, PIECES)
-                window = state[EARLY + target][:].indirect(offsets[:, part * PIECE // GROUP : (part + 1) * PIECE // GROUP])
-                nc.vector.tensor_copy(slots[:, k, :], window)
-            if i == first_woven - 1:
-                encode(1)
-                h_w.append(held("h_w1", [P, BANK], U32))
-                quantize(h_w[1], h_s[1], h_in[1])
-            if i == LEAD:
+        def update(m, first, count, scale, home):
+            step = held(f"step{m}_{first}", [P, count], F32, on=home)
+            for at in range(first, first + count, BANK):
+                b, inside = divmod(at, BANK)
+                width = min(count, BANK)
+                if (m, b) not in sums:
+                    decode(m, b)
+                nc.scalar.activation(
+                    out=step[:, at - first : at - first + width],
+                    in_=sums[(m, b)][:, inside : inside + width],
+                    func=ACT.Copy,
+                    scale=scale,
+                )
+            put_back(m, first, count, step[:])
+            if first + count == S:
+                nc.sync.dma_start(out=out[m * P : (m + 1) * P, :], in_=state[m][:])
+
+        def late_window(at, count):
+            target, first = divmod(at, S)
+            return state[EARLY + target][:].indirect(offsets[:, first // GROUP : (first + count) // GROUP])
+
+        update(0, 0, BANK, lead_d[:], "step0")
+        update(1, 0, BANK, late[:, 0:1], "step1")
+        nc.vector.tensor_copy(late[:, 0:PIECE], late_window(0, PIECE))
+        encode(1)
+        h_w.append(held("h_w1", [P, BANK], U32))
+        quantize(h_w[1], h_s[1], h_in[1])
+        update(2, 0, BANK, late[:, PIECE : PIECE + 1], "h_rows1")
+        nc.vector.tensor_copy(late[:, PIECE : 2 * PIECE], late_window(PIECE, PIECE))
+        spread_d(late_cols, TILES_A_PASS, ROW_TILES)
+        negate(neg_d[:], late_cols[:, TILES_A_PASS - 2 : TILES_A_PASS])
+        homes = ["step0", "h_rows1"]
+        for g, pair in enumerate(pairs_of):
+            for q in range(2):
+                for s, (m, half) in enumerate(pair):
+                    update(m, half * BANK + q * PIECE, PIECE, bits[:, g, q, s, 0:1], homes[s])
+                    at = 2 * PIECE + (4 * g + 2 * q + s) * BIT
+                    nc.vector.tensor_tensor(bits[:, g, q, s, :], late_window(at, BIT), zeros[:], ADD)
+            if g == 0:
                 turn_w(1)
                 dec_w.append(held("dec_w1", [P, K_PASS], U32))
                 quantize(dec_w[1], dec_s[1], dec_in[1])
-            if b == HALVES - 1:
-                nc.sync.dma_start(out=out[m * P : (m + 1) * P, :], in_=state[m][:])
+        update(ROW_TILES - 2, BANK, BANK, neg_d[:, 0:1], homes[0])
+        update(ROW_TILES - 1, 0, S, neg_d[:, 1:2], homes[1])

@@ -31,11 +31,13 @@ QUAD = P // QUADS
 LIVE = 4
 RUN = 8
 LINE = 4
-EARLY = 5
-PIECE = 256
+QUARTER = 256
+QUARTERS = S // QUARTER
 BIT = 128
+BITS = S // BIT
 LEAD = 3
 SHARE = 3
+RING = 3
 
 
 def tile_list_tied_vessel_residual_kernel(tc, tab_words, tab_scales, offs, w, e, w4_words, w4_scales, gT, d, out):
@@ -47,14 +49,17 @@ def tile_list_tied_vessel_residual_kernel(tc, tab_words, tab_scales, offs, w, e,
         def held(name, shape, dtype, on=None):
             return keep.tile(shape, dtype, name=name, tag=on or name, align_bytes=64)
 
+        def bank(name, shape, tag):
+            return psum.tile(shape, F32, name=name, tag=tag, bufs=1)
+
         offsets = held("offsets", [P, S // GROUP], U16)
         tab_s = held("tab_s", [P, T], U8)
         tab_w = [held(f"tab_w{a}", [P, T], I32) for a in range(PASSES)]
         w_raw = [held(f"w_raw{a}", [P, PACK * H], F32) for a in range(PASSES)]
         state = [held(f"state{m}", [P, T], F32) for m in range(ROW_TILES)]
-        picked = [held(f"picked{m}", [P, S], F32)[:] for m in range(EARLY)]
-        late = held("late", [P, (ROW_TILES - EARLY) * S], F32)
-        picked = picked + [late[:, j * S : (j + 1) * S] for j in range(ROW_TILES - EARLY)]
+        late = held("late", [P, (ROW_TILES - LEAD) * S], F32)
+        picked = [held(f"picked{m}", [P, S], F32)[:] for m in range(LEAD)]
+        picked = picked + [late[:, j * S : (j + 1) * S] for j in range(ROW_TILES - LEAD)]
         w4_lead = held("w4_lead", [P, PASSES, 2 * LEAD * P], U8)
         w4_rest = held("w4_rest", [P, PASSES, 2 * (K - LEAD * P)], U8)
         w4_lead_s = held("w4_lead_s", [P, PASSES, LEAD * P], U8)
@@ -68,14 +73,18 @@ def tile_list_tied_vessel_residual_kernel(tc, tab_words, tab_scales, offs, w, e,
         enc_in = [held(f"enc_in{a}", [P, H * PACK], BF16) for a in range(PASSES)]
         enc_s = [held(f"enc_s{a}", [P, H], U8) for a in range(PASSES)]
         dec_s = [held(f"dec_s{a}", [P, K_PASS], U8) for a in range(PASSES)]
-        h_rows = [held(f"h_rows{b}", [P, PACK * BANK], BF16) for b in range(HALVES)]
-        lead_d = held("lead_d", [P, 1], F32)
-        h_in = [held("h_in0", [P, BANK * PACK], BF16), held("h_in1", [P, BANK * PACK], BF16)]
-        dec_in = [held("dec_in0", [P, K_PASS * PACK], BF16), held("dec_in1", [P, K_PASS * PACK], BF16, on="h_in1")]
+        h_rows = [held(f"h_rows{q}", [P, PACK * QUARTER], BF16) for q in range(QUARTERS)]
+        h_in = [held(f"h_in{q}", [P, QUARTER * PACK], BF16) for q in range(QUARTERS)]
+        dec_in = [
+            held("dec_in0", [P, K_PASS * PACK], BF16),
+            held("dec_in1", [P, K_PASS * PACK], BF16, on=f"h_in{QUARTERS - 1}"),
+        ]
         h_s = [held(f"h_s{b}", [P, BANK], U8) for b in range(HALVES)]
-        neg_d = held("neg_d", [P, 2], F32)
-        zeros = held("zeros", [P, BIT], F32)
+        first_d = held("first_d", [P, 1], F32)
+        lead_d = held("lead_d", [P, LEAD - 1], F32)
+        tail_d = held("tail_d", [P, 3], F32)
         e_cols = held("e_cols", [P, PACK], F32)
+        zeros = held("zeros", [P, BIT], F32)
         warm = held("warm", [P, 1], F32)
 
         nc.gpsimd.memset(tab_s[QUAD : 2 * QUAD, :].bitcast(I32), 0)
@@ -86,6 +95,9 @@ def tile_list_tied_vessel_residual_kernel(tc, tab_words, tab_scales, offs, w, e,
         make_identity(nc, ident[:])
 
         nc.scalar.activation(out=warm[:], in_=e_rows[:, 0:1], func=ACT.Gelu_apprx_tanh)
+
+        def listed(window, first, count):
+            return window.indirect(offsets[:, first // GROUP : (first + count) // GROUP])
 
         def load_table(a):
             nc.sync.dma_start(out=tab_w[a][:], in_=tab_words[a].rearrange("p t i -> p (t i)").bitcast(I32))
@@ -100,19 +112,14 @@ def tile_list_tied_vessel_residual_kernel(tc, tab_words, tab_scales, offs, w, e,
         def load_state(m):
             nc.sync.dma_start(out=state[m][:], in_=gT[m * P : (m + 1) * P, :])
 
-        def pick_words(a):
-            if a < PASSES - 1:
-                nc.vector.tensor_copy(v_w[a][:], tab_w[a][:].bitcast(U32).indirect(offsets[:]))
-                return
-            for b in range(HALVES):
-                window = tab_w[a][:].bitcast(U32).indirect(offsets[:, b * BANK // GROUP : (b + 1) * BANK // GROUP])
-                nc.vector.tensor_copy(v_w[a][:, b * BANK : (b + 1) * BANK], window)
+        def pick_words(a, first, count):
+            nc.vector.tensor_copy(v_w[a][:, first : first + count], listed(tab_w[a][:].bitcast(U32), first, count))
 
         def pick_state(m):
             nc.vector.tensor_copy(picked[m], state[m][:].indirect(offsets[:]))
 
         def quantize(codes, scales, grouped):
-            nc.vector.quantize_mx(out=codes[:].bitcast(FP8X4), scales=scales[:], in_=grouped[:])
+            nc.vector.quantize_mx(out=codes.bitcast(FP8X4), scales=scales, in_=grouped)
 
         def cast_w(a):
             nc.vector.tensor_copy(
@@ -124,18 +131,18 @@ def tile_list_tied_vessel_residual_kernel(tc, tab_words, tab_scales, offs, w, e,
             for t in range(SHARE, PACK):
                 nc.scalar.copy(out=target[:, t], in_=source[:, t])
 
-        def turn_w(a):
+        def turn_w(a, tags):
             words = enc_in[a][:].bitcast(F32).rearrange("p (t c u) -> p t c u", t=PACK, u=2)
             target = dec_in[a][:].rearrange("c (p u x t) -> c p u x t", u=2, x=2, t=PACK)
             for u in range(2):
-                turned = psum.tile([P, PACK, P], F32, name="turned", tag="t1" if a else f"t{u}", bufs=1)
+                turned = bank("turned", [P, PACK, P], tags[u])
                 for t in range(PACK):
                     nc.tensor.transpose(turned[:, t, :], words[:, t, :, u], ident[:])
                 pairs = turned[:].rearrange("c t p -> c (t p)").bitcast(BF16)
                 nc.scalar.copy(out=target[:, :, u, :, :], in_=pairs.rearrange("c (t p x) -> c p x t", t=PACK, x=2))
 
-        def to_partitions(rows, bank):
-            columns = psum.tile([P, BANK], F32, name="columns", tag=bank, bufs=1)
+        def to_partitions(rows, tag):
+            columns = bank("columns", [P, BANK], tag)
             nc.tensor.transpose(columns[:, 0:P], rows[:], ident[:])
             return columns
 
@@ -174,29 +181,30 @@ def tile_list_tied_vessel_residual_kernel(tc, tab_words, tab_scales, offs, w, e,
             rows = w4_words.rearrange("a p c -> p a c")
             nc.sync.dma_start(out=words[:].bitcast(I32), in_=rows[:, :, 2 * first : 2 * last].bitcast(I32))
 
-        for m in range(1, EARLY - 1):
-            load_state(m)
+        load_state(1)
         load_d(d_rows[0:TILES_A_PASS, :], TILES_A_PASS, ROW_TILES)
         load_w4_scales(w4_lead_s, 0, LEAD * P)
-        load_state(EARLY - 1)
+        load_state(2)
         load_w4_words(w4_lead, 0, LEAD * P)
-        load_state(EARLY)
+        load_state(3)
+        load_state(4)
         load_w4_scales(w4_rest_s, LEAD * P, K)
         load_w4_words(w4_rest, LEAD * P, K)
-        for m in range(EARLY + 1, ROW_TILES):
+        for m in range(5, ROW_TILES):
             load_state(m)
 
         enc_w, dec_w = [], []
         for a in range(PASSES):
             cast_w(a)
             enc_w.append(held(f"enc_w{a}", [P, H], U32))
-            quantize(enc_w[a], enc_s[a], enc_in[a])
+            quantize(enc_w[a][:], enc_s[a][:], enc_in[a][:])
             if a == 0:
-                turn_w(a)
-            pick_words(a)
-            if a == 0:
+                turn_w(a, ["t0", "t1"])
+                pick_words(a, 0, S)
                 dec_w.append(held("dec_w0", [P, K_PASS], U32, on="tab_w0"))
-                quantize(dec_w[0], dec_s[0], dec_in[0])
+                quantize(dec_w[0][:], dec_s[0][:], dec_in[0][:])
+        pick_words(1, 0, QUARTER)
+        pick_words(1, QUARTER, S - QUARTER)
         pick_state(0)
         columns = to_partitions(e_rows, "y2")
         nc.scalar.copy(out=e_cols[:], in_=columns[:, 0:PACK])
@@ -205,36 +213,33 @@ def tile_list_tied_vessel_residual_kernel(tc, tab_words, tab_scales, offs, w, e,
         def negate(target, source):
             nc.scalar.activation(out=target, in_=source, func=ACT.Copy, scale=-1.0)
 
-        pairs_of = [((1, 1), (0, 1))] + [((m + 1, 0), (m, 1)) for m in range(LEAD - 1, ROW_TILES - 2)]
-        bits = late[:, 2 * PIECE :].rearrange("p (g q s c) -> p g q s c", q=2, s=2, c=BIT)
+        runs = [(0, range(LEAD), BITS - 2), (18, range(3, 5), BITS), (34, range(5, 7), 3)]
+        marks = late[:].rearrange("p (n c) -> p n c", c=BIT)[:, :, 0]
 
-        def spread_d(columns, first, last):
-            for g, pair in enumerate(pairs_of):
-                for s, (m, half) in enumerate(pair):
+        def spread_d(source, first, last):
+            for start, tiles, turns in runs:
+                for place, m in enumerate(tiles):
                     if first <= m < last:
-                        negate(bits[:, g, :, s, 0], columns[:, m - first : m - first + 1].to_broadcast([P, 2]))
+                        target = marks[:, start + place : start + turns * len(tiles) : len(tiles)]
+                        negate(target, source[:, m - first : m - first + 1].to_broadcast([P, turns]))
 
-        negate(lead_d[:], d_cols[:, 0:1])
-        negate(late[:, 0 : 2 * PIECE : PIECE], d_cols[:, 1:LEAD])
+        negate(first_d[:], d_cols[:, 0:1])
+        negate(lead_d[:], d_cols[:, 1:LEAD])
         spread_d(d_cols, 0, TILES_A_PASS)
 
-        def encode(b):
-            entries = slice(b * BANK, (b + 1) * BANK)
+        def encode(q):
+            entries = slice(q * QUARTER, (q + 1) * QUARTER)
+            homes = ["acts0" if q < 2 else "lead_d", "acts1" if q < 1 else "first_d"]
+            pairs = [held(f"acts{q}_{z}", [P, 2, QUARTER], F32, on=homes[z]) for z in range(2)]
             acts = []
-            if b == 0:
-                pairs = [held("acts0", [P, 2, BANK], F32)] * 2
-            else:
-                pairs = [held(f"acts_{home}", [P, 2, BANK], F32, on=home) for home in ("h_rows0", "lead_d")]
 
             def scale_units(t):
-                nc.scalar.activation(
-                    out=h_rows[b][:, t * BANK : (t + 1) * BANK], in_=acts[t], func=ACT.Copy, scale=e_cols[:, t : t + 1]
-                )
+                target = h_rows[q][:, t * QUARTER : (t + 1) * QUARTER]
+                nc.scalar.activation(out=target, in_=acts[t], func=ACT.Copy, scale=e_cols[:, t : t + 1])
 
             for t in range(PACK):
                 units = slice(t * P, (t + 1) * P)
-                bank = "t1" if b and t == PACK - 1 else f"a{(PACK * b + t) % 3}"
-                acc = psum.tile([P, BANK], F32, name="acc", tag=bank, bufs=1)
+                acc = bank("acc", [P, QUARTER], f"a{(PACK * q + t) % 3}")
                 for a in reversed(range(PASSES)):
                     nc.tensor.matmul_mx(
                         out=acc[:],
@@ -252,95 +257,109 @@ def tile_list_tied_vessel_residual_kernel(tc, tab_words, tab_scales, offs, w, e,
                     scale_units(t - 1)
             scale_units(PACK - 1)
             nc.scalar.copy(
-                out=h_in[b][:].rearrange("p (c x t) -> p c t x", x=LINE, t=PACK),
-                in_=h_rows[b][:].rearrange("p (t c x) -> p c t x", t=PACK, x=LINE),
+                out=h_in[q][:].rearrange("p (c x t) -> p c t x", x=LINE, t=PACK),
+                in_=h_rows[q][:].rearrange("p (t c x) -> p c t x", t=PACK, x=LINE),
             )
 
-        encode(0)
-        for m in range(1, EARLY - 1):
-            pick_state(m)
-        late_cols = to_partitions(d_rows, "t0")
-        h_w = [held("h_w0", [P, BANK], U32, on="d_rows")]
-        quantize(h_w[0], h_s[0], h_in[0])
-        pick_state(EARLY - 1)
+        def quantize_h(q):
+            b, inside = divmod(q * QUARTER, BANK)
+            quantize(h_w[b][:, inside : inside + QUARTER], h_s[b][:, inside : inside + QUARTER], h_in[q][:])
 
-        banks = ["y0", "y1", "y2", "a1"]
+        y_tags = ["y0", "y1", "y2", "t0", "t1"]
         sums = {}
 
-        def decode(m, b):
-            entries = slice(b * BANK, (b + 1) * BANK)
+        def decode(m, first, count):
             half, place = divmod(m, TILES_A_PASS)
             own = slice(place * P, (place + 1) * P)
             w4_part, w4_s, tile_in_part = (w4_lead, w4_lead_s, m) if m < LEAD else (w4_rest, w4_rest_s, m - LEAD)
-            y = psum.tile([P, BANK], F32, name="y", tag=banks[len(sums) % len(banks)], bufs=1)
-            sums.setdefault((m, b), y)
-            short_cut = [
-                (
-                    w4_part[:, a, 2 * tile_in_part * P : 2 * (tile_in_part + 1) * P].bitcast(FP4X4),
-                    w4_s[:, a, tile_in_part * P : (tile_in_part + 1) * P],
-                    v_w[a][:, entries].bitcast(FP8X4),
-                    v_s[a][:, entries],
-                )
-                for a in range(PASSES)
-            ]
-            tied = [(dec_w[half][:, own].bitcast(FP8X4), dec_s[half][:, own], h_w[b][:].bitcast(FP8X4), h_s[b][:])]
-            terms = short_cut + tied
-            for number, (lhsT, lhsT_scale, rhs, rhs_scale) in enumerate(terms):
-                nc.tensor.matmul_mx(
-                    out=y[:],
-                    lhsT=lhsT,
-                    lhsT_scale=lhsT_scale,
-                    rhs=rhs,
-                    rhs_scale=rhs_scale,
-                    start=(number == 0),
-                    stop=(number == len(terms) - 1),
-                )
+            y = bank("y", [P, count], y_tags[len(sums) % len(y_tags)])
+            sums.setdefault((m, first), y)
+            width = BANK if count == BANK else P
+            for a in range(PASSES):
+                for at in range(0, count, width):
+                    entries = slice(first + at, first + at + width)
+                    nc.tensor.matmul_mx(
+                        out=y[:, at : at + width],
+                        lhsT=w4_part[:, a, 2 * tile_in_part * P : 2 * (tile_in_part + 1) * P].bitcast(FP4X4),
+                        lhsT_scale=w4_s[:, a, tile_in_part * P : (tile_in_part + 1) * P],
+                        rhs=v_w[a][:, entries].bitcast(FP8X4),
+                        rhs_scale=v_s[a][:, entries],
+                        start=(a == 0 and at == 0),
+                        stop=False,
+                    )
+            b, inside = divmod(first, BANK)
+            nc.tensor.matmul_mx(
+                out=y[:],
+                lhsT=dec_w[half][:, own].bitcast(FP8X4),
+                lhsT_scale=dec_s[half][:, own],
+                rhs=h_w[b][:, inside : inside + count].bitcast(FP8X4),
+                rhs_scale=h_s[b][:, inside : inside + count],
+                start=False,
+                stop=True,
+            )
 
-        def put_back(m, first, count, step):
-            window = state[m][:].indirect(offsets[:, first // GROUP : (first + count) // GROUP])
-            nc.vector.tensor_tensor(window, picked[m][:, first : first + count], step, ADD)
-
-        def update(m, first, count, scale, home):
-            step = held(f"step{m}_{first}", [P, count], F32, on=home)
+        def update(m, first, count, scale, step):
+            part = QUARTER if m < LEAD else BANK
             for at in range(first, first + count, BANK):
-                b, inside = divmod(at, BANK)
+                start = at - at % part
                 width = min(count, BANK)
-                if (m, b) not in sums:
-                    decode(m, b)
-                nc.scalar.activation(
-                    out=step[:, at - first : at - first + width],
-                    in_=sums[(m, b)][:, inside : inside + width],
-                    func=ACT.Copy,
-                    scale=scale,
-                )
-            put_back(m, first, count, step[:])
+                if (m, start) not in sums:
+                    decode(m, start, part)
+                source = sums[(m, start)][:, at - start : at - start + width]
+                nc.scalar.activation(out=step[:, at - first : at - first + width], in_=source, func=ACT.Copy, scale=scale)
+            nc.vector.tensor_tensor(listed(state[m][:], first, count), picked[m][:, first : first + count], step, ADD)
             if first + count == S:
                 nc.sync.dma_start(out=out[m * P : (m + 1) * P, :], in_=state[m][:])
 
-        def late_window(at, count):
-            target, first = divmod(at, S)
-            return state[EARLY + target][:].indirect(offsets[:, first // GROUP : (first + count) // GROUP])
+        steps = []
 
-        update(0, 0, BANK, lead_d[:], "step0")
-        update(1, 0, BANK, late[:, 0:1], "step1")
-        nc.vector.tensor_copy(late[:, 0:PIECE], late_window(0, PIECE))
+        def ring_step(count):
+            steps.append(held(f"step{len(steps)}", [P, count], F32, on=f"ring{len(steps) % RING}"))
+            return steps[-1][:]
+
+        def beat(n, m, first, count, step):
+            update(m, first, count, marks[:, n : n + 1], step)
+            target, at = divmod(n * BIT, S)
+            window = listed(state[LEAD + target][:], at, BIT)
+            nc.vector.tensor_tensor(late[:, n * BIT : (n + 1) * BIT], window, zeros[:], ADD)
+
+        encode(0)
+        pick_state(1)
+        late_cols = to_partitions(d_rows, "t1")
+        h_w = [held("h_w0", [P, BANK], U32, on="d_rows"), held("h_w1", [P, BANK], U32)]
+        quantize_h(0)
+        pick_state(2)
+        update(0, 0, QUARTER, first_d[:], ring_step(QUARTER))
+        update(1, 0, QUARTER, lead_d[:, 0:1], ring_step(QUARTER))
         encode(1)
-        h_w.append(held("h_w1", [P, BANK], U32))
-        quantize(h_w[1], h_s[1], h_in[1])
-        update(2, 0, BANK, late[:, PIECE : PIECE + 1], "h_rows1")
-        nc.vector.tensor_copy(late[:, PIECE : 2 * PIECE], late_window(PIECE, PIECE))
+        quantize_h(1)
+        update(2, 0, QUARTER, lead_d[:, 1:2], held("step_q0", [P, QUARTER], F32, on="h_rows1")[:])
         spread_d(late_cols, TILES_A_PASS, ROW_TILES)
-        negate(neg_d[:], late_cols[:, TILES_A_PASS - 2 : TILES_A_PASS])
-        homes = ["step0", "h_rows1"]
-        for g, pair in enumerate(pairs_of):
-            for q in range(2):
-                for s, (m, half) in enumerate(pair):
-                    update(m, half * BANK + q * PIECE, PIECE, bits[:, g, q, s, 0:1], homes[s])
-                    at = 2 * PIECE + (4 * g + 2 * q + s) * BIT
-                    nc.vector.tensor_tensor(bits[:, g, q, s, :], late_window(at, BIT), zeros[:], ADD)
-            if g == 0:
-                turn_w(1)
+        negate(tail_d[:], late_cols[:, 1:TILES_A_PASS])
+
+        free = 2 * LEAD - 2
+        for q in range(1, QUARTERS):
+            for j in range(2 * LEAD):
+                c, m = divmod(j, LEAD)
+                if j == free and q + 1 < QUARTERS:
+                    encode(q + 1)
+                    quantize_h(q + 1)
+                    waiting = held(f"waiting{q}", [P, 2, BIT], F32, on=f"h_rows{q + 1}")
+                step = waiting[:, j - free, :] if j >= free and q + 1 < QUARTERS else ring_step(BIT)
+                beat(2 * LEAD * (q - 1) + j, m, q * QUARTER + c * BIT, BIT, step)
+            if q + 2 == QUARTERS:
+                turn_w(1, ["a0", "a1"])
                 dec_w.append(held("dec_w1", [P, K_PASS], U32))
-                quantize(dec_w[1], dec_s[1], dec_in[1])
-        update(ROW_TILES - 2, BANK, BANK, neg_d[:, 0:1], homes[0])
-        update(ROW_TILES - 1, 0, S, neg_d[:, 1:2], homes[1])
+                quantize(dec_w[1][:], dec_s[1][:], dec_in[1][:])
+        start, tiles, turns = runs[1]
+        for c in range(turns):
+            for place, m in enumerate(tiles):
+                beat(start + c * len(tiles) + place, m, c * BIT, BIT, ring_step(BIT))
+        start, tiles, turns = runs[2]
+        for c in range(QUARTERS):
+            for place, m in enumerate(tiles):
+                if c < turns:
+                    beat(start + c * len(tiles) + place, m, c * QUARTER, QUARTER, ring_step(QUARTER))
+                else:
+                    update(m, c * QUARTER, QUARTER, tail_d[:, place : place + 1], ring_step(QUARTER))
+        update(ROW_TILES - 1, 0, S, tail_d[:, 2:3], ring_step(S))

@@ -57,9 +57,8 @@ def tile_list_tied_vessel_residual_kernel(tc, tab_words, tab_scales, offs, w, e,
         tab_w = [held(f"tab_w{a}", [P, T], I32) for a in range(PASSES)]
         w_raw = [held(f"w_raw{a}", [P, PACK * H], F32) for a in range(PASSES)]
         state = [held(f"state{m}", [P, T], F32) for m in range(ROW_TILES)]
-        late = held("late", [P, (ROW_TILES - LEAD) * S], F32)
-        picked = [held(f"picked{m}", [P, S], F32)[:] for m in range(LEAD)]
-        picked = picked + [late[:, j * S : (j + 1) * S] for j in range(ROW_TILES - LEAD)]
+        picks = held("picks", [P, ROW_TILES * S], F32)
+        picked = [picks[:, m * S : (m + 1) * S] for m in range(ROW_TILES)]
         w4_lead = held("w4_lead", [P, PASSES, 2 * LEAD * P], U8)
         w4_rest = held("w4_rest", [P, PASSES, 2 * (K - LEAD * P)], U8)
         w4_lead_s = held("w4_lead_s", [P, PASSES, LEAD * P], U8)
@@ -74,7 +73,8 @@ def tile_list_tied_vessel_residual_kernel(tc, tab_words, tab_scales, offs, w, e,
         enc_s = [held(f"enc_s{a}", [P, H], U8) for a in range(PASSES)]
         dec_s = [held(f"dec_s{a}", [P, K_PASS], U8) for a in range(PASSES)]
         h_rows = [held(f"h_rows{q}", [P, PACK * QUARTER], BF16) for q in range(QUARTERS)]
-        h_in = [held(f"h_in{q}", [P, QUARTER * PACK], BF16) for q in range(QUARTERS)]
+        h_in = [picked[1][:, BANK:S].bitcast(BF16)]
+        h_in = h_in + [held(f"h_in{q}", [P, QUARTER * PACK], BF16)[:] for q in range(1, QUARTERS)]
         dec_in = [
             held("dec_in0", [P, K_PASS * PACK], BF16),
             held("dec_in1", [P, K_PASS * PACK], BF16, on=f"h_in{QUARTERS - 1}"),
@@ -87,8 +87,8 @@ def tile_list_tied_vessel_residual_kernel(tc, tab_words, tab_scales, offs, w, e,
         zeros = held("zeros", [P, BIT], F32)
         warm = held("warm", [P, 1], F32)
 
-        nc.gpsimd.memset(tab_s[QUAD : 2 * QUAD, :].bitcast(I32), 0)
-        nc.gpsimd.memset(tab_s[2 * QUAD : P, :].bitcast(I32), 0)
+        nc.vector.memset(tab_s[QUAD : 2 * QUAD, :].bitcast(I32), 0)
+        nc.vector.memset(tab_s[2 * QUAD : P, :].bitcast(I32), 0)
         nc.vector.memset(e_rows[:], 0.0)
         nc.vector.memset(d_rows[:], 0.0)
         nc.vector.memset(zeros[:], 0.0)
@@ -182,10 +182,10 @@ def tile_list_tied_vessel_residual_kernel(tc, tab_words, tab_scales, offs, w, e,
             nc.sync.dma_start(out=words[:].bitcast(I32), in_=rows[:, :, 2 * first : 2 * last].bitcast(I32))
 
         load_state(1)
-        load_d(d_rows[0:TILES_A_PASS, :], TILES_A_PASS, ROW_TILES)
+        load_d(d_rows[TILES_A_PASS:ROW_TILES, :], TILES_A_PASS, ROW_TILES)
         load_w4_scales(w4_lead_s, 0, LEAD * P)
-        load_state(2)
         load_w4_words(w4_lead, 0, LEAD * P)
+        load_state(2)
         load_state(3)
         load_state(4)
         load_w4_scales(w4_rest_s, LEAD * P, K)
@@ -206,22 +206,38 @@ def tile_list_tied_vessel_residual_kernel(tc, tab_words, tab_scales, offs, w, e,
         pick_words(1, 0, QUARTER)
         pick_words(1, QUARTER, S - QUARTER)
         pick_state(0)
-        columns = to_partitions(e_rows, "y2")
+        columns = to_partitions(e_rows, "y1")
         nc.scalar.copy(out=e_cols[:], in_=columns[:, 0:PACK])
-        d_cols = columns[:, PACK : 2 * PACK]
+        d_cols = columns[:, PACK : PACK + ROW_TILES]
 
         def negate(target, source):
             nc.scalar.activation(out=target, in_=source, func=ACT.Copy, scale=-1.0)
 
-        runs = [(0, range(LEAD), BITS - 2), (18, range(3, 5), BITS), (34, range(5, 7), 3)]
-        marks = late[:].rearrange("p (n c) -> p n c", c=BIT)[:, :, 0]
+        beats = []
+        ahead = [m * S + at for m in (3, 4) for at in (0, BIT, 2 * BIT, 3 * BIT, 4 * BIT, 6 * BIT)] + [5 * S]
+        for c in range(2, BITS):
+            beats.append((0, c * BIT, BIT, 2 * S + c * BIT, BIT))
+            for m in (1, 2):
+                k = 2 * (c - 2) + m - 1
+                beats.append((m, c * BIT, BIT, ahead[k], ahead[k + 1] - ahead[k]))
+        for c in range(BITS):
+            for m in (3, 4):
+                beats.append((m, c * BIT, BIT, 5 * S + (2 * c + m - 3) * BIT, BIT))
+        for c, (first, count) in enumerate([(0, BIT), (BIT, BIT), (QUARTER, QUARTER), (2 * QUARTER, QUARTER)]):
+            for m in (5, 6):
+                beats.append((m, first, count, 7 * S + (2 * c + m - 5) * BIT, BIT))
 
         def spread_d(source, first, last):
-            for start, tiles, turns in runs:
-                for place, m in enumerate(tiles):
-                    if first <= m < last:
-                        target = marks[:, start + place : start + turns * len(tiles) : len(tiles)]
-                        negate(target, source[:, m - first : m - first + 1].to_broadcast([P, turns]))
+            for m in range(first, last):
+                places = [at for tile, start, count, at, width in beats if tile == m]
+                while places:
+                    step = places[1] - places[0] if len(places) > 1 else 1
+                    run = 1
+                    while run < len(places) and places[run] - places[run - 1] == step:
+                        run = run + 1
+                    target = picks[:, places[0] : places[run - 1] + 1 : step]
+                    negate(target, source[:, m : m + 1].to_broadcast([P, run]))
+                    places = places[run:]
 
         negate(first_d[:], d_cols[:, 0:1])
         negate(lead_d[:], d_cols[:, 1:LEAD])
@@ -229,7 +245,7 @@ def tile_list_tied_vessel_residual_kernel(tc, tab_words, tab_scales, offs, w, e,
 
         def encode(q):
             entries = slice(q * QUARTER, (q + 1) * QUARTER)
-            homes = ["acts0" if q < 2 else "lead_d", "acts1" if q < 1 else "first_d"]
+            homes = [["acts0", "h_rows0", "lead_d", "h_in2"][q], "acts1" if q < 1 else "first_d"]
             pairs = [held(f"acts{q}_{z}", [P, 2, QUARTER], F32, on=homes[z]) for z in range(2)]
             acts = []
 
@@ -239,16 +255,16 @@ def tile_list_tied_vessel_residual_kernel(tc, tab_words, tab_scales, offs, w, e,
 
             for t in range(PACK):
                 units = slice(t * P, (t + 1) * P)
-                acc = bank("acc", [P, QUARTER], f"a{(PACK * q + t) % 3}")
-                for a in reversed(range(PASSES)):
+                acc = bank("acc", [P, QUARTER], f"a{(t + 2 * (q // 2)) % PACK}")
+                for a in range(PASSES):
                     nc.tensor.matmul_mx(
                         out=acc[:],
                         lhsT=enc_w[a][:, units].bitcast(FP8X4),
                         lhsT_scale=enc_s[a][:, units],
                         rhs=v_w[a][:, entries].bitcast(FP8X4),
                         rhs_scale=v_s[a][:, entries],
-                        start=(a == PASSES - 1),
-                        stop=(a == 0),
+                        start=(a == 0),
+                        stop=(a == PASSES - 1),
                     )
                 act = pairs[t // 2][:, t % 2, :]
                 nc.scalar.activation(out=act, in_=acc[:], func=ACT.Gelu_apprx_tanh, scale=e_cols[:, t : t + 1])
@@ -257,22 +273,22 @@ def tile_list_tied_vessel_residual_kernel(tc, tab_words, tab_scales, offs, w, e,
                     scale_units(t - 1)
             scale_units(PACK - 1)
             nc.scalar.copy(
-                out=h_in[q][:].rearrange("p (c x t) -> p c t x", x=LINE, t=PACK),
+                out=h_in[q].rearrange("p (c x t) -> p c t x", x=LINE, t=PACK),
                 in_=h_rows[q][:].rearrange("p (t c x) -> p c t x", t=PACK, x=LINE),
             )
 
         def quantize_h(q):
             b, inside = divmod(q * QUARTER, BANK)
-            quantize(h_w[b][:, inside : inside + QUARTER], h_s[b][:, inside : inside + QUARTER], h_in[q][:])
+            quantize(h_w[b][:, inside : inside + QUARTER], h_s[b][:, inside : inside + QUARTER], h_in[q])
 
-        y_tags = ["y0", "y1", "y2", "t0", "t1"]
+        y_tags = ["y0", "y1", "t0", "t1"]
         sums = {}
 
         def decode(m, first, count):
             half, place = divmod(m, TILES_A_PASS)
             own = slice(place * P, (place + 1) * P)
             w4_part, w4_s, tile_in_part = (w4_lead, w4_lead_s, m) if m < LEAD else (w4_rest, w4_rest_s, m - LEAD)
-            y = bank("y", [P, count], y_tags[len(sums) % len(y_tags)])
+            y = bank("y", [P, count], f"a{len(sums) - 1}" if len(sums) in (1, 2) else y_tags[max(len(sums) - 2, 0) % len(y_tags)])
             sums.setdefault((m, first), y)
             width = BANK if count == BANK else P
             for a in range(PASSES):
@@ -317,49 +333,46 @@ def tile_list_tied_vessel_residual_kernel(tc, tab_words, tab_scales, offs, w, e,
             steps.append(held(f"step{len(steps)}", [P, count], F32, on=f"ring{len(steps) % RING}"))
             return steps[-1][:]
 
-        def beat(n, m, first, count, step):
-            update(m, first, count, marks[:, n : n + 1], step)
-            target, at = divmod(n * BIT, S)
-            window = listed(state[LEAD + target][:], at, BIT)
-            nc.vector.tensor_tensor(late[:, n * BIT : (n + 1) * BIT], window, zeros[:], ADD)
+        def beat(n, step):
+            m, first, count, place, width = beats[n]
+            update(m, first, count, picks[:, place : place + 1], step)
+            target, at = divmod(place, S)
+            window = listed(state[target][:], at, width)
+            if width == BIT:
+                nc.vector.tensor_tensor(picks[:, place : place + width], window, zeros[:], ADD)
+            else:
+                nc.vector.tensor_copy(picks[:, place : place + width], window)
 
         encode(0)
-        pick_state(1)
+        nc.vector.tensor_copy(picked[1][:, 0:BANK], listed(state[1][:], 0, BANK))
         late_cols = to_partitions(d_rows, "t1")
         h_w = [held("h_w0", [P, BANK], U32, on="d_rows"), held("h_w1", [P, BANK], U32)]
         quantize_h(0)
-        pick_state(2)
+        nc.vector.tensor_copy(picked[1][:, BANK:S], listed(state[1][:], BANK, BANK))
         update(0, 0, QUARTER, first_d[:], ring_step(QUARTER))
         update(1, 0, QUARTER, lead_d[:, 0:1], ring_step(QUARTER))
+        nc.vector.tensor_copy(picked[2][:, 0:QUARTER], listed(state[2][:], 0, QUARTER))
         encode(1)
         quantize_h(1)
         update(2, 0, QUARTER, lead_d[:, 1:2], held("step_q0", [P, QUARTER], F32, on="h_rows1")[:])
         spread_d(late_cols, TILES_A_PASS, ROW_TILES)
-        negate(tail_d[:], late_cols[:, 1:TILES_A_PASS])
+        negate(tail_d[:], late_cols[:, 5:ROW_TILES])
 
         free = 2 * LEAD - 2
         for q in range(1, QUARTERS):
             for j in range(2 * LEAD):
-                c, m = divmod(j, LEAD)
                 if j == free and q + 1 < QUARTERS:
                     encode(q + 1)
                     quantize_h(q + 1)
                     waiting = held(f"waiting{q}", [P, 2, BIT], F32, on=f"h_rows{q + 1}")
                 step = waiting[:, j - free, :] if j >= free and q + 1 < QUARTERS else ring_step(BIT)
-                beat(2 * LEAD * (q - 1) + j, m, q * QUARTER + c * BIT, BIT, step)
+                beat(2 * LEAD * (q - 1) + j, step)
             if q + 2 == QUARTERS:
-                turn_w(1, ["a0", "a1"])
+                turn_w(1, ["a2", "a3"])
                 dec_w.append(held("dec_w1", [P, K_PASS], U32))
                 quantize(dec_w[1][:], dec_s[1][:], dec_in[1][:])
-        start, tiles, turns = runs[1]
-        for c in range(turns):
-            for place, m in enumerate(tiles):
-                beat(start + c * len(tiles) + place, m, c * BIT, BIT, ring_step(BIT))
-        start, tiles, turns = runs[2]
-        for c in range(QUARTERS):
-            for place, m in enumerate(tiles):
-                if c < turns:
-                    beat(start + c * len(tiles) + place, m, c * QUARTER, QUARTER, ring_step(QUARTER))
-                else:
-                    update(m, c * QUARTER, QUARTER, tail_d[:, place : place + 1], ring_step(QUARTER))
+        for n in range(2 * LEAD * (QUARTERS - 1), len(beats)):
+            beat(n, ring_step(beats[n][2]))
+        for place, m in enumerate((5, 6)):
+            update(m, S - QUARTER, QUARTER, tail_d[:, place : place + 1], ring_step(QUARTER))
         update(ROW_TILES - 1, 0, S, tail_d[:, 2:3], ring_step(S))

@@ -36,7 +36,8 @@ QUARTERS = S // QUARTER
 BIT = 128
 BITS = S // BIT
 LEAD = 3
-SHARE = 3
+W4_PARTS = [(0, 1), (1, 3), (3, 8)]
+SHARE = (3, 4)
 RING = 3
 
 
@@ -59,8 +60,7 @@ def tile_list_tied_vessel_residual_kernel(tc, tab_words, tab_scales, offs, w, e,
         state = [held(f"state{m}", [P, T], F32) for m in range(ROW_TILES)]
         picks = held("picks", [P, ROW_TILES * S], F32)
         picked = [picks[:, m * S : (m + 1) * S] for m in range(ROW_TILES)]
-        w4_lead = held("w4_lead", [P, PASSES, 2 * LEAD * P], U8)
-        w4_rest = held("w4_rest", [P, PASSES, 2 * (K - LEAD * P)], U8)
+        w4_w = [held(f"w4_w{first}", [P, PASSES, 2 * (last - first) * P], U8) for first, last in W4_PARTS]
         w4_lead_s = held("w4_lead_s", [P, PASSES, LEAD * P], U8)
         w4_rest_s = held("w4_rest_s", [P, PASSES, K - LEAD * P], U8)
         e_rows = held("e_rows", [P, P], F32)
@@ -73,12 +73,8 @@ def tile_list_tied_vessel_residual_kernel(tc, tab_words, tab_scales, offs, w, e,
         enc_s = [held(f"enc_s{a}", [P, H], U8) for a in range(PASSES)]
         dec_s = [held(f"dec_s{a}", [P, K_PASS], U8) for a in range(PASSES)]
         h_rows = [held(f"h_rows{q}", [P, PACK * QUARTER], BF16) for q in range(QUARTERS)]
-        h_in = [picked[1][:, BANK:S].bitcast(BF16)]
-        h_in = h_in + [held(f"h_in{q}", [P, QUARTER * PACK], BF16)[:] for q in range(1, QUARTERS)]
-        dec_in = [
-            held("dec_in0", [P, K_PASS * PACK], BF16),
-            held("dec_in1", [P, K_PASS * PACK], BF16, on=f"h_in{QUARTERS - 1}"),
-        ]
+        h_in = [held(f"h_in{q}", [P, QUARTER * PACK], BF16)[:] for q in range(QUARTERS)]
+        dec_in = [held(f"dec_in{a}", [P, K_PASS * PACK], BF16) for a in range(PASSES)]
         h_s = [held(f"h_s{b}", [P, BANK], U8) for b in range(HALVES)]
         first_d = held("first_d", [P, 1], F32)
         lead_d = held("lead_d", [P, LEAD - 1], F32)
@@ -123,12 +119,12 @@ def tile_list_tied_vessel_residual_kernel(tc, tab_words, tab_scales, offs, w, e,
 
         def cast_w(a):
             nc.vector.tensor_copy(
-                enc_in[a][:].rearrange("p (t g s i) -> p g t s i", t=PACK, s=RUN, i=PACK)[:, :, 0:SHARE],
-                w_raw[a][:].rearrange("p (i g t s) -> p g t s i", i=PACK, t=PACK, s=RUN)[:, :, 0:SHARE],
+                enc_in[a][:].rearrange("p (t g s i) -> p g t s i", t=PACK, s=RUN, i=PACK)[:, :, 0 : SHARE[a]],
+                w_raw[a][:].rearrange("p (i g t s) -> p g t s i", i=PACK, t=PACK, s=RUN)[:, :, 0 : SHARE[a]],
             )
             target = enc_in[a][:].rearrange("p (t g z x i) -> p t g z i x", t=PACK, z=RUN // LINE, x=LINE, i=PACK)
             source = w_raw[a][:].rearrange("p (i g t z x) -> p t g z i x", i=PACK, t=PACK, z=RUN // LINE, x=LINE)
-            for t in range(SHARE, PACK):
+            for t in range(SHARE[a], PACK):
                 nc.scalar.copy(out=target[:, t], in_=source[:, t])
 
         def turn_w(a, tags):
@@ -160,14 +156,15 @@ def tile_list_tied_vessel_residual_kernel(tc, tab_words, tab_scales, offs, w, e,
 
         for a in range(PASSES):
             load_w(a)
-            if a == PASSES - 1:
-                nc.sync.dma_start(
-                    out=e_rows[0:PACK, :].rearrange("t (g s) -> t g s", s=RUN),
-                    in_=e.rearrange("(g t s) -> t g s", t=PACK, s=RUN),
-                )
-                load_d(e_rows[PACK : 2 * PACK, :], 0, TILES_A_PASS)
-            load_table(a)
-            move_plane(a)
+        load_table(0)
+        move_plane(0)
+        nc.sync.dma_start(
+            out=e_rows[0:PACK, :].rearrange("t (g s) -> t g s", s=RUN),
+            in_=e.rearrange("(g t s) -> t g s", t=PACK, s=RUN),
+        )
+        load_d(e_rows[PACK : 2 * PACK, :], 0, TILES_A_PASS)
+        load_table(1)
+        move_plane(1)
         load_state(0)
 
         def load_w4_scales(scales, first, last):
@@ -177,19 +174,21 @@ def tile_list_tied_vessel_residual_kernel(tc, tab_words, tab_scales, offs, w, e,
                     in_=w4_scales[:, LIVE * q : LIVE * (q + 1), first:last].rearrange("a j n -> j a n").bitcast(I32),
                 )
 
-        def load_w4_words(words, first, last):
+        def load_w4_words(part):
+            first, last = W4_PARTS[part]
             rows = w4_words.rearrange("a p c -> p a c")
-            nc.sync.dma_start(out=words[:].bitcast(I32), in_=rows[:, :, 2 * first : 2 * last].bitcast(I32))
+            nc.sync.dma_start(out=w4_w[part][:].bitcast(I32), in_=rows[:, :, 2 * first * P : 2 * last * P].bitcast(I32))
 
         load_state(1)
         load_d(d_rows[TILES_A_PASS:ROW_TILES, :], TILES_A_PASS, ROW_TILES)
         load_w4_scales(w4_lead_s, 0, LEAD * P)
-        load_w4_words(w4_lead, 0, LEAD * P)
         load_state(2)
+        load_w4_words(0)
+        load_w4_words(1)
         load_state(3)
         load_state(4)
         load_w4_scales(w4_rest_s, LEAD * P, K)
-        load_w4_words(w4_rest, LEAD * P, K)
+        load_w4_words(2)
         for m in range(5, ROW_TILES):
             load_state(m)
 
@@ -198,11 +197,12 @@ def tile_list_tied_vessel_residual_kernel(tc, tab_words, tab_scales, offs, w, e,
             cast_w(a)
             enc_w.append(held(f"enc_w{a}", [P, H], U32))
             quantize(enc_w[a][:], enc_s[a][:], enc_in[a][:])
+            turn_w(a, ["t0", "t1"])
+        for a in range(PASSES):
+            dec_w.append(held(f"dec_w{a}", [P, K_PASS], U32))
+            quantize(dec_w[a][:], dec_s[a][:], dec_in[a][:])
             if a == 0:
-                turn_w(a, ["t0", "t1"])
                 pick_words(a, 0, S)
-                dec_w.append(held("dec_w0", [P, K_PASS], U32, on="tab_w0"))
-                quantize(dec_w[0][:], dec_s[0][:], dec_in[0][:])
         pick_words(1, 0, QUARTER)
         pick_words(1, QUARTER, S - QUARTER)
         pick_state(0)
@@ -213,19 +213,10 @@ def tile_list_tied_vessel_residual_kernel(tc, tab_words, tab_scales, offs, w, e,
         def negate(target, source):
             nc.scalar.activation(out=target, in_=source, func=ACT.Copy, scale=-1.0)
 
-        beats = []
-        ahead = [m * S + at for m in (3, 4) for at in (0, BIT, 2 * BIT, 3 * BIT, 4 * BIT, 6 * BIT)] + [5 * S]
-        for c in range(2, BITS):
-            beats.append((0, c * BIT, BIT, 2 * S + c * BIT, BIT))
-            for m in (1, 2):
-                k = 2 * (c - 2) + m - 1
-                beats.append((m, c * BIT, BIT, ahead[k], ahead[k + 1] - ahead[k]))
-        for c in range(BITS):
-            for m in (3, 4):
-                beats.append((m, c * BIT, BIT, 5 * S + (2 * c + m - 3) * BIT, BIT))
-        for c, (first, count) in enumerate([(0, BIT), (BIT, BIT), (QUARTER, QUARTER), (2 * QUARTER, QUARTER)]):
-            for m in (5, 6):
-                beats.append((m, first, count, 7 * S + (2 * c + m - 5) * BIT, BIT))
+        beats = [(m, at, BIT) for at in range(QUARTER, S, BIT) for m in range(LEAD)]
+        beats = beats + [(m, at, BIT) for at in range(0, S, BIT) for m in (3, 4)]
+        beats = beats + [(m, at, QUARTER) for at in range(0, S - QUARTER, QUARTER) for m in (5, 6)]
+        beats = [one + (LEAD * S + n * BIT, BIT) for n, one in enumerate(beats)]
 
         def spread_d(source, first, last):
             for m in range(first, last):
@@ -287,7 +278,9 @@ def tile_list_tied_vessel_residual_kernel(tc, tab_words, tab_scales, offs, w, e,
         def decode(m, first, count):
             half, place = divmod(m, TILES_A_PASS)
             own = slice(place * P, (place + 1) * P)
-            w4_part, w4_s, tile_in_part = (w4_lead, w4_lead_s, m) if m < LEAD else (w4_rest, w4_rest_s, m - LEAD)
+            part = sum(m >= last for start, last in W4_PARTS)
+            tile_in_part = m - W4_PARTS[part][0]
+            w4_s, scales = (w4_lead_s, m) if m < LEAD else (w4_rest_s, m - LEAD)
             y = bank("y", [P, count], f"a{len(sums) - 1}" if len(sums) in (1, 2) else y_tags[max(len(sums) - 2, 0) % len(y_tags)])
             sums.setdefault((m, first), y)
             width = BANK if count == BANK else P
@@ -296,8 +289,8 @@ def tile_list_tied_vessel_residual_kernel(tc, tab_words, tab_scales, offs, w, e,
                     entries = slice(first + at, first + at + width)
                     nc.tensor.matmul_mx(
                         out=y[:, at : at + width],
-                        lhsT=w4_part[:, a, 2 * tile_in_part * P : 2 * (tile_in_part + 1) * P].bitcast(FP4X4),
-                        lhsT_scale=w4_s[:, a, tile_in_part * P : (tile_in_part + 1) * P],
+                        lhsT=w4_w[part][:, a, 2 * tile_in_part * P : 2 * (tile_in_part + 1) * P].bitcast(FP4X4),
+                        lhsT_scale=w4_s[:, a, scales * P : (scales + 1) * P],
                         rhs=v_w[a][:, entries].bitcast(FP8X4),
                         rhs_scale=v_s[a][:, entries],
                         start=(a == 0 and at == 0),
@@ -338,20 +331,16 @@ def tile_list_tied_vessel_residual_kernel(tc, tab_words, tab_scales, offs, w, e,
             update(m, first, count, picks[:, place : place + 1], step)
             target, at = divmod(place, S)
             window = listed(state[target][:], at, width)
-            if width == BIT:
-                nc.vector.tensor_tensor(picks[:, place : place + width], window, zeros[:], ADD)
-            else:
-                nc.vector.tensor_copy(picks[:, place : place + width], window)
+            nc.vector.tensor_tensor(picks[:, place : place + width], window, zeros[:], ADD)
 
         encode(0)
-        nc.vector.tensor_copy(picked[1][:, 0:BANK], listed(state[1][:], 0, BANK))
+        pick_state(1)
         late_cols = to_partitions(d_rows, "t1")
         h_w = [held("h_w0", [P, BANK], U32, on="d_rows"), held("h_w1", [P, BANK], U32)]
         quantize_h(0)
-        nc.vector.tensor_copy(picked[1][:, BANK:S], listed(state[1][:], BANK, BANK))
+        pick_state(2)
         update(0, 0, QUARTER, first_d[:], ring_step(QUARTER))
         update(1, 0, QUARTER, lead_d[:, 0:1], ring_step(QUARTER))
-        nc.vector.tensor_copy(picked[2][:, 0:QUARTER], listed(state[2][:], 0, QUARTER))
         encode(1)
         quantize_h(1)
         update(2, 0, QUARTER, lead_d[:, 1:2], held("step_q0", [P, QUARTER], F32, on="h_rows1")[:])
@@ -367,10 +356,6 @@ def tile_list_tied_vessel_residual_kernel(tc, tab_words, tab_scales, offs, w, e,
                     waiting = held(f"waiting{q}", [P, 2, BIT], F32, on=f"h_rows{q + 1}")
                 step = waiting[:, j - free, :] if j >= free and q + 1 < QUARTERS else ring_step(BIT)
                 beat(2 * LEAD * (q - 1) + j, step)
-            if q + 2 == QUARTERS:
-                turn_w(1, ["a2", "a3"])
-                dec_w.append(held("dec_w1", [P, K_PASS], U32))
-                quantize(dec_w[1][:], dec_s[1][:], dec_in[1][:])
         for n in range(2 * LEAD * (QUARTERS - 1), len(beats)):
             beat(n, ring_step(beats[n][2]))
         for place, m in enumerate((5, 6)):

@@ -63,6 +63,8 @@ def tile_list_tied_vessel_residual_kernel(tc, tab_words, tab_scales, offs, w, e,
         w4_w = [held(f"w4_w{first}", [P, PASSES, 2 * (last - first) * P], U8) for first, last in W4_PARTS]
         w4_lead_s = held("w4_lead_s", [P, PASSES, LEAD * P], U8)
         w4_rest_s = held("w4_rest_s", [P, PASSES, K - LEAD * P], U8)
+        e_line = held("e_line", [1, H], F32)
+        e_sorted = held("e_sorted", [P, H], F32)
         e_rows = held("e_rows", [P, P], F32)
         d_rows = held("d_rows", [P, P], F32)
         ident = held("ident", [P, P], F32)
@@ -73,11 +75,12 @@ def tile_list_tied_vessel_residual_kernel(tc, tab_words, tab_scales, offs, w, e,
         enc_s = [held(f"enc_s{a}", [P, H], U8) for a in range(PASSES)]
         dec_s = [held(f"dec_s{a}", [P, K_PASS], U8) for a in range(PASSES)]
         h_rows = [held(f"h_rows{q}", [P, PACK * QUARTER], BF16) for q in range(QUARTERS)]
-        h_in = [held(f"h_in{q}", [P, QUARTER * PACK], BF16)[:] for q in range(QUARTERS)]
+        second_d = held("second_d", [P, 1], F32)
+        h_in = [held(f"h_in{q}", [P, QUARTER * PACK], BF16, on="second_d" if q == 1 else None)[:] for q in range(QUARTERS)]
         dec_in = [held(f"dec_in{a}", [P, K_PASS * PACK], BF16) for a in range(PASSES)]
         h_s = [held(f"h_s{b}", [P, BANK], U8) for b in range(HALVES)]
         first_d = held("first_d", [P, 1], F32)
-        lead_d = held("lead_d", [P, LEAD - 1], F32)
+        lead_d = held("lead_d", [P, 1], F32)
         tail_d = held("tail_d", [P, 3], F32)
         e_cols = held("e_cols", [P, PACK], F32)
         zeros = held("zeros", [P, BIT], F32)
@@ -89,6 +92,7 @@ def tile_list_tied_vessel_residual_kernel(tc, tab_words, tab_scales, offs, w, e,
         nc.vector.memset(d_rows[:], 0.0)
         nc.vector.memset(zeros[:], 0.0)
         make_identity(nc, ident[:])
+        nc.gpsimd.memset(e_sorted[:], 0.0)
 
         nc.scalar.activation(out=warm[:], in_=e_rows[:, 0:1], func=ACT.Gelu_apprx_tanh)
 
@@ -158,10 +162,7 @@ def tile_list_tied_vessel_residual_kernel(tc, tab_words, tab_scales, offs, w, e,
             load_w(a)
         load_table(0)
         move_plane(0)
-        nc.sync.dma_start(
-            out=e_rows[0:PACK, :].rearrange("t (g s) -> t g s", s=RUN),
-            in_=e.rearrange("(g t s) -> t g s", t=PACK, s=RUN),
-        )
+        nc.sync.dma_start(out=e_line[:], in_=e.rearrange("(o r) -> o r", o=1))
         load_d(e_rows[PACK : 2 * PACK, :], 0, TILES_A_PASS)
         load_table(1)
         move_plane(1)
@@ -207,7 +208,14 @@ def tile_list_tied_vessel_residual_kernel(tc, tab_words, tab_scales, offs, w, e,
         pick_words(1, QUARTER, S - QUARTER)
         pick_state(0)
         columns = to_partitions(e_rows, "y1")
-        nc.scalar.copy(out=e_cols[:], in_=columns[:, 0:PACK])
+        nc.scalar.copy(
+            out=e_sorted[0:1, :].rearrange("o (t g s) -> o t g s", t=PACK, s=RUN),
+            in_=e_line[:].rearrange("o (g t s) -> o t g s", t=PACK, s=RUN),
+        )
+        e_turned = bank("e_turned", [P, PACK, P], "y0")
+        for t in range(PACK):
+            nc.tensor.transpose(e_turned[:, t, :], e_sorted[:, t * P : (t + 1) * P], ident[:])
+        nc.scalar.copy(out=e_cols[:], in_=e_turned[:, :, 0])
         d_cols = columns[:, PACK : PACK + ROW_TILES]
 
         def negate(target, source):
@@ -231,12 +239,13 @@ def tile_list_tied_vessel_residual_kernel(tc, tab_words, tab_scales, offs, w, e,
                     places = places[run:]
 
         negate(first_d[:], d_cols[:, 0:1])
-        negate(lead_d[:], d_cols[:, 1:LEAD])
+        negate(second_d[:], d_cols[:, 1:2])
+        negate(lead_d[:], d_cols[:, 2:3])
         spread_d(d_cols, 0, TILES_A_PASS)
 
         def encode(q):
             entries = slice(q * QUARTER, (q + 1) * QUARTER)
-            homes = [["acts0", "h_rows0", "lead_d", "h_in2"][q], "acts1" if q < 1 else "first_d"]
+            homes = [["acts0", "h_rows0", "first_d", "h_rows0"][q], "acts1" if q < 2 else "lead_d"]
             pairs = [held(f"acts{q}_{z}", [P, 2, QUARTER], F32, on=homes[z]) for z in range(2)]
             acts = []
 
@@ -246,7 +255,7 @@ def tile_list_tied_vessel_residual_kernel(tc, tab_words, tab_scales, offs, w, e,
 
             for t in range(PACK):
                 units = slice(t * P, (t + 1) * P)
-                acc = bank("acc", [P, QUARTER], f"a{(t + 2 * (q // 2)) % PACK}")
+                acc = bank("acc", [P, QUARTER], f"a{t if q < 2 else t % 2}")
                 for a in range(PASSES):
                     nc.tensor.matmul_mx(
                         out=acc[:],
@@ -263,6 +272,8 @@ def tile_list_tied_vessel_residual_kernel(tc, tab_words, tab_scales, offs, w, e,
                 if t > 0:
                     scale_units(t - 1)
             scale_units(PACK - 1)
+
+        def weave(q):
             nc.scalar.copy(
                 out=h_in[q].rearrange("p (c x t) -> p c t x", x=LINE, t=PACK),
                 in_=h_rows[q][:].rearrange("p (t c x) -> p c t x", t=PACK, x=LINE),
@@ -272,7 +283,7 @@ def tile_list_tied_vessel_residual_kernel(tc, tab_words, tab_scales, offs, w, e,
             b, inside = divmod(q * QUARTER, BANK)
             quantize(h_w[b][:, inside : inside + QUARTER], h_s[b][:, inside : inside + QUARTER], h_in[q])
 
-        y_tags = ["y0", "y1", "t0", "t1"]
+        y_tags = ["y0", "y1", "t0", "a3", "a2", "t1"]
         sums = {}
 
         def decode(m, first, count):
@@ -281,7 +292,7 @@ def tile_list_tied_vessel_residual_kernel(tc, tab_words, tab_scales, offs, w, e,
             part = sum(m >= last for start, last in W4_PARTS)
             tile_in_part = m - W4_PARTS[part][0]
             w4_s, scales = (w4_lead_s, m) if m < LEAD else (w4_rest_s, m - LEAD)
-            y = bank("y", [P, count], f"a{len(sums) - 1}" if len(sums) in (1, 2) else y_tags[max(len(sums) - 2, 0) % len(y_tags)])
+            y = bank("y", [P, count], f"a{len(sums)}" if len(sums) < LEAD else y_tags[(len(sums) - LEAD) % len(y_tags)])
             sums.setdefault((m, first), y)
             width = BANK if count == BANK else P
             for a in range(PASSES):
@@ -334,24 +345,28 @@ def tile_list_tied_vessel_residual_kernel(tc, tab_words, tab_scales, offs, w, e,
             nc.vector.tensor_tensor(picks[:, place : place + width], window, zeros[:], ADD)
 
         encode(0)
+        weave(0)
         pick_state(1)
         late_cols = to_partitions(d_rows, "t1")
         h_w = [held("h_w0", [P, BANK], U32, on="d_rows"), held("h_w1", [P, BANK], U32)]
         quantize_h(0)
         pick_state(2)
-        update(0, 0, QUARTER, first_d[:], ring_step(QUARTER))
-        update(1, 0, QUARTER, lead_d[:, 0:1], ring_step(QUARTER))
         encode(1)
+        update(0, 0, QUARTER, first_d[:], ring_step(QUARTER))
+        update(1, 0, QUARTER, second_d[:], ring_step(QUARTER))
+        weave(1)
         quantize_h(1)
-        update(2, 0, QUARTER, lead_d[:, 1:2], held("step_q0", [P, QUARTER], F32, on="h_rows1")[:])
+        update(2, 0, QUARTER, lead_d[:], held("step_q0", [P, QUARTER], F32, on="h_rows1")[:])
         spread_d(late_cols, TILES_A_PASS, ROW_TILES)
         negate(tail_d[:], late_cols[:, 5:ROW_TILES])
 
         free = 2 * LEAD - 2
         for q in range(1, QUARTERS):
+            if q + 1 < QUARTERS:
+                encode(q + 1)
             for j in range(2 * LEAD):
                 if j == free and q + 1 < QUARTERS:
-                    encode(q + 1)
+                    weave(q + 1)
                     quantize_h(q + 1)
                     waiting = held(f"waiting{q}", [P, 2, BIT], F32, on=f"h_rows{q + 1}")
                 step = waiting[:, j - free, :] if j >= free and q + 1 < QUARTERS else ring_step(BIT)

@@ -182,8 +182,8 @@ def tile_list_tied_vessel_residual_kernel(tc, tab_words, tab_scales, offs, w, e,
 
         load_state(1)
         load_d(d_rows[TILES_A_PASS:ROW_TILES, :], TILES_A_PASS, ROW_TILES)
-        load_w4_scales(w4_lead_s, 0, LEAD * P)
         load_state(2)
+        load_w4_scales(w4_lead_s, 0, LEAD * P)
         load_w4_words(0)
         load_w4_words(1)
         load_state(3)

@@ -31,24 +31,26 @@ QUAD = P // QUADS
 LIVE = 4
 RUN = 8
 LINE = 4
-QUARTER = 256
-QUARTERS = S // QUARTER
-BIT = 128
-BITS = S // BIT
+PIECE = 128
+PIECES = S // PIECE
 LEAD = 3
-W4_PARTS = [(0, 1), (1, 3), (3, 8)]
+FIRST = 256
 SHARE = (3, 4)
-RING = 3
+LAST = ROW_TILES - 1
 
 
 def tile_list_tied_vessel_residual_kernel(tc, tab_words, tab_scales, offs, w, e, w4_words, w4_scales, gT, d, out):
     nc = tc.nc
     with ExitStack() as ctx:
         keep = ctx.enter_context(tc.tile_pool(name="keep", bufs=1))
+        lane = ctx.enter_context(tc.tile_pool(name="lane", bufs=1))
         psum = ctx.enter_context(tc.psum_pool(name="psum", bufs=1))
 
         def held(name, shape, dtype, on=None):
             return keep.tile(shape, dtype, name=name, tag=on or name, align_bytes=64)
+
+        def placed(name, shape, dtype, half):
+            return lane.tile(shape, dtype, name=name, tag=name, align_bytes=64, offset=int(half * 4 * PIECE))
 
         def bank(name, shape, tag):
             return psum.tile(shape, F32, name=name, tag=tag, bufs=1)
@@ -58,14 +60,12 @@ def tile_list_tied_vessel_residual_kernel(tc, tab_words, tab_scales, offs, w, e,
         tab_w = [held(f"tab_w{a}", [P, T], I32) for a in range(PASSES)]
         w_raw = [held(f"w_raw{a}", [P, PACK * H], F32) for a in range(PASSES)]
         state = [held(f"state{m}", [P, T], F32) for m in range(ROW_TILES)]
-        picks = held("picks", [P, ROW_TILES * S], F32)
-        picked = [picks[:, m * S : (m + 1) * S] for m in range(ROW_TILES)]
-        w4_w = [held(f"w4_w{first}", [P, PASSES, 2 * (last - first) * P], U8) for first, last in W4_PARTS]
-        w4_lead_s = held("w4_lead_s", [P, PASSES, LEAD * P], U8)
-        w4_rest_s = held("w4_rest_s", [P, PASSES, K - LEAD * P], U8)
+        picks = held("picks", [P, LAST * S], F32)
+        w4_parts = [(0, LEAD), (LEAD, ROW_TILES)]
+        w4_w = [held(f"w4_w{first}", [P, PASSES, 2 * (last - first) * P], U8) for first, last in w4_parts]
+        w4_s = [held(f"w4_s{first}", [P, PASSES, (last - first) * P], U8) for first, last in w4_parts]
         e_line = held("e_line", [1, H], F32)
         e_sorted = held("e_sorted", [P, H], F32)
-        e_rows = held("e_rows", [P, P], F32)
         d_rows = held("d_rows", [P, P], F32)
         ident = held("ident", [P, P], F32)
         v_w = [held(f"v_w{a}", [P, S], U32) for a in range(PASSES)]
@@ -73,28 +73,30 @@ def tile_list_tied_vessel_residual_kernel(tc, tab_words, tab_scales, offs, w, e,
         v_s = [held(f"v_s{a}", [P, S], U8) for a in range(PASSES)]
         enc_in = [held(f"enc_in{a}", [P, H * PACK], BF16) for a in range(PASSES)]
         enc_s = [held(f"enc_s{a}", [P, H], U8) for a in range(PASSES)]
-        dec_s = [held(f"dec_s{a}", [P, K_PASS], U8) for a in range(PASSES)]
-        h_rows = [held(f"h_rows{q}", [P, PACK * QUARTER], BF16) for q in range(QUARTERS)]
-        second_d = held("second_d", [P, 1], F32)
-        h_in = [held(f"h_in{q}", [P, QUARTER * PACK], BF16, on="second_d" if q == 1 else None)[:] for q in range(QUARTERS)]
+        enc_w = [held(f"enc_w{a}", [P, H], U32) for a in range(PASSES)]
         dec_in = [held(f"dec_in{a}", [P, K_PASS * PACK], BF16) for a in range(PASSES)]
-        h_s = [held(f"h_s{b}", [P, BANK], U8) for b in range(HALVES)]
+        dec_s = []
+        dec_w = [held(f"dec_w{a}", [P, K_PASS], U32) for a in range(PASSES)]
+        h_in = [held(f"h_in{j}", [P, PIECE * PACK], BF16) for j in range(PIECES)]
+        h_w = [held(f"h_w{j}", [P, PIECE], U32) for j in range(PIECES)]
+        h_s = [held(f"h_s{j}", [P, PIECE], U8) for j in range(PIECES)]
         first_d = held("first_d", [P, 1], F32)
-        lead_d = held("lead_d", [P, 1], F32)
-        tail_d = held("tail_d", [P, 3], F32)
+        third_d = held("third_d", [P, 1], F32)
+        tail_d = held("tail_d", [P, 2], F32)
+        zeros = placed("zeros", [P, PIECE], F32, 20.5)
+        no_bias = held("no_bias", [P, 1], F32)
         e_cols = held("e_cols", [P, PACK], F32)
-        zeros = held("zeros", [P, BIT], F32)
         warm = held("warm", [P, 1], F32)
 
         nc.vector.memset(tab_s[QUAD : 2 * QUAD, :].bitcast(I32), 0)
         nc.vector.memset(tab_s[2 * QUAD : P, :].bitcast(I32), 0)
-        nc.vector.memset(e_rows[:], 0.0)
         nc.vector.memset(d_rows[:], 0.0)
         nc.vector.memset(zeros[:], 0.0)
+        nc.vector.memset(no_bias[:], 0.0)
         make_identity(nc, ident[:])
         nc.gpsimd.memset(e_sorted[:], 0.0)
 
-        nc.scalar.activation(out=warm[:], in_=e_rows[:, 0:1], func=ACT.Gelu_apprx_tanh)
+        nc.scalar.activation(out=warm[:], in_=d_rows[:, P - 1 : P], func=ACT.Gelu_apprx_tanh)
 
         def listed(window, first, count):
             return window.indirect(offsets[:, first // GROUP : (first + count) // GROUP])
@@ -106,17 +108,32 @@ def tile_list_tied_vessel_residual_kernel(tc, tab_words, tab_scales, offs, w, e,
             rows = w[a * K_PASS : (a + 1) * K_PASS, :]
             nc.sync.dma_start(out=w_raw[a][:], in_=rows.rearrange("(p i) r -> p (i r)", i=PACK))
 
-        def load_d(rows, first, last):
-            nc.sync.dma_start(out=rows, in_=d[first * P : last * P].rearrange("(m p) -> m p", p=P))
-
         def load_state(m):
             nc.sync.dma_start(out=state[m][:], in_=gT[m * P : (m + 1) * P, :])
+
+        def load_w4(part):
+            first, last = w4_parts[part]
+            for q in range(QUADS):
+                nc.sync.dma_start(
+                    out=w4_s[part][QUAD * q : QUAD * q + LIVE, :, :].bitcast(I32),
+                    in_=w4_scales[:, LIVE * q : LIVE * (q + 1), first * P : last * P].rearrange("a j n -> j a n").bitcast(I32),
+                )
+            rows = w4_words.rearrange("a p c -> p a c")
+            nc.sync.dma_start(out=w4_w[part][:].bitcast(I32), in_=rows[:, :, 2 * first * P : 2 * last * P].bitcast(I32))
+
+        def move_plane(a):
+            for q in range(QUADS):
+                row = LIVE * (QUADS * a + q)
+                nc.sync.dma_start(
+                    out=v_s[a][QUAD * q : QUAD * q + LIVE, :].bitcast(I32),
+                    in_=v_rows[row : row + LIVE, :].bitcast(I32),
+                )
 
         def pick_words(a, first, count):
             nc.vector.tensor_copy(v_w[a][:, first : first + count], listed(tab_w[a][:].bitcast(U32), first, count))
 
-        def pick_state(m):
-            nc.vector.tensor_copy(picked[m], state[m][:].indirect(offsets[:]))
+        def pick_state(target, m, first, count):
+            nc.vector.tensor_copy(target, listed(state[m][:], first, count))
 
         def quantize(codes, scales, grouped):
             nc.vector.quantize_mx(out=codes.bitcast(FP8X4), scales=scales, in_=grouped)
@@ -141,73 +158,34 @@ def tile_list_tied_vessel_residual_kernel(tc, tab_words, tab_scales, offs, w, e,
                 pairs = turned[:].rearrange("c t p -> c (t p)").bitcast(BF16)
                 nc.scalar.copy(out=target[:, :, u, :, :], in_=pairs.rearrange("c (t p x) -> c p x t", t=PACK, x=2))
 
-        def to_partitions(rows, tag):
-            columns = bank("columns", [P, BANK], tag)
-            nc.tensor.transpose(columns[:, 0:P], rows[:], ident[:])
-            return columns
-
         nc.sync.dma_start(offsets[:], offs)
         nc.sync.dma_start(out=tab_s[0:QUAD, :].bitcast(I32), in_=tab_scales.rearrange("a j t -> (a j) t").bitcast(I32))
         nc.vector.tensor_copy(v_rows[:], tab_s[:].indirect(offsets[:]))
-
-        def move_plane(a):
-            for q in range(QUADS):
-                row = LIVE * (QUADS * a + q)
-                nc.sync.dma_start(
-                    out=v_s[a][QUAD * q : QUAD * q + LIVE, :].bitcast(I32),
-                    in_=v_rows[row : row + LIVE, :].bitcast(I32),
-                )
-
-        for a in range(PASSES):
-            load_w(a)
-        load_table(0)
-        move_plane(0)
+        load_w(0)
         nc.sync.dma_start(out=e_line[:], in_=e.rearrange("(o r) -> o r", o=1))
-        load_d(e_rows[PACK : 2 * PACK, :], 0, TILES_A_PASS)
-        load_table(1)
+        nc.sync.dma_start(out=d_rows[0:ROW_TILES, :], in_=d.rearrange("(m p) -> m p", p=P))
+        load_w(1)
+        move_plane(0)
+        load_table(0)
         move_plane(1)
+        load_table(1)
         load_state(0)
-
-        def load_w4_scales(scales, first, last):
-            for q in range(QUADS):
-                nc.sync.dma_start(
-                    out=scales[QUAD * q : QUAD * q + LIVE, :, :].bitcast(I32),
-                    in_=w4_scales[:, LIVE * q : LIVE * (q + 1), first:last].rearrange("a j n -> j a n").bitcast(I32),
-                )
-
-        def load_w4_words(part):
-            first, last = W4_PARTS[part]
-            rows = w4_words.rearrange("a p c -> p a c")
-            nc.sync.dma_start(out=w4_w[part][:].bitcast(I32), in_=rows[:, :, 2 * first * P : 2 * last * P].bitcast(I32))
-
-        load_state(1)
-        load_d(d_rows[TILES_A_PASS:ROW_TILES, :], TILES_A_PASS, ROW_TILES)
-        load_state(2)
-        load_w4_scales(w4_lead_s, 0, LEAD * P)
-        load_w4_words(0)
-        load_w4_words(1)
-        load_state(3)
-        load_state(4)
-        load_w4_scales(w4_rest_s, LEAD * P, K)
-        load_w4_words(2)
-        for m in range(5, ROW_TILES):
+        load_w4(0)
+        for m in range(1, LEAD + 1):
+            load_state(m)
+        load_w4(1)
+        for m in range(LEAD + 1, ROW_TILES):
             load_state(m)
 
-        enc_w, dec_w = [], []
-        for a in range(PASSES):
-            cast_w(a)
-            enc_w.append(held(f"enc_w{a}", [P, H], U32))
-            quantize(enc_w[a][:], enc_s[a][:], enc_in[a][:])
-            turn_w(a, ["t0", "t1"])
-        for a in range(PASSES):
-            dec_w.append(held(f"dec_w{a}", [P, K_PASS], U32))
-            quantize(dec_w[a][:], dec_s[a][:], dec_in[a][:])
-            if a == 0:
-                pick_words(a, 0, S)
-        pick_words(1, 0, QUARTER)
-        pick_words(1, QUARTER, S - QUARTER)
-        pick_state(0)
-        columns = to_partitions(e_rows, "y1")
+        def negate(target, source):
+            nc.scalar.activation(out=target, in_=source, func=ACT.Copy, scale=-1.0)
+
+        cast_w(0)
+        quantize(enc_w[0][:], enc_s[0][:], enc_in[0][:])
+        turn_w(0, ["t0", "t1"])
+
+        d_turned = bank("d_turned", [P, P], "y1")
+        nc.tensor.transpose(d_turned[:], d_rows[:], ident[:])
         nc.scalar.copy(
             out=e_sorted[0:1, :].rearrange("o (t g s) -> o t g s", t=PACK, s=RUN),
             in_=e_line[:].rearrange("o (g t s) -> o t g s", t=PACK, s=RUN),
@@ -215,164 +193,182 @@ def tile_list_tied_vessel_residual_kernel(tc, tab_words, tab_scales, offs, w, e,
         e_turned = bank("e_turned", [P, PACK, P], "y0")
         for t in range(PACK):
             nc.tensor.transpose(e_turned[:, t, :], e_sorted[:, t * P : (t + 1) * P], ident[:])
+        heads = picks[:].rearrange("p (m j x) -> p m j x", m=LAST, x=PIECE)[:, :, :, 0]
+        end = PIECES - 1
+        negate(first_d[:], d_turned[:, 0:1])
+        negate(heads[:, 0, 1:end], d_turned[:, 0:1].to_broadcast([P, end - 1]))
+        negate(heads[:, 1:LAST, 0:end], d_turned[:, 1:LAST].unsqueeze(2).to_broadcast([P, LAST - 1, end]))
+        negate(heads[:, 0 : LEAD - 1, end], d_turned[:, 0 : LEAD - 1])
+        negate(heads[:, LEAD : LAST - 2, end], d_turned[:, LEAD : LAST - 2])
+        negate(third_d[:], d_turned[:, LEAD - 1 : LEAD])
+        lone_d = {LEAD - 1: third_d[:], LAST - 1: tail_d[:, 0:1]}
+        negate(heads[:, LAST - 1, end : end + 1], d_turned[:, LAST - 2 : LAST - 1])
+        negate(tail_d[:], d_turned[:, LAST - 1 : ROW_TILES])
         nc.scalar.copy(out=e_cols[:], in_=e_turned[:, :, 0])
-        d_cols = columns[:, PACK : PACK + ROW_TILES]
 
-        def negate(target, source):
-            nc.scalar.activation(out=target, in_=source, func=ACT.Copy, scale=-1.0)
+        cast_w(1)
+        quantize(enc_w[1][:], enc_s[1][:], enc_in[1][:])
+        turn_w(1, ["t0", "t1"])
+        dec_s.append(held("dec_s0", [P, K_PASS], U8))
+        quantize(dec_w[0][:], dec_s[0][:], dec_in[0][:])
+        pick_words(0, 0, 2 * PIECE)
+        pick_words(0, 2 * PIECE, S - 2 * PIECE)
+        pick_words(1, 0, PIECE)
+        pick_words(1, PIECE, PIECE)
+        pick_words(1, 2 * PIECE, S - 2 * PIECE)
+        steps = [held(f"steps{z}", [P, 2 * S], F32, on=f"w_raw{z}" if z < PASSES else None) for z in range(ROW_TILES // 2)]
 
-        beats = [(m, at, BIT) for at in range(QUARTER, S, BIT) for m in range(LEAD)]
-        beats = beats + [(m, at, BIT) for at in range(0, S, BIT) for m in (3, 4)]
-        beats = beats + [(m, at, QUARTER) for at in range(0, S - QUARTER, QUARTER) for m in (5, 6)]
-        beats = [one + (LEAD * S + n * BIT, BIT) for n, one in enumerate(beats)]
+        waiting = {}
 
-        def spread_d(source, first, last):
-            for m in range(first, last):
-                places = [at for tile, start, count, at, width in beats if tile == m]
-                while places:
-                    step = places[1] - places[0] if len(places) > 1 else 1
-                    run = 1
-                    while run < len(places) and places[run] - places[run - 1] == step:
-                        run = run + 1
-                    target = picks[:, places[0] : places[run - 1] + 1 : step]
-                    negate(target, source[:, m : m + 1].to_broadcast([P, run]))
-                    places = places[run:]
+        sums_of = {}
 
-        negate(first_d[:], d_cols[:, 0:1])
-        negate(second_d[:], d_cols[:, 1:2])
-        negate(lead_d[:], d_cols[:, 2:3])
-        spread_d(d_cols, 0, TILES_A_PASS)
-
-        def encode(q):
-            entries = slice(q * QUARTER, (q + 1) * QUARTER)
-            homes = [["acts0", "h_rows0", "first_d", "h_rows0"][q], "acts1" if q < 2 else "lead_d"]
-            pairs = [held(f"acts{q}_{z}", [P, 2, QUARTER], F32, on=homes[z]) for z in range(2)]
-            acts = []
-
-            def scale_units(t):
-                target = h_rows[q][:, t * QUARTER : (t + 1) * QUARTER]
-                nc.scalar.activation(out=target, in_=acts[t], func=ACT.Copy, scale=e_cols[:, t : t + 1])
-
-            for t in range(PACK):
-                units = slice(t * P, (t + 1) * P)
-                acc = bank("acc", [P, QUARTER], f"a{t if q < 2 else t % 2}")
-                for a in range(PASSES):
+        def encode(first, count, places, alone):
+            entries = slice(first * PIECE, (first + count) * PIECE)
+            for a in range(PASSES):
+                for t in range(PACK):
+                    units = slice(t * P, (t + 1) * P)
                     nc.tensor.matmul_mx(
-                        out=acc[:],
+                        out=places[t],
                         lhsT=enc_w[a][:, units].bitcast(FP8X4),
                         lhsT_scale=enc_s[a][:, units],
                         rhs=v_w[a][:, entries].bitcast(FP8X4),
                         rhs_scale=v_s[a][:, entries],
-                        start=(a == 0),
-                        stop=(a == PASSES - 1),
+                        start=(a == 0 and t % alone == 0),
+                        stop=(a == PASSES - 1 and t % alone == alone - 1),
                     )
-                act = pairs[t // 2][:, t % 2, :]
-                nc.scalar.activation(out=act, in_=acc[:], func=ACT.Gelu_apprx_tanh, scale=e_cols[:, t : t + 1])
-                acts.append(act)
-                if t > 0:
-                    scale_units(t - 1)
-            scale_units(PACK - 1)
+            for j in range(count):
+                sums_of.setdefault(first + j, [place[:, j * PIECE : (j + 1) * PIECE] for place in places])
 
-        def weave(q):
+        def encode_group(first, count, tags):
+            alone = PACK // len(tags)
+            banks = [bank("acc", [P, alone, count * PIECE], tag) for tag in tags]
+            encode(first, count, [banks[t // alone][:, t % alone, :] for t in range(PACK)], alone)
+
+        groups = {0: (1, ["a0", "a1", "a2", "a3"]), 1: (1, ["t0"]), 2: (1, ["t1"]), 3: (2, ["a0", "a1"]), 5: (2, ["a2", "a3"]), 7: (1, ["a0"])}
+
+        def make_h(j):
+            if j in groups:
+                encode_group(j, *groups[j])
+            sums = sums_of[j]
+            acts = held(f"acts{j}", [P, PACK * PIECE], F32, on={1: "acts0", 2: "first_d", 3: "no_bias"}.get(j))
+            if j == 0:
+                h_rows = placed("h_first", [P, PACK * PIECE], BF16, PIECES + 2)[:]
+            else:
+                h_rows = placed(f"h_rows{j}", [P, PACK * PIECE], BF16, j)[:]
+            for t in range(PACK):
+                own = slice(t * PIECE, (t + 1) * PIECE)
+                nc.scalar.activation(out=acts[:, own], in_=sums[t], func=ACT.Gelu_apprx_tanh, scale=e_cols[:, t : t + 1])
+            for t in range(PACK):
+                own = slice(t * PIECE, (t + 1) * PIECE)
+                nc.scalar.activation(out=h_rows[:, own], in_=acts[:, own], func=ACT.Copy, scale=e_cols[:, t : t + 1])
             nc.scalar.copy(
-                out=h_in[q].rearrange("p (c x t) -> p c t x", x=LINE, t=PACK),
-                in_=h_rows[q][:].rearrange("p (t c x) -> p c t x", t=PACK, x=LINE),
+                out=h_in[j][:].rearrange("p (c x t) -> p c t x", x=LINE, t=PACK),
+                in_=h_rows.rearrange("p (t c x) -> p c t x", t=PACK, x=LINE),
             )
+            quantize(h_w[j][:], h_s[j][:], h_in[j][:])
+            if j > 1:
+                home = placed(f"first_step{j}", [P, PIECE], F32, j) if j > 2 else placed("second_step", [P, PIECE], F32, 20)
+                waiting.setdefault((0, j - 1), home[:])
+            if j > 2:
+                waiting.setdefault((LEAD - 1, j - 3), acts[:, 0:PIECE])
+            if j == end:
+                waiting.setdefault((LEAD - 1, j - 2), placed("third_step", [P, PIECE], F32, j + 1)[:])
 
-        def quantize_h(q):
-            b, inside = divmod(q * QUARTER, BANK)
-            quantize(h_w[b][:, inside : inside + QUARTER], h_s[b][:, inside : inside + QUARTER], h_in[q])
-
-        y_tags = ["y0", "y1", "t0", "a3", "a2", "t1"]
-        sums = {}
+        y_tags = ["y0", "y1"]
+        y_first = ["a0", "a1", "a2", "a3", "a2"]
+        made = []
 
         def decode(m, first, count):
             half, place = divmod(m, TILES_A_PASS)
             own = slice(place * P, (place + 1) * P)
-            part = sum(m >= last for start, last in W4_PARTS)
-            tile_in_part = m - W4_PARTS[part][0]
-            w4_s, scales = (w4_lead_s, m) if m < LEAD else (w4_rest_s, m - LEAD)
-            y = bank("y", [P, count], f"a{len(sums)}" if len(sums) < LEAD else y_tags[(len(sums) - LEAD) % len(y_tags)])
-            sums.setdefault((m, first), y)
-            width = BANK if count == BANK else P
+            part = 0 if m < LEAD else 1
+            col = (m - w4_parts[part][0]) * P
+            y = bank("y", [P, count], y_first[len(made)] if len(made) < len(y_first) else y_tags[len(made) % len(y_tags)])
+            made.append(y)
+            entries = slice(first, first + count)
             for a in range(PASSES):
-                for at in range(0, count, width):
-                    entries = slice(first + at, first + at + width)
-                    nc.tensor.matmul_mx(
-                        out=y[:, at : at + width],
-                        lhsT=w4_w[part][:, a, 2 * tile_in_part * P : 2 * (tile_in_part + 1) * P].bitcast(FP4X4),
-                        lhsT_scale=w4_s[:, a, scales * P : (scales + 1) * P],
-                        rhs=v_w[a][:, entries].bitcast(FP8X4),
-                        rhs_scale=v_s[a][:, entries],
-                        start=(a == 0 and at == 0),
-                        stop=False,
-                    )
-            b, inside = divmod(first, BANK)
-            nc.tensor.matmul_mx(
-                out=y[:],
-                lhsT=dec_w[half][:, own].bitcast(FP8X4),
-                lhsT_scale=dec_s[half][:, own],
-                rhs=h_w[b][:, inside : inside + count].bitcast(FP8X4),
-                rhs_scale=h_s[b][:, inside : inside + count],
-                start=False,
-                stop=True,
-            )
+                nc.tensor.matmul_mx(
+                    out=y[:],
+                    lhsT=w4_w[part][:, a, 2 * col : 2 * (col + P)].bitcast(FP4X4),
+                    lhsT_scale=w4_s[part][:, a, col : col + P],
+                    rhs=v_w[a][:, entries].bitcast(FP8X4),
+                    rhs_scale=v_s[a][:, entries],
+                    start=(a == 0),
+                    stop=False,
+                )
+            for at in range(0, count, PIECE):
+                j = (first + at) // PIECE
+                nc.tensor.matmul_mx(
+                    out=y[:, at : at + PIECE],
+                    lhsT=dec_w[half][:, own].bitcast(FP8X4),
+                    lhsT_scale=dec_s[half][:, own],
+                    rhs=h_w[j][:].bitcast(FP8X4),
+                    rhs_scale=h_s[j][:],
+                    start=False,
+                    stop=(at + PIECE == count),
+                )
+            return y
 
-        def update(m, first, count, scale, step):
-            part = QUARTER if m < LEAD else BANK
-            for at in range(first, first + count, BANK):
-                start = at - at % part
-                width = min(count, BANK)
-                if (m, start) not in sums:
-                    decode(m, start, part)
-                source = sums[(m, start)][:, at - start : at - start + width]
-                nc.scalar.activation(out=step[:, at - first : at - first + width], in_=source, func=ACT.Copy, scale=scale)
-            nc.vector.tensor_tensor(listed(state[m][:], first, count), picked[m][:, first : first + count], step, ADD)
+        def step_of(m, first, count):
+            if (m, first // PIECE) in waiting:
+                return waiting[(m, first // PIECE)]
+            at = (m % 2) * S + first
+            return steps[m // 2][:, at : at + count]
+
+        def picked(m, first, count):
+            if m > 0:
+                return picks[:, (m - 1) * S + first : (m - 1) * S + first + count]
+            return first_picks[:, first : first + count]
+
+        def scatter(m, first, count):
+            nc.vector.tensor_tensor(listed(state[m][:], first, count), picked(m, first, count), step_of(m, first, count), ADD)
             if first + count == S:
                 nc.sync.dma_start(out=out[m * P : (m + 1) * P, :], in_=state[m][:])
 
-        steps = []
+        def follower(m, j):
+            if m == LEAD - 1:
+                return (LEAD, (j - 1) * PIECE, (2 if j == end else 1) * PIECE) if j > 0 else None
+            if j < end - 1 or m < LAST - 2 or (m, j) == (LAST - 1, end - 1):
+                return (m + 1, j * PIECE, PIECE)
+            if (m, j) == (LAST - 2, end - 1):
+                return (m + 1, j * PIECE, 2 * PIECE)
+            if m == LAST - 2:
+                return (LAST, j * PIECE, PIECE)
+            return None
 
-        def ring_step(count):
-            steps.append(held(f"step{len(steps)}", [P, count], F32, on=f"ring{len(steps) % RING}"))
-            return steps[-1][:]
+        def beat(m, j):
+            behind = follower(m, j)
+            scale = picked(behind[0], behind[1], 1) if behind else lone_d[m]
+            if (m, j) == (0, 0):
+                scale = first_d[:]
+            y = decode(m, j * PIECE, PIECE)
+            if (m, j) == (0, 1):
+                nc.scalar.activation(out=step_of(m, j * PIECE, PIECE), in_=y[:], func=ACT.Identity, scale=scale, bias=no_bias[:])
+            else:
+                nc.scalar.activation(out=step_of(m, j * PIECE, PIECE), in_=y[:], func=ACT.Copy, scale=scale)
+            scatter(m, j * PIECE, PIECE)
+            if (m, j) == (1, 0):
+                nc.vector.tensor_tensor(picked(*behind), listed(state[2][:], 0, PIECE), zeros[:], ADD)
+                dec_s.append(placed("dec_s1", [P, K_PASS], U8, 21))
+                quantize(dec_w[1][:], dec_s[1][:], dec_in[1][:])
+            elif behind:
+                pick_state(picked(*behind), *behind)
 
-        def beat(n, step):
-            m, first, count, place, width = beats[n]
-            update(m, first, count, picks[:, place : place + 1], step)
-            target, at = divmod(place, S)
-            window = listed(state[target][:], at, width)
-            nc.vector.tensor_tensor(picks[:, place : place + width], window, zeros[:], ADD)
+        make_h(0)
+        first_picks = placed("first_picks", [P, S], F32, PIECES + 2)
+        pick_state(first_picks[:], 0, 0, S)
 
-        encode(0)
-        weave(0)
-        pick_state(1)
-        late_cols = to_partitions(d_rows, "t1")
-        h_w = [held("h_w0", [P, BANK], U32, on="d_rows"), held("h_w1", [P, BANK], U32)]
-        quantize_h(0)
-        pick_state(2)
-        encode(1)
-        update(0, 0, QUARTER, first_d[:], ring_step(QUARTER))
-        update(1, 0, QUARTER, second_d[:], ring_step(QUARTER))
-        weave(1)
-        quantize_h(1)
-        update(2, 0, QUARTER, lead_d[:], held("step_q0", [P, QUARTER], F32, on="h_rows1")[:])
-        spread_d(late_cols, TILES_A_PASS, ROW_TILES)
-        negate(tail_d[:], late_cols[:, 5:ROW_TILES])
-
-        free = 2 * LEAD - 2
-        for q in range(1, QUARTERS):
-            if q + 1 < QUARTERS:
-                encode(q + 1)
-            for j in range(2 * LEAD):
-                if j == free and q + 1 < QUARTERS:
-                    weave(q + 1)
-                    quantize_h(q + 1)
-                    waiting = held(f"waiting{q}", [P, 2, BIT], F32, on=f"h_rows{q + 1}")
-                step = waiting[:, j - free, :] if j >= free and q + 1 < QUARTERS else ring_step(BIT)
-                beat(2 * LEAD * (q - 1) + j, step)
-        for n in range(2 * LEAD * (QUARTERS - 1), len(beats)):
-            beat(n, ring_step(beats[n][2]))
-        for place, m in enumerate((5, 6)):
-            update(m, S - QUARTER, QUARTER, tail_d[:, place : place + 1], ring_step(QUARTER))
-        update(ROW_TILES - 1, 0, S, tail_d[:, 2:3], ring_step(S))
+        begins = [m if m < LEAD else PIECES + m - LEAD for m in range(LAST)]
+        order = sorted((begins[m] + j, -m, j) for m in range(LAST) for j in range(PIECES))
+        for turn, back, j in order:
+            if (back, j) == (0, 0):
+                make_h(1)
+            if (back, j) == (0, 1):
+                make_h(2)
+            beat(-back, j)
+            if back == 0 and 0 < j < end - 1:
+                make_h(j + 2)
+        for first in range(0, S, BANK):
+            y = decode(LAST, first, BANK)
+            nc.scalar.activation(out=step_of(LAST, first, BANK), in_=y[:], func=ACT.Copy, scale=tail_d[:, 1:2])
+        scatter(LAST, 0, S)

@@ -34,7 +34,7 @@ LINE = 4
 PIECE = 128
 PIECES = S // PIECE
 LEAD = 3
-FIRST = 256
+FIRST = 512
 SHARE = (3, 4)
 LAST = ROW_TILES - 1
 
@@ -77,14 +77,14 @@ def tile_list_tied_vessel_residual_kernel(tc, tab_words, tab_scales, offs, w, e,
         dec_in = [held(f"dec_in{a}", [P, K_PASS * PACK], BF16) for a in range(PASSES)]
         dec_s = []
         dec_w = [held(f"dec_w{a}", [P, K_PASS], U32) for a in range(PASSES)]
-        h_in = [held(f"h_in{j}", [P, PIECE * PACK], BF16) for j in range(PIECES)]
+        h_in = [placed("h_in1", [P, PIECE * PACK], BF16, 28.125) if j == 1 else held(f"h_in{j}", [P, PIECE * PACK], BF16) for j in range(PIECES)]
         h_w = [held(f"h_w{j}", [P, PIECE], U32) for j in range(PIECES)]
-        h_s = [held(f"h_s{j}", [P, PIECE], U8) for j in range(PIECES)]
-        first_d = held("first_d", [P, 1], F32)
+        h_s = [placed("h_s2", [P, PIECE], U8, 36.125) if j == 2 else held(f"h_s{j}", [P, PIECE], U8) for j in range(PIECES)]
+        first_d = placed("first_d", [P, 2 * GROUP], F32, 28)[:, 0:1]
         third_d = held("third_d", [P, 1], F32)
         tail_d = held("tail_d", [P, 2], F32)
         zeros = placed("zeros", [P, PIECE], F32, 20.5)
-        no_bias = held("no_bias", [P, 1], F32)
+        no_bias = placed("no_bias", [P, 2 * GROUP], F32, 36)[:, 0:1]
         e_cols = held("e_cols", [P, PACK], F32)
         warm = held("warm", [P, 1], F32)
 
@@ -92,7 +92,7 @@ def tile_list_tied_vessel_residual_kernel(tc, tab_words, tab_scales, offs, w, e,
         nc.vector.memset(tab_s[2 * QUAD : P, :].bitcast(I32), 0)
         nc.vector.memset(d_rows[:], 0.0)
         nc.vector.memset(zeros[:], 0.0)
-        nc.vector.memset(no_bias[:], 0.0)
+        nc.vector.memset(no_bias, 0.0)
         make_identity(nc, ident[:])
         nc.gpsimd.memset(e_sorted[:], 0.0)
 
@@ -195,7 +195,7 @@ def tile_list_tied_vessel_residual_kernel(tc, tab_words, tab_scales, offs, w, e,
             nc.tensor.transpose(e_turned[:, t, :], e_sorted[:, t * P : (t + 1) * P], ident[:])
         heads = picks[:].rearrange("p (m j x) -> p m j x", m=LAST, x=PIECE)[:, :, :, 0]
         end = PIECES - 1
-        negate(first_d[:], d_turned[:, 0:1])
+        negate(first_d, d_turned[:, 0:1])
         negate(heads[:, 0, 1:end], d_turned[:, 0:1].to_broadcast([P, end - 1]))
         negate(heads[:, 1:LAST, 0:end], d_turned[:, 1:LAST].unsqueeze(2).to_broadcast([P, LAST - 1, end]))
         negate(heads[:, 0 : LEAD - 1, end], d_turned[:, 0 : LEAD - 1])
@@ -216,6 +216,8 @@ def tile_list_tied_vessel_residual_kernel(tc, tab_words, tab_scales, offs, w, e,
         pick_words(1, 0, PIECE)
         pick_words(1, PIECE, PIECE)
         pick_words(1, 2 * PIECE, S - 2 * PIECE)
+        first_picks = held("first_picks", [P, FIRST], F32)
+        pick_state(first_picks[:], 0, 0, FIRST)
         steps = [held(f"steps{z}", [P, 2 * S], F32, on=f"w_raw{z}" if z < PASSES else None) for z in range(ROW_TILES // 2)]
 
         waiting = {}
@@ -246,11 +248,27 @@ def tile_list_tied_vessel_residual_kernel(tc, tab_words, tab_scales, offs, w, e,
 
         groups = {0: (1, ["a0", "a1", "a2", "a3"]), 1: (1, ["t0"]), 2: (1, ["t1"]), 3: (2, ["a0", "a1"]), 5: (2, ["a2", "a3"]), 7: (1, ["a0"])}
 
+        rows_of = []
+
+        def weave(j):
+            nc.scalar.copy(
+                out=h_in[j][:].rearrange("p (c x t) -> p c t x", x=LINE, t=PACK),
+                in_=rows_of[j].rearrange("p (t c x) -> p c t x", t=PACK, x=LINE),
+            )
+
+        def quantize_h(j):
+            quantize(h_w[j][:], h_s[j][:], h_in[j][:])
+
         def make_h(j):
             if j in groups:
                 encode_group(j, *groups[j])
             sums = sums_of[j]
-            acts = held(f"acts{j}", [P, PACK * PIECE], F32, on={1: "acts0", 2: "first_d", 3: "no_bias"}.get(j))
+            if j == 2:
+                acts = placed("acts2", [P, PACK * PIECE], F32, 24.125)
+            elif j == 3:
+                acts = placed("acts3", [P, PACK * PIECE], F32, 32.125)
+            else:
+                acts = held(f"acts{j}", [P, PACK * PIECE], F32)
             if j == 0:
                 h_rows = placed("h_first", [P, PACK * PIECE], BF16, PIECES + 2)[:]
             else:
@@ -261,11 +279,11 @@ def tile_list_tied_vessel_residual_kernel(tc, tab_words, tab_scales, offs, w, e,
             for t in range(PACK):
                 own = slice(t * PIECE, (t + 1) * PIECE)
                 nc.scalar.activation(out=h_rows[:, own], in_=acts[:, own], func=ACT.Copy, scale=e_cols[:, t : t + 1])
-            nc.scalar.copy(
-                out=h_in[j][:].rearrange("p (c x t) -> p c t x", x=LINE, t=PACK),
-                in_=h_rows.rearrange("p (t c x) -> p c t x", t=PACK, x=LINE),
-            )
-            quantize(h_w[j][:], h_s[j][:], h_in[j][:])
+            rows_of.append(h_rows)
+            if j != 1:
+                weave(j)
+            if j not in (1, 2):
+                quantize_h(j)
             if j > 1:
                 home = placed(f"first_step{j}", [P, PIECE], F32, j) if j > 2 else placed("second_step", [P, PIECE], F32, 20)
                 waiting.setdefault((0, j - 1), home[:])
@@ -318,7 +336,9 @@ def tile_list_tied_vessel_residual_kernel(tc, tab_words, tab_scales, offs, w, e,
         def picked(m, first, count):
             if m > 0:
                 return picks[:, (m - 1) * S + first : (m - 1) * S + first + count]
-            return first_picks[:, first : first + count]
+            if first < FIRST:
+                return first_picks[:, first : first + count]
+            return rest_picks[:, first - FIRST : first - FIRST + count]
 
         def scatter(m, first, count):
             nc.vector.tensor_tensor(listed(state[m][:], first, count), picked(m, first, count), step_of(m, first, count), ADD)
@@ -340,10 +360,10 @@ def tile_list_tied_vessel_residual_kernel(tc, tab_words, tab_scales, offs, w, e,
             behind = follower(m, j)
             scale = picked(behind[0], behind[1], 1) if behind else lone_d[m]
             if (m, j) == (0, 0):
-                scale = first_d[:]
+                scale = first_d
             y = decode(m, j * PIECE, PIECE)
             if (m, j) == (0, 1):
-                nc.scalar.activation(out=step_of(m, j * PIECE, PIECE), in_=y[:], func=ACT.Identity, scale=scale, bias=no_bias[:])
+                nc.scalar.activation(out=step_of(m, j * PIECE, PIECE), in_=y[:], func=ACT.Identity, scale=scale, bias=no_bias)
             else:
                 nc.scalar.activation(out=step_of(m, j * PIECE, PIECE), in_=y[:], func=ACT.Copy, scale=scale)
             scatter(m, j * PIECE, PIECE)
@@ -355,8 +375,8 @@ def tile_list_tied_vessel_residual_kernel(tc, tab_words, tab_scales, offs, w, e,
                 pick_state(picked(*behind), *behind)
 
         make_h(0)
-        first_picks = placed("first_picks", [P, S], F32, PIECES + 2)
-        pick_state(first_picks[:], 0, 0, S)
+        rest_picks = placed("rest_picks", [P, S - FIRST], F32, PIECES + 2)
+        pick_state(rest_picks[:], 0, FIRST, S - FIRST)
 
         begins = [m if m < LEAD else PIECES + m - LEAD for m in range(LAST)]
         order = sorted((begins[m] + j, -m, j) for m in range(LAST) for j in range(PIECES))
@@ -366,6 +386,11 @@ def tile_list_tied_vessel_residual_kernel(tc, tab_words, tab_scales, offs, w, e,
             if (back, j) == (0, 1):
                 make_h(2)
             beat(-back, j)
+            if (back, j) == (0, 0):
+                weave(1)
+                quantize_h(1)
+            if (back, j) == (0, 1):
+                quantize_h(2)
             if back == 0 and 0 < j < end - 1:
                 make_h(j + 2)
         for first in range(0, S, BANK):

@@ -81,8 +81,8 @@ def tile_list_tied_vessel_residual_kernel(tc, tab_words, tab_scales, offs, w, e,
         h_w = [held(f"h_w{j}", [P, PIECE], U32) for j in range(PIECES)]
         h_s = [placed("h_s2", [P, PIECE], U8, 36.125) if j == 2 else held(f"h_s{j}", [P, PIECE], U8) for j in range(PIECES)]
         first_d = placed("first_d", [P, 2 * GROUP], F32, 28)[:, 0:1]
-        third_d = held("third_d", [P, 1], F32)
-        tail_d = held("tail_d", [P, 2], F32)
+        even_d = held("even_d", [P, 3], F32)
+        tail_d = held("tail_d", [P, 1], F32)
         zeros = placed("zeros", [P, PIECE], F32, 20.5)
         no_bias = placed("no_bias", [P, 2 * GROUP], F32, 36)[:, 0:1]
         e_cols = held("e_cols", [P, PACK], F32)
@@ -180,6 +180,23 @@ def tile_list_tied_vessel_residual_kernel(tc, tab_words, tab_scales, offs, w, e,
         def negate(target, source):
             nc.scalar.activation(out=target, in_=source, func=ACT.Copy, scale=-1.0)
 
+        end = PIECES - 1
+
+        def follower(m, j):
+            if m == LEAD - 1:
+                return (LEAD, j - 1, 2 if j == end else 1) if j > 0 else None
+            if m < LEAD:
+                return (m + 1, j, 1)
+            if m == 3:
+                return (4, j, 1) if j < 2 else (5, j - 1, 2 if j == end else 1)
+            if m == 4:
+                if j == 0:
+                    return (5, 0, 1)
+                return (6, j - 1, 3 if j == end - 1 else 1) if j < end else None
+            if m == 5:
+                return (LAST, j, 1)
+            return (4, j + 2, 1) if j + 2 <= end else None
+
         cast_w(0)
         quantize(enc_w[0][:], enc_s[0][:], enc_in[0][:])
         turn_w(0, ["t0", "t1"])
@@ -194,16 +211,15 @@ def tile_list_tied_vessel_residual_kernel(tc, tab_words, tab_scales, offs, w, e,
         for t in range(PACK):
             nc.tensor.transpose(e_turned[:, t, :], e_sorted[:, t * P : (t + 1) * P], ident[:])
         heads = picks[:].rearrange("p (m j x) -> p m j x", m=LAST, x=PIECE)[:, :, :, 0]
-        end = PIECES - 1
         negate(first_d, d_turned[:, 0:1])
-        negate(heads[:, 0, 1:end], d_turned[:, 0:1].to_broadcast([P, end - 1]))
-        negate(heads[:, 1:LAST, 0:end], d_turned[:, 1:LAST].unsqueeze(2).to_broadcast([P, LAST - 1, end]))
-        negate(heads[:, 0 : LEAD - 1, end], d_turned[:, 0 : LEAD - 1])
-        negate(heads[:, LEAD : LAST - 2, end], d_turned[:, LEAD : LAST - 2])
-        negate(third_d[:], d_turned[:, LEAD - 1 : LEAD])
-        lone_d = {LEAD - 1: third_d[:], LAST - 1: tail_d[:, 0:1]}
-        negate(heads[:, LAST - 1, end : end + 1], d_turned[:, LAST - 2 : LAST - 1])
-        negate(tail_d[:], d_turned[:, LAST - 1 : ROW_TILES])
+        for m in range(LAST):
+            served = [follower(m, j) for j in range(PIECES) if follower(m, j) and (m, j) != (0, 0)]
+            for tile in sorted({one[0] for one in served}):
+                own = [one[1] for one in served if one[0] == tile]
+                negate(heads[:, tile - 1, own[0] : own[-1] + 1], d_turned[:, m : m + 1].to_broadcast([P, len(own)]))
+        negate(even_d[:], d_turned[:, 2:ROW_TILES:2])
+        negate(tail_d[:], d_turned[:, LAST:ROW_TILES])
+        lone_d = {m: even_d[:, m // 2 - 1 : m // 2] for m in (2, 4, 6)}
         nc.scalar.copy(out=e_cols[:], in_=e_turned[:, :, 0])
 
         cast_w(1)
@@ -345,19 +361,10 @@ def tile_list_tied_vessel_residual_kernel(tc, tab_words, tab_scales, offs, w, e,
             if first + count == S:
                 nc.sync.dma_start(out=out[m * P : (m + 1) * P, :], in_=state[m][:])
 
-        def follower(m, j):
-            if m == LEAD - 1:
-                return (LEAD, (j - 1) * PIECE, (2 if j == end else 1) * PIECE) if j > 0 else None
-            if j < end - 1 or m < LAST - 2 or (m, j) == (LAST - 1, end - 1):
-                return (m + 1, j * PIECE, PIECE)
-            if (m, j) == (LAST - 2, end - 1):
-                return (m + 1, j * PIECE, 2 * PIECE)
-            if m == LAST - 2:
-                return (LAST, j * PIECE, PIECE)
-            return None
-
         def beat(m, j):
             behind = follower(m, j)
+            if behind:
+                behind = (behind[0], behind[1] * PIECE, behind[2] * PIECE)
             scale = picked(behind[0], behind[1], 1) if behind else lone_d[m]
             if (m, j) == (0, 0):
                 scale = first_d
@@ -395,5 +402,5 @@ def tile_list_tied_vessel_residual_kernel(tc, tab_words, tab_scales, offs, w, e,
                 make_h(j + 2)
         for first in range(0, S, BANK):
             y = decode(LAST, first, BANK)
-            nc.scalar.activation(out=step_of(LAST, first, BANK), in_=y[:], func=ACT.Copy, scale=tail_d[:, 1:2])
+            nc.scalar.activation(out=step_of(LAST, first, BANK), in_=y[:], func=ACT.Copy, scale=tail_d[:])
         scatter(LAST, 0, S)

@@ -34,7 +34,7 @@ LINE = 4
 PIECE = 128
 PIECES = S // PIECE
 LEAD = 3
-FIRST = 512
+FIRST = 384
 SHARE = (3, 4)
 LAST = ROW_TILES - 1
 
@@ -77,7 +77,7 @@ def tile_list_tied_vessel_residual_kernel(tc, tab_words, tab_scales, offs, w, e,
         dec_in = [held(f"dec_in{a}", [P, K_PASS * PACK], BF16) for a in range(PASSES)]
         dec_s = []
         dec_w = [held(f"dec_w{a}", [P, K_PASS], U32) for a in range(PASSES)]
-        h_in = [placed("h_in1", [P, PIECE * PACK], BF16, 28.125) if j == 1 else held(f"h_in{j}", [P, PIECE * PACK], BF16) for j in range(PIECES)]
+        h_in = [held(f"h_in{j}", [P, PIECE * PACK], BF16) for j in range(PIECES)]
         h_w = [held(f"h_w{j}", [P, PIECE], U32) for j in range(PIECES)]
         h_s = [placed("h_s2", [P, PIECE], U8, 36.125) if j == 2 else held(f"h_s{j}", [P, PIECE], U8) for j in range(PIECES)]
         first_d = placed("first_d", [P, 2 * GROUP], F32, 28)[:, 0:1]
@@ -267,9 +267,13 @@ def tile_list_tied_vessel_residual_kernel(tc, tab_words, tab_scales, offs, w, e,
         rows_of = []
 
         def weave(j):
+            h_rows, acts = rows_of[j]
+            for t in range(PACK):
+                own = slice(t * PIECE, (t + 1) * PIECE)
+                nc.scalar.activation(out=h_rows[:, own], in_=acts[:, own], func=ACT.Copy, scale=e_cols[:, t : t + 1])
             nc.scalar.copy(
                 out=h_in[j][:].rearrange("p (c x t) -> p c t x", x=LINE, t=PACK),
-                in_=rows_of[j].rearrange("p (t c x) -> p c t x", t=PACK, x=LINE),
+                in_=h_rows.rearrange("p (t c x) -> p c t x", t=PACK, x=LINE),
             )
 
         def quantize_h(j):
@@ -284,18 +288,15 @@ def tile_list_tied_vessel_residual_kernel(tc, tab_words, tab_scales, offs, w, e,
             elif j == 3:
                 acts = placed("acts3", [P, PACK * PIECE], F32, 32.125)
             else:
-                acts = held(f"acts{j}", [P, PACK * PIECE], F32)
+                acts = held(f"acts{j}", [P, PACK * PIECE], F32, on="acts0" if j == 1 else None)
             if j == 0:
                 h_rows = placed("h_first", [P, PACK * PIECE], BF16, PIECES + 2)[:]
             else:
-                h_rows = placed(f"h_rows{j}", [P, PACK * PIECE], BF16, j)[:]
+                h_rows = placed(f"h_rows{j}", [P, PACK * PIECE], BF16, j if j > 1 else 28.125)[:]
             for t in range(PACK):
                 own = slice(t * PIECE, (t + 1) * PIECE)
                 nc.scalar.activation(out=acts[:, own], in_=sums[t], func=ACT.Gelu_apprx_tanh, scale=e_cols[:, t : t + 1])
-            for t in range(PACK):
-                own = slice(t * PIECE, (t + 1) * PIECE)
-                nc.scalar.activation(out=h_rows[:, own], in_=acts[:, own], func=ACT.Copy, scale=e_cols[:, t : t + 1])
-            rows_of.append(h_rows)
+            rows_of.append((h_rows, acts))
             if j != 1:
                 weave(j)
             if j not in (1, 2):

@@ -22,8 +22,7 @@ PACK = 4
 K_PASS = P * PACK
 PASSES = K // K_PASS
 BANK = 512
-HALVES = S // BANK
-ROW_TILES = K // P
+TILES = K // P
 TILES_A_PASS = K_PASS // P
 GROUP = 16
 QUADS = 4
@@ -34,9 +33,11 @@ LINE = 4
 PIECE = 128
 PIECES = S // PIECE
 LEAD = 3
-FIRST = 384
-SHARE = (3, 4)
-LAST = ROW_TILES - 1
+LAST = TILES - 1
+END = PIECES - 1
+STEP = 4 * PIECE
+SHARE = (3, 2)
+AHEAD = (512, 128, 256)
 
 
 def tile_list_tied_vessel_residual_kernel(tc, tab_words, tab_scales, offs, w, e, w4_words, w4_scales, gT, d, out):
@@ -49,24 +50,23 @@ def tile_list_tied_vessel_residual_kernel(tc, tab_words, tab_scales, offs, w, e,
         def held(name, shape, dtype, on=None):
             return keep.tile(shape, dtype, name=name, tag=on or name, align_bytes=64)
 
-        def placed(name, shape, dtype, half):
-            return lane.tile(shape, dtype, name=name, tag=name, align_bytes=64, offset=int(half * 4 * PIECE))
+        def placed(name, shape, dtype, offset):
+            return lane.tile(shape, dtype, name=name, tag=name, align_bytes=64, offset=offset)
 
-        def bank(name, shape, tag):
-            return psum.tile(shape, F32, name=name, tag=tag, bufs=1)
+        def bank(shape, tag):
+            return psum.tile(shape, F32, name="sums", tag=tag, bufs=1)
 
         offsets = held("offsets", [P, S // GROUP], U16)
         tab_s = held("tab_s", [P, T], U8)
         tab_w = [held(f"tab_w{a}", [P, T], I32) for a in range(PASSES)]
         w_raw = [held(f"w_raw{a}", [P, PACK * H], F32) for a in range(PASSES)]
-        state = [held(f"state{m}", [P, T], F32) for m in range(ROW_TILES)]
-        picks = held("picks", [P, LAST * S], F32)
-        w4_parts = [(0, LEAD), (LEAD, ROW_TILES)]
+        state = [held(f"state{m}", [P, T], F32) for m in range(TILES)]
+        picks = held("picks", [P, TILES * S], F32)
+        w4_parts = [(0, LEAD), (LEAD, TILES)]
         w4_w = [held(f"w4_w{first}", [P, PASSES, 2 * (last - first) * P], U8) for first, last in w4_parts]
         w4_s = [held(f"w4_s{first}", [P, PASSES, (last - first) * P], U8) for first, last in w4_parts]
         e_line = held("e_line", [1, H], F32)
-        e_sorted = held("e_sorted", [P, H], F32)
-        d_rows = held("d_rows", [P, P], F32)
+        vec_rows = held("vec_rows", [P, H], F32)
         ident = held("ident", [P, P], F32)
         v_w = [held(f"v_w{a}", [P, S], U32) for a in range(PASSES)]
         v_rows = held("v_rows", [P, S], U8)
@@ -75,28 +75,27 @@ def tile_list_tied_vessel_residual_kernel(tc, tab_words, tab_scales, offs, w, e,
         enc_s = [held(f"enc_s{a}", [P, H], U8) for a in range(PASSES)]
         enc_w = [held(f"enc_w{a}", [P, H], U32) for a in range(PASSES)]
         dec_in = [held(f"dec_in{a}", [P, K_PASS * PACK], BF16) for a in range(PASSES)]
-        dec_s = []
+        dec_s = [held(f"dec_s{a}", [P, K_PASS], U8) for a in range(PASSES)]
         dec_w = [held(f"dec_w{a}", [P, K_PASS], U32) for a in range(PASSES)]
-        h_in = [held(f"h_in{j}", [P, PIECE * PACK], BF16) for j in range(PIECES)]
-        h_w = [held(f"h_w{j}", [P, PIECE], U32) for j in range(PIECES)]
-        h_s = [placed("h_s2", [P, PIECE], U8, 36.125) if j == 2 else held(f"h_s{j}", [P, PIECE], U8) for j in range(PIECES)]
-        first_d = placed("first_d", [P, 2 * GROUP], F32, 28)[:, 0:1]
-        even_d = held("even_d", [P, 3], F32)
-        tail_d = held("tail_d", [P, 1], F32)
-        zeros = placed("zeros", [P, PIECE], F32, 20.5)
-        no_bias = placed("no_bias", [P, 2 * GROUP], F32, 36)[:, 0:1]
+        h_w = {}
+        h_s = {}
+        minus_d = held("minus_d", [P, TILES], F32)
+        first_d = held("first_d", [P, 1], F32, on="h_in1")
+        first_row = placed("first_row", [P, P], F32, 2 * P)
+        later_rows = placed("later_rows", [P, P], F32, 7 * STEP)
+        second_row = placed("second_row", [P, P], F32, 21 * STEP // 2)
+        minus_rows = held("minus_rows", [P, P], F32)
         e_cols = held("e_cols", [P, PACK], F32)
         warm = held("warm", [P, 1], F32)
 
+        nc.vector.memset(vec_rows[:], 0.0)
+        nc.vector.memset(first_row[:], 0.0)
+        nc.vector.memset(minus_rows[:], 0.0)
         nc.vector.memset(tab_s[QUAD : 2 * QUAD, :].bitcast(I32), 0)
         nc.vector.memset(tab_s[2 * QUAD : P, :].bitcast(I32), 0)
-        nc.vector.memset(d_rows[:], 0.0)
-        nc.vector.memset(zeros[:], 0.0)
-        nc.vector.memset(no_bias, 0.0)
         make_identity(nc, ident[:])
-        nc.gpsimd.memset(e_sorted[:], 0.0)
 
-        nc.scalar.activation(out=warm[:], in_=d_rows[:, P - 1 : P], func=ACT.Gelu_apprx_tanh)
+        nc.scalar.activation(out=warm[:], in_=vec_rows[:, H - 1 : H], func=ACT.Gelu_apprx_tanh)
 
         def listed(window, first, count):
             return window.indirect(offsets[:, first // GROUP : (first + count) // GROUP])
@@ -129,119 +128,112 @@ def tile_list_tied_vessel_residual_kernel(tc, tab_words, tab_scales, offs, w, e,
                     in_=v_rows[row : row + LIVE, :].bitcast(I32),
                 )
 
-        def pick_words(a, first, count):
-            nc.vector.tensor_copy(v_w[a][:, first : first + count], listed(tab_w[a][:].bitcast(U32), first, count))
-
-        def pick_state(target, m, first, count):
-            nc.vector.tensor_copy(target, listed(state[m][:], first, count))
-
         def quantize(codes, scales, grouped):
             nc.vector.quantize_mx(out=codes.bitcast(FP8X4), scales=scales, in_=grouped)
 
-        def cast_w(a):
+        def cast_on_vector(a, first, last):
             nc.vector.tensor_copy(
-                enc_in[a][:].rearrange("p (t g s i) -> p g t s i", t=PACK, s=RUN, i=PACK)[:, :, 0 : SHARE[a]],
-                w_raw[a][:].rearrange("p (i g t s) -> p g t s i", i=PACK, t=PACK, s=RUN)[:, :, 0 : SHARE[a]],
+                enc_in[a][:].rearrange("p (t g s i) -> p g t s i", t=PACK, s=RUN, i=PACK)[:, :, first:last],
+                w_raw[a][:].rearrange("p (i g t s) -> p g t s i", i=PACK, t=PACK, s=RUN)[:, :, first:last],
             )
+
+        def cast_on_scalar(a, t):
             target = enc_in[a][:].rearrange("p (t g z x i) -> p t g z i x", t=PACK, z=RUN // LINE, x=LINE, i=PACK)
             source = w_raw[a][:].rearrange("p (i g t z x) -> p t g z i x", i=PACK, t=PACK, z=RUN // LINE, x=LINE)
-            for t in range(SHARE[a], PACK):
-                nc.scalar.copy(out=target[:, t], in_=source[:, t])
+            nc.scalar.copy(out=target[:, t], in_=source[:, t])
 
-        def turn_w(a, tags):
+        def turn_w(a):
             words = enc_in[a][:].bitcast(F32).rearrange("p (t c u) -> p t c u", t=PACK, u=2)
             target = dec_in[a][:].rearrange("c (p u x t) -> c p u x t", u=2, x=2, t=PACK)
             for u in range(2):
-                turned = bank("turned", [P, PACK, P], tags[u])
+                turned = bank([P, PACK, P], f"x{u}")
                 for t in range(PACK):
                     nc.tensor.transpose(turned[:, t, :], words[:, t, :, u], ident[:])
                 pairs = turned[:].rearrange("c t p -> c (t p)").bitcast(BF16)
                 nc.scalar.copy(out=target[:, :, u, :, :], in_=pairs.rearrange("c (t p x) -> c p x t", t=PACK, x=2))
+            quantize(dec_w[a][:], dec_s[a][:], dec_in[a][:])
 
         nc.sync.dma_start(offsets[:], offs)
         nc.sync.dma_start(out=tab_s[0:QUAD, :].bitcast(I32), in_=tab_scales.rearrange("a j t -> (a j) t").bitcast(I32))
         nc.vector.tensor_copy(v_rows[:], tab_s[:].indirect(offsets[:]))
-        load_w(0)
-        nc.sync.dma_start(out=e_line[:], in_=e.rearrange("(o r) -> o r", o=1))
-        nc.sync.dma_start(out=d_rows[0:ROW_TILES, :], in_=d.rearrange("(m p) -> m p", p=P))
-        load_w(1)
-        move_plane(0)
         load_table(0)
-        move_plane(1)
+        nc.sync.dma_start(out=e_line[:], in_=e.rearrange("(o r) -> o r", o=1))
+        d_rows = d.rearrange("(m p) -> m p", p=P)
+        load_w(0)
         load_table(1)
+        move_plane(0)
+        load_w(1)
+        move_plane(1)
         load_state(0)
+        nc.sync.dma_start(out=first_row[0:2, :], in_=d_rows[0:2])
         load_w4(0)
-        for m in range(1, LEAD + 1):
-            load_state(m)
+        load_state(1)
+        nc.sync.dma_start(out=second_row[0:2, :], in_=d_rows[2:4])
+        load_state(2)
+        nc.sync.dma_start(out=later_rows[QUAD : QUAD + 4, :], in_=d_rows[4:TILES])
+        load_state(3)
         load_w4(1)
-        for m in range(LEAD + 1, ROW_TILES):
+        for m in range(LEAD + 1, TILES):
             load_state(m)
+
+        begins = [m if m < LEAD else PIECES + m - LEAD for m in range(LAST)]
+        beats = [(-back, j) for turn, back, j in sorted((begins[m] + j, -m, j) for m in range(LAST) for j in range(PIECES))]
+        spare = [(1, 0, 1), (2, 0, 1), (0, END, 1)] + [(3, j, 1) for j in range(5)]
+        spare += [(4, 0, 1), (3, 5, 1), (5, 0, 1), (3, 6, 1), (6, 0, 1), (3, 7, 1)] + [(LAST, j, 1) for j in range(6)] + [(LAST, 6, 2)]
+        follower = {}
+        for b, (m, j) in enumerate(beats[:-1]):
+            before = beats[b - 1] if b > 0 else (0, 0)
+            if before == (LAST - 1, END - 2):
+                follower[(m, j)] = (before[0], before[1] + 1, 2)
+            elif before[0] not in (0, LEAD) and before[1] < END and before != (LAST - 1, END - 1):
+                follower[(m, j)] = (before[0], before[1] + 1, 1)
+            else:
+                follower[(m, j)] = spare.pop(0)
+        assert not spare
+
+        nc.scalar.copy(
+            out=vec_rows[0:1, :].rearrange("o (t g s) -> o t g s", t=PACK, s=RUN),
+            in_=e_line[:].rearrange("o (g t s) -> o t g s", t=PACK, s=RUN),
+        )
+        vec_cols = bank([P, PACK, P], "vec")
+        for t in range(PACK):
+            nc.tensor.transpose(vec_cols[:, t, :], vec_rows[:, t * P : (t + 1) * P], ident[:])
+        nc.scalar.copy(out=e_cols[:], in_=vec_cols[:, :, 0])
+        heads = picks[:].rearrange("p (m j x) -> p m j x", m=TILES, x=PIECE)[:, :, :, 0]
 
         def negate(target, source):
             nc.scalar.activation(out=target, in_=source, func=ACT.Copy, scale=-1.0)
 
-        end = PIECES - 1
+        runs = []
+        for host, tile, piece in sorted((m, one[0], one[1]) for (m, j), one in follower.items() if (m, j) != (0, 0)):
+            if runs and runs[-1][:2] == [host, tile] and runs[-1][3] == piece:
+                runs[-1][3] = piece + 1
+            else:
+                runs.append([host, tile, piece, piece + 1])
 
-        def follower(m, j):
-            if m == LEAD - 1:
-                return (LEAD, j - 1, 2 if j == end else 1) if j > 0 else None
-            if m < LEAD:
-                return (m + 1, j, 1)
-            if m == 3:
-                return (4, j, 1) if j < 2 else (5, j - 1, 2 if j == end else 1)
-            if m == 4:
-                if j == 0:
-                    return (5, 0, 1)
-                return (6, j - 1, 3 if j == end - 1 else 1) if j < end else None
-            if m == 5:
-                return (LAST, j, 1)
-            return (4, j + 2, 1) if j + 2 <= end else None
+        def lay_heads(m, column, write):
+            for host, tile, first, last in runs:
+                if host == m:
+                    write(heads[:, tile, first:last], column.to_broadcast([P, last - first]))
 
-        cast_w(0)
+        nc.vector.tensor_copy(v_w[0][:], tab_w[0][:].bitcast(U32).indirect(offsets[:]))
+        cast_on_vector(0, 0, SHARE[0])
+        for t in range(SHARE[0], PACK):
+            cast_on_scalar(0, t)
         quantize(enc_w[0][:], enc_s[0][:], enc_in[0][:])
-        turn_w(0, ["t0", "t1"])
-
-        d_turned = bank("d_turned", [P, P], "y1")
-        nc.tensor.transpose(d_turned[:], d_rows[:], ident[:])
-        nc.scalar.copy(
-            out=e_sorted[0:1, :].rearrange("o (t g s) -> o t g s", t=PACK, s=RUN),
-            in_=e_line[:].rearrange("o (g t s) -> o t g s", t=PACK, s=RUN),
-        )
-        e_turned = bank("e_turned", [P, PACK, P], "y0")
+        nc.vector.tensor_copy(v_w[1][:], tab_w[1][:].bitcast(U32).indirect(offsets[:]))
+        turn_w(0)
         for t in range(PACK):
-            nc.tensor.transpose(e_turned[:, t, :], e_sorted[:, t * P : (t + 1) * P], ident[:])
-        heads = picks[:].rearrange("p (m j x) -> p m j x", m=LAST, x=PIECE)[:, :, :, 0]
-        negate(first_d, d_turned[:, 0:1])
-        for m in range(LAST):
-            served = [follower(m, j) for j in range(PIECES) if follower(m, j) and (m, j) != (0, 0)]
-            for tile in sorted({one[0] for one in served}):
-                own = [one[1] for one in served if one[0] == tile]
-                negate(heads[:, tile - 1, own[0] : own[-1] + 1], d_turned[:, m : m + 1].to_broadcast([P, len(own)]))
-        negate(even_d[:], d_turned[:, 2:ROW_TILES:2])
-        negate(tail_d[:], d_turned[:, LAST:ROW_TILES])
-        lone_d = {m: even_d[:, m // 2 - 1 : m // 2] for m in (2, 4, 6)}
-        nc.scalar.copy(out=e_cols[:], in_=e_turned[:, :, 0])
+            if t < SHARE[1]:
+                cast_on_vector(1, t, t + 1)
+            else:
+                cast_on_scalar(1, t)
+        for t in range(PACK):
+            units = slice(t * P, (t + 1) * P)
+            quantize(enc_w[1][:, units], enc_s[1][:, units], enc_in[1][:, t * K_PASS : (t + 1) * K_PASS])
 
-        cast_w(1)
-        quantize(enc_w[1][:], enc_s[1][:], enc_in[1][:])
-        turn_w(1, ["t0", "t1"])
-        dec_s.append(held("dec_s0", [P, K_PASS], U8))
-        quantize(dec_w[0][:], dec_s[0][:], dec_in[0][:])
-        pick_words(0, 0, 2 * PIECE)
-        pick_words(0, 2 * PIECE, S - 2 * PIECE)
-        pick_words(1, 0, PIECE)
-        pick_words(1, PIECE, PIECE)
-        pick_words(1, 2 * PIECE, S - 2 * PIECE)
-        first_picks = held("first_picks", [P, FIRST], F32)
-        pick_state(first_picks[:], 0, 0, FIRST)
-        steps = [held(f"steps{z}", [P, 2 * S], F32, on=f"w_raw{z}" if z < PASSES else None) for z in range(ROW_TILES // 2)]
-
-        waiting = {}
-
-        sums_of = {}
-
-        def encode(first, count, places, alone):
-            entries = slice(first * PIECE, (first + count) * PIECE)
+        def encode(j, places, alone):
+            entries = slice(j * PIECE, (j + 1) * PIECE)
             for a in range(PASSES):
                 for t in range(PACK):
                     units = slice(t * P, (t + 1) * P)
@@ -251,75 +243,75 @@ def tile_list_tied_vessel_residual_kernel(tc, tab_words, tab_scales, offs, w, e,
                         lhsT_scale=enc_s[a][:, units],
                         rhs=v_w[a][:, entries].bitcast(FP8X4),
                         rhs_scale=v_s[a][:, entries],
-                        start=(a == 0 and t % alone == 0),
-                        stop=(a == PASSES - 1 and t % alone == alone - 1),
+                        start=(a == 0 and (alone or t == 0)),
+                        stop=(a == PASSES - 1 and (alone or t == PACK - 1)),
                     )
-            for j in range(count):
-                sums_of.setdefault(first + j, [place[:, j * PIECE : (j + 1) * PIECE] for place in places])
 
-        def encode_group(first, count, tags):
-            alone = PACK // len(tags)
-            banks = [bank("acc", [P, alone, count * PIECE], tag) for tag in tags]
-            encode(first, count, [banks[t // alone][:, t % alone, :] for t in range(PACK)], alone)
+        def room(j):
+            return (5 * j + 1) * STEP
 
-        groups = {0: (1, ["a0", "a1", "a2", "a3"]), 1: (1, ["t0"]), 2: (1, ["t1"]), 3: (2, ["a0", "a1"]), 5: (2, ["a2", "a3"]), 7: (1, ["a0"])}
+        acts = {}
+        h_rows = {}
+        h_in = {}
+        homes = {}
 
-        rows_of = []
+        def gelu(j):
+            if j == 0:
+                places = [bank([P, PIECE], f"a{t}")[:] for t in range(PACK)]
+            else:
+                shared = bank([P, PACK, PIECE], f"x{j % 2}")
+                places = [shared[:, t, :] for t in range(PACK)]
+            encode(j, places, j == 0)
+            if j < LEAD - 1:
+                acts[j] = held(f"acts{j}", [P, PACK * PIECE], F32)
+            elif j == LEAD - 1:
+                acts[j] = placed(f"acts{j}", [P, PACK * PIECE], F32, 3 * STEP)
+            else:
+                acts[j] = placed(f"acts{j}", [P, PACK * PIECE], F32, room(j - 1) + STEP)
+            for t in range(PACK):
+                nc.scalar.activation(out=acts[j][:, t * PIECE : (t + 1) * PIECE], in_=places[t], func=ACT.Gelu_apprx_tanh, scale=e_cols[:, t : t + 1])
+
+        def scale_h(j):
+            if j < LEAD - 1:
+                h_rows[j] = held(f"h_rows{j}", [P, PACK * PIECE], BF16)
+            else:
+                h_rows[j] = placed(f"h_rows{j}", [P, PACK * PIECE], BF16, room(j))
+            for t in range(PACK):
+                own = slice(t * PIECE, (t + 1) * PIECE)
+                nc.scalar.activation(out=h_rows[j][:, own], in_=acts[j][:, own], func=ACT.Copy, scale=e_cols[:, t : t + 1])
+            if j >= LEAD:
+                homes[(0, j - 1)] = placed(f"step0_{j}", [P, PIECE], F32, room(j - 1) + 2 * STEP)[:]
+            elif j == LEAD - 1:
+                homes[(0, j - 1)] = placed(f"step0_{j}", [P, PIECE], F32, 13 * STEP // 2)[:]
+            elif j > 0:
+                homes[(0, j - 1)] = held(f"step0_{j}", [P, PIECE], F32, on=f"acts{j}")[:]
 
         def weave(j):
-            h_rows, acts = rows_of[j]
-            for t in range(PACK):
-                own = slice(t * PIECE, (t + 1) * PIECE)
-                nc.scalar.activation(out=h_rows[:, own], in_=acts[:, own], func=ACT.Copy, scale=e_cols[:, t : t + 1])
+            if j == LEAD - 1:
+                h_in[j] = placed(f"h_in{j}", [P, PIECE * PACK], BF16, 15 * STEP // 2)
+            else:
+                h_in[j] = held(f"h_in{j}", [P, PIECE * PACK], BF16)
             nc.scalar.copy(
                 out=h_in[j][:].rearrange("p (c x t) -> p c t x", x=LINE, t=PACK),
-                in_=h_rows.rearrange("p (t c x) -> p c t x", t=PACK, x=LINE),
+                in_=h_rows[j][:].rearrange("p (t c x) -> p c t x", t=PACK, x=LINE),
             )
-
-        def quantize_h(j):
+            if j >= LEAD - 1:
+                homes[(LEAD - 1, j - 2)] = placed(f"step2_{j}", [P, PIECE], F32, room(j))[:]
+                if j == END:
+                    homes[(1, j - 1)] = placed(f"step1_{j}", [P, PIECE], F32, room(j) + STEP)[:]
+            h_w[j] = held(f"h_w{j}", [P, PIECE], U32)
+            if j == 1:
+                h_s[j] = placed(f"h_s{j}", [P, PIECE], U8, 43 * STEP // 4)
+            else:
+                h_s[j] = held(f"h_s{j}", [P, PIECE], U8)
             quantize(h_w[j][:], h_s[j][:], h_in[j][:])
 
-        def make_h(j):
-            if j in groups:
-                encode_group(j, *groups[j])
-            sums = sums_of[j]
-            if j == 2:
-                acts = placed("acts2", [P, PACK * PIECE], F32, 24.125)
-            elif j == 3:
-                acts = placed("acts3", [P, PACK * PIECE], F32, 32.125)
-            else:
-                acts = held(f"acts{j}", [P, PACK * PIECE], F32, on="acts0" if j == 1 else None)
-            if j == 0:
-                h_rows = placed("h_first", [P, PACK * PIECE], BF16, PIECES + 2)[:]
-            else:
-                h_rows = placed(f"h_rows{j}", [P, PACK * PIECE], BF16, j if j > 1 else 28.125)[:]
-            for t in range(PACK):
-                own = slice(t * PIECE, (t + 1) * PIECE)
-                nc.scalar.activation(out=acts[:, own], in_=sums[t], func=ACT.Gelu_apprx_tanh, scale=e_cols[:, t : t + 1])
-            rows_of.append((h_rows, acts))
-            if j != 1:
-                weave(j)
-            if j not in (1, 2):
-                quantize_h(j)
-            if j > 1:
-                home = placed(f"first_step{j}", [P, PIECE], F32, j) if j > 2 else placed("second_step", [P, PIECE], F32, 20)
-                waiting.setdefault((0, j - 1), home[:])
-            if j > 2:
-                waiting.setdefault((LEAD - 1, j - 3), acts[:, 0:PIECE])
-            if j == end:
-                waiting.setdefault((LEAD - 1, j - 2), placed("third_step", [P, PIECE], F32, j + 1)[:])
-
-        y_tags = ["y0", "y1"]
-        y_first = ["a0", "a1", "a2", "a3", "a2"]
-        made = []
-
-        def decode(m, first, count):
+        def decode(m, first, count, tag):
             half, place = divmod(m, TILES_A_PASS)
             own = slice(place * P, (place + 1) * P)
             part = 0 if m < LEAD else 1
             col = (m - w4_parts[part][0]) * P
-            y = bank("y", [P, count], y_first[len(made)] if len(made) < len(y_first) else y_tags[len(made) % len(y_tags)])
-            made.append(y)
+            y = bank([P, count], tag)
             entries = slice(first, first + count)
             for a in range(PASSES):
                 nc.tensor.matmul_mx(
@@ -344,64 +336,92 @@ def tile_list_tied_vessel_residual_kernel(tc, tab_words, tab_scales, offs, w, e,
                 )
             return y
 
-        def step_of(m, first, count):
-            if (m, first // PIECE) in waiting:
-                return waiting[(m, first // PIECE)]
-            at = (m % 2) * S + first
-            return steps[m // 2][:, at : at + count]
+        steps = [held(f"steps{z}", [P, 2 * S], F32, on={0: "w_raw0", 3: "w_raw1"}.get(z)) for z in range(TILES // 2)]
+        late = sum(AHEAD[:2])
 
         def picked(m, first, count):
-            if m > 0:
-                return picks[:, (m - 1) * S + first : (m - 1) * S + first + count]
-            if first < FIRST:
-                return first_picks[:, first : first + count]
-            return rest_picks[:, first - FIRST : first - FIRST + count]
+            if m == 0 and late <= first < sum(AHEAD):
+                return late_picks[:, first - late : first - late + count]
+            if m == 0 and AHEAD[0] <= first < late:
+                return mid_picks[:, first - AHEAD[0] : first - AHEAD[0] + count]
+            return picks[:, m * S + first : m * S + first + count]
+
+        def step_of(m, first, count):
+            at = (m % 2) * S + first
+            return homes.get((m, first // PIECE), steps[m // 2][:, at : at + count])
+
+        def gather(m, first, count):
+            nc.vector.tensor_copy(picked(m, first, count), listed(state[m][:], first, count))
 
         def scatter(m, first, count):
             nc.vector.tensor_tensor(listed(state[m][:], first, count), picked(m, first, count), step_of(m, first, count), ADD)
             if first + count == S:
                 nc.sync.dma_start(out=out[m * P : (m + 1) * P, :], in_=state[m][:])
 
+        turns = []
+
         def beat(m, j):
-            behind = follower(m, j)
-            if behind:
-                behind = (behind[0], behind[1] * PIECE, behind[2] * PIECE)
-            scale = picked(behind[0], behind[1], 1) if behind else lone_d[m]
+            behind = follower.get((m, j))
             if (m, j) == (0, 0):
-                scale = first_d
-            y = decode(m, j * PIECE, PIECE)
-            if (m, j) == (0, 1):
-                nc.scalar.activation(out=step_of(m, j * PIECE, PIECE), in_=y[:], func=ACT.Identity, scale=scale, bias=no_bias)
+                scale, tag = first_d[:], "x1"
             else:
-                nc.scalar.activation(out=step_of(m, j * PIECE, PIECE), in_=y[:], func=ACT.Copy, scale=scale)
+                scale = heads[:, behind[0], behind[1] : behind[1] + 1] if behind else minus_d[:, m : m + 1]
+                if m == 1 and j + 2 <= END:
+                    tag = f"x{j % 2}"
+                else:
+                    tag = f"a{len(turns) % 2}"
+                    turns.append((m, j))
+            y = decode(m, j * PIECE, PIECE, tag)
+            nc.scalar.activation(out=step_of(m, j * PIECE, PIECE), in_=y[:], func=ACT.Copy, scale=scale)
             scatter(m, j * PIECE, PIECE)
+            if behind:
+                gather(behind[0], behind[1] * PIECE, behind[2] * PIECE)
+
+        gelu(0)
+        scale_h(0)
+        gather(0, 0, AHEAD[0])
+        first_col = bank([P, P], "vec")
+        nc.tensor.transpose(first_col[:], first_row[:], ident[:])
+        negate(first_d[:], first_col[:, 0:1])
+        for m in range(2):
+            lay_heads(m, first_col[:, m : m + 1], negate)
+        h_in[0] = placed("h_in0", [P, PIECE * PACK], BF16, 4 * P)
+        mid_picks = placed("mid_picks", [P, AHEAD[1]], F32, 0)
+        nc.vector.tensor_copy(
+            h_in[0][:].rearrange("p (c t) -> p c t", t=PACK), h_rows[0][:].rearrange("p (t c) -> p c t", t=PACK)
+        )
+        gather(0, AHEAD[0], AHEAD[1])
+        h_w[0] = held("h_w0", [P, PIECE], U32)
+        h_s[0] = held("h_s0", [P, PIECE], U8)
+        quantize(h_w[0][:], h_s[0][:], h_in[0][:])
+        late_picks = held("late_picks", [P, AHEAD[2]], F32, on="h_rows0")
+        gather(0, late, AHEAD[2])
+        gelu(1)
+        scale_h(1)
+        for m, j in beats:
             if (m, j) == (1, 0):
-                nc.vector.tensor_tensor(picked(*behind), listed(state[2][:], 0, PIECE), zeros[:], ADD)
-                dec_s.append(placed("dec_s1", [P, K_PASS], U8, 21))
-                quantize(dec_w[1][:], dec_s[1][:], dec_in[1][:])
-            elif behind:
-                pick_state(picked(*behind), *behind)
-
-        make_h(0)
-        rest_picks = placed("rest_picks", [P, S - FIRST], F32, PIECES + 2)
-        pick_state(rest_picks[:], 0, FIRST, S - FIRST)
-
-        begins = [m if m < LEAD else PIECES + m - LEAD for m in range(LAST)]
-        order = sorted((begins[m] + j, -m, j) for m in range(LAST) for j in range(PIECES))
-        for turn, back, j in order:
-            if (back, j) == (0, 0):
-                make_h(1)
-            if (back, j) == (0, 1):
-                make_h(2)
-            beat(-back, j)
-            if (back, j) == (0, 0):
+                negate(minus_rows[0:2, :], second_row[0:2, :])
                 weave(1)
-                quantize_h(1)
-            if (back, j) == (0, 1):
-                quantize_h(2)
-            if back == 0 and 0 < j < end - 1:
-                make_h(j + 2)
-        for first in range(0, S, BANK):
-            y = decode(LAST, first, BANK)
-            nc.scalar.activation(out=step_of(LAST, first, BANK), in_=y[:], func=ACT.Copy, scale=tail_d[:])
+                homes[(1, 0)] = placed("step1_0", [P, PIECE], F32, 39 * STEP // 4)[:]
+            if m == 1 and j + 2 <= END:
+                gelu(j + 2)
+            if (m == 1 and 0 < j <= END - 2) or (m, j) == (0, 1):
+                scale_h(j + 2 if m == 1 else 2)
+            if (m == 0 and 1 < j < END) or (m, j) == (2, 0):
+                weave(j + 1 if m == 0 else 2)
+            if (m, j) == (LEAD, 0):
+                turn_w(1)
+            if (m, j) == (0, 1):
+                negate(minus_rows[QUAD : QUAD + 4, :], later_rows[QUAD : QUAD + 4, :])
+            if (m, j) == (2, 0):
+                later_cols = bank([P, P], "vec")
+                nc.tensor.transpose(later_cols[:], minus_rows[:], ident[:])
+                nc.scalar.copy(out=minus_d[:, 2:4], in_=later_cols[:, 0:2])
+                nc.scalar.copy(out=minus_d[:, 4:TILES], in_=later_cols[:, QUAD : QUAD + 4])
+            if m >= 2 and j == 0:
+                lay_heads(m, minus_d[:, m : m + 1], nc.scalar.copy)
+            beat(m, j)
+        for half in range(S // BANK):
+            y = decode(LAST, half * BANK, BANK, f"a{half}")
+            nc.scalar.activation(out=step_of(LAST, half * BANK, BANK), in_=y[:], func=ACT.Copy, scale=minus_d[:, LAST:TILES])
         scatter(LAST, 0, S)

@@ -82,7 +82,7 @@ def tile_list_tied_vessel_residual_kernel(tc, tab_words, tab_scales, offs, w, e,
         minus_d = held("minus_d", [P, TILES], F32)
         first_d = held("first_d", [P, 1], F32, on="h_in1")
         first_row = placed("first_row", [P, P], F32, 2 * P)
-        later_rows = placed("later_rows", [P, P], F32, 7 * STEP)
+        later_rows = placed("later_rows", [P, P], F32, 63 * STEP // 4)
         second_row = placed("second_row", [P, P], F32, 21 * STEP // 2)
         minus_rows = held("minus_rows", [P, P], F32)
         e_cols = held("e_cols", [P, PACK], F32)
@@ -176,16 +176,17 @@ def tile_list_tied_vessel_residual_kernel(tc, tab_words, tab_scales, offs, w, e,
         for m in range(LEAD + 1, TILES):
             load_state(m)
 
-        begins = [m if m < LEAD else PIECES + m - LEAD for m in range(LAST)]
-        beats = [(-back, j) for turn, back, j in sorted((begins[m] + j, -m, j) for m in range(LAST) for j in range(PIECES))]
-        spare = [(1, 0, 1), (2, 0, 1), (0, END, 1)] + [(3, j, 1) for j in range(5)]
-        spare += [(4, 0, 1), (3, 5, 1), (5, 0, 1), (3, 6, 1), (6, 0, 1), (3, 7, 1)] + [(LAST, j, 1) for j in range(6)] + [(LAST, 6, 2)]
+        first_wave = [(m, j - m // 2) for j in range(PIECES) for m in range(LEAD) if j >= m // 2]
+        later = sorted((m + j, -m, j) for m, j in [(LEAD - 1, 2)] + [(m, j) for m in range(LEAD, LAST) for j in range(PIECES)])
+        beats = first_wave + [(-back, END if -back < LEAD else j) for turn, back, j in later]
+        spare = [(1, 0, 2), None, (2, 0, 1), (0, END, 1)] + [(3, j, 1) for j in range(6)]
+        spare += [(4, 0, 1), (5, 0, 1), (3, 6, 1), (6, 0, 1), (3, 7, 1)] + [(LAST, j, 1) for j in range(6)] + [(LAST, 6, 2)]
         follower = {}
         for b, (m, j) in enumerate(beats[:-1]):
             before = beats[b - 1] if b > 0 else (0, 0)
             if before == (LAST - 1, END - 2):
                 follower[(m, j)] = (before[0], before[1] + 1, 2)
-            elif before[0] not in (0, LEAD) and before[1] < END and before != (LAST - 1, END - 1):
+            elif before[0] not in (0, LEAD) and before[1] < END and before not in ((1, 0), (LAST - 1, END - 1)):
                 follower[(m, j)] = (before[0], before[1] + 1, 1)
             else:
                 follower[(m, j)] = spare.pop(0)
@@ -205,7 +206,7 @@ def tile_list_tied_vessel_residual_kernel(tc, tab_words, tab_scales, offs, w, e,
             nc.scalar.activation(out=target, in_=source, func=ACT.Copy, scale=-1.0)
 
         runs = []
-        for host, tile, piece in sorted((m, one[0], one[1]) for (m, j), one in follower.items() if (m, j) != (0, 0)):
+        for host, tile, piece in sorted((m, one[0], one[1]) for (m, j), one in follower.items() if one and (m, j) != (0, 0)):
             if runs and runs[-1][:2] == [host, tile] and runs[-1][3] == piece:
                 runs[-1][3] = piece + 1
             else:
@@ -248,7 +249,7 @@ def tile_list_tied_vessel_residual_kernel(tc, tab_words, tab_scales, offs, w, e,
                     )
 
         def room(j):
-            return (5 * j + 1) * STEP
+            return (5 * j + 1 + 2 * (j >= LEAD)) * STEP
 
         acts = {}
         h_rows = {}
@@ -262,10 +263,8 @@ def tile_list_tied_vessel_residual_kernel(tc, tab_words, tab_scales, offs, w, e,
                 shared = bank([P, PACK, PIECE], f"x{j % 2}")
                 places = [shared[:, t, :] for t in range(PACK)]
             encode(j, places, j == 0)
-            if j < LEAD - 1:
+            if j < LEAD:
                 acts[j] = held(f"acts{j}", [P, PACK * PIECE], F32)
-            elif j == LEAD - 1:
-                acts[j] = placed(f"acts{j}", [P, PACK * PIECE], F32, 3 * STEP)
             else:
                 acts[j] = placed(f"acts{j}", [P, PACK * PIECE], F32, room(j - 1) + STEP)
             for t in range(PACK):
@@ -280,17 +279,10 @@ def tile_list_tied_vessel_residual_kernel(tc, tab_words, tab_scales, offs, w, e,
                 own = slice(t * PIECE, (t + 1) * PIECE)
                 nc.scalar.activation(out=h_rows[j][:, own], in_=acts[j][:, own], func=ACT.Copy, scale=e_cols[:, t : t + 1])
             if j >= LEAD:
-                homes[(0, j - 1)] = placed(f"step0_{j}", [P, PIECE], F32, room(j - 1) + 2 * STEP)[:]
-            elif j == LEAD - 1:
-                homes[(0, j - 1)] = placed(f"step0_{j}", [P, PIECE], F32, 13 * STEP // 2)[:]
-            elif j > 0:
-                homes[(0, j - 1)] = held(f"step0_{j}", [P, PIECE], F32, on=f"acts{j}")[:]
+                homes[(1, j - 1)] = placed(f"step1_{j}", [P, PIECE], F32, room(j - 1) + 2 * STEP)[:]
 
         def weave(j):
-            if j == LEAD - 1:
-                h_in[j] = placed(f"h_in{j}", [P, PIECE * PACK], BF16, 15 * STEP // 2)
-            else:
-                h_in[j] = held(f"h_in{j}", [P, PIECE * PACK], BF16)
+            h_in[j] = held(f"h_in{j}", [P, PIECE * PACK], BF16)
             nc.scalar.copy(
                 out=h_in[j][:].rearrange("p (c x t) -> p c t x", x=LINE, t=PACK),
                 in_=h_rows[j][:].rearrange("p (t c x) -> p c t x", t=PACK, x=LINE),
@@ -298,10 +290,12 @@ def tile_list_tied_vessel_residual_kernel(tc, tab_words, tab_scales, offs, w, e,
             if j >= LEAD - 1:
                 homes[(LEAD - 1, j - 2)] = placed(f"step2_{j}", [P, PIECE], F32, room(j))[:]
                 if j == END:
-                    homes[(1, j - 1)] = placed(f"step1_{j}", [P, PIECE], F32, room(j) + STEP)[:]
+                    homes[(0, j)] = placed(f"step0_{j}", [P, PIECE], F32, room(j) + STEP)[:]
             h_w[j] = held(f"h_w{j}", [P, PIECE], U32)
             if j == 1:
                 h_s[j] = placed(f"h_s{j}", [P, PIECE], U8, 43 * STEP // 4)
+            elif j == 2:
+                h_s[j] = placed(f"h_s{j}", [P, PIECE], U8, 16 * STEP)
             else:
                 h_s[j] = held(f"h_s{j}", [P, PIECE], U8)
             quantize(h_w[j][:], h_s[j][:], h_in[j][:])
@@ -366,8 +360,8 @@ def tile_list_tied_vessel_residual_kernel(tc, tab_words, tab_scales, offs, w, e,
                 scale, tag = first_d[:], "x1"
             else:
                 scale = heads[:, behind[0], behind[1] : behind[1] + 1] if behind else minus_d[:, m : m + 1]
-                if m == 1 and j + 2 <= END:
-                    tag = f"x{j % 2}"
+                if m == 0 and j < END:
+                    tag = f"x{(j + 1) % 2}"
                 else:
                     tag = f"a{len(turns) % 2}"
                     turns.append((m, j))
@@ -383,6 +377,7 @@ def tile_list_tied_vessel_residual_kernel(tc, tab_words, tab_scales, offs, w, e,
         first_col = bank([P, P], "vec")
         nc.tensor.transpose(first_col[:], first_row[:], ident[:])
         negate(first_d[:], first_col[:, 0:1])
+        negate(minus_d[:, 1:2], first_col[:, 1:2])
         for m in range(2):
             lay_heads(m, first_col[:, m : m + 1], negate)
         h_in[0] = placed("h_in0", [P, PIECE * PACK], BF16, 4 * P)
@@ -396,23 +391,20 @@ def tile_list_tied_vessel_residual_kernel(tc, tab_words, tab_scales, offs, w, e,
         quantize(h_w[0][:], h_s[0][:], h_in[0][:])
         late_picks = held("late_picks", [P, AHEAD[2]], F32, on="h_rows0")
         gather(0, late, AHEAD[2])
-        gelu(1)
-        scale_h(1)
         for m, j in beats:
+            if m == 0 and j < END:
+                gelu(j + 1)
+                scale_h(j + 1)
             if (m, j) == (1, 0):
                 negate(minus_rows[0:2, :], second_row[0:2, :])
-                weave(1)
                 homes[(1, 0)] = placed("step1_0", [P, PIECE], F32, 39 * STEP // 4)[:]
-            if m == 1 and j + 2 <= END:
-                gelu(j + 2)
-            if (m == 1 and 0 < j <= END - 2) or (m, j) == (0, 1):
-                scale_h(j + 2 if m == 1 else 2)
-            if (m == 0 and 1 < j < END) or (m, j) == (2, 0):
-                weave(j + 1 if m == 0 else 2)
+            if (m, j) == (1, 1):
+                negate(minus_rows[QUAD : QUAD + 4, :], later_rows[QUAD : QUAD + 4, :])
+                homes[(1, 1)] = placed("step1_1", [P, PIECE], F32, 65 * STEP // 4)[:]
+            if m == 1 and j < END:
+                weave(j + 1)
             if (m, j) == (LEAD, 0):
                 turn_w(1)
-            if (m, j) == (0, 1):
-                negate(minus_rows[QUAD : QUAD + 4, :], later_rows[QUAD : QUAD + 4, :])
             if (m, j) == (2, 0):
                 later_cols = bank([P, P], "vec")
                 nc.tensor.transpose(later_cols[:], minus_rows[:], ident[:])

@@ -37,7 +37,7 @@ LAST = TILES - 1
 END = PIECES - 1
 STEP = 4 * PIECE
 SHARE = (3, 2)
-AHEAD = (512, 128, 256)
+AHEAD = (384, 128, 384)
 
 
 def tile_list_tied_vessel_residual_kernel(tc, tab_words, tab_scales, offs, w, e, w4_words, w4_scales, gT, d, out):
@@ -75,7 +75,7 @@ def tile_list_tied_vessel_residual_kernel(tc, tab_words, tab_scales, offs, w, e,
         enc_s = [held(f"enc_s{a}", [P, H], U8) for a in range(PASSES)]
         enc_w = [held(f"enc_w{a}", [P, H], U32) for a in range(PASSES)]
         dec_in = [held(f"dec_in{a}", [P, K_PASS * PACK], BF16) for a in range(PASSES)]
-        dec_s = [held(f"dec_s{a}", [P, K_PASS], U8) for a in range(PASSES)]
+        dec_s = {}
         dec_w = [held(f"dec_w{a}", [P, K_PASS], U32) for a in range(PASSES)]
         h_w = {}
         h_s = {}
@@ -151,6 +151,9 @@ def tile_list_tied_vessel_residual_kernel(tc, tab_words, tab_scales, offs, w, e,
                     nc.tensor.transpose(turned[:, t, :], words[:, t, :, u], ident[:])
                 pairs = turned[:].rearrange("c t p -> c (t p)").bitcast(BF16)
                 nc.scalar.copy(out=target[:, :, u, :, :], in_=pairs.rearrange("c (t p x) -> c p x t", t=PACK, x=2))
+
+        def quantize_turned(a):
+            dec_s[a] = held(f"dec_s{a}", [P, K_PASS], U8, on="w_raw1" if a == 0 else None)
             quantize(dec_w[a][:], dec_s[a][:], dec_in[a][:])
 
         nc.sync.dma_start(offsets[:], offs)
@@ -159,18 +162,19 @@ def tile_list_tied_vessel_residual_kernel(tc, tab_words, tab_scales, offs, w, e,
         load_table(0)
         nc.sync.dma_start(out=e_line[:], in_=e.rearrange("(o r) -> o r", o=1))
         d_rows = d.rearrange("(m p) -> m p", p=P)
+        nc.sync.dma_start(out=vec_rows[1:3, 0:P], in_=d_rows[0:2])
         load_w(0)
         load_table(1)
         move_plane(0)
         load_w(1)
         move_plane(1)
         load_state(0)
-        nc.sync.dma_start(out=first_row[0:2, :], in_=d_rows[0:2])
+        nc.sync.dma_start(out=first_row[0:2, :], in_=d_rows[2:4])
         load_w4(0)
         load_state(1)
-        nc.sync.dma_start(out=second_row[0:2, :], in_=d_rows[2:4])
+        nc.sync.dma_start(out=second_row[0:2, :], in_=d_rows[4:6])
         load_state(2)
-        nc.sync.dma_start(out=later_rows[QUAD : QUAD + 4, :], in_=d_rows[4:TILES])
+        nc.sync.dma_start(out=later_rows[QUAD : QUAD + 2, :], in_=d_rows[6:TILES])
         load_state(3)
         load_w4(1)
         for m in range(LEAD + 1, TILES):
@@ -217,6 +221,11 @@ def tile_list_tied_vessel_residual_kernel(tc, tab_words, tab_scales, offs, w, e,
                 if host == m:
                     write(heads[:, tile, first:last], column.to_broadcast([P, last - first]))
 
+        negate(first_d[:], vec_cols[:, 0, 1:2])
+        negate(minus_d[:, 0:2], vec_cols[:, 0, 1:3])
+        for m in range(2):
+            lay_heads(m, vec_cols[:, 0, 1 + m : 2 + m], negate)
+
         nc.vector.tensor_copy(v_w[0][:], tab_w[0][:].bitcast(U32).indirect(offsets[:]))
         cast_on_vector(0, 0, SHARE[0])
         for t in range(SHARE[0], PACK):
@@ -232,6 +241,7 @@ def tile_list_tied_vessel_residual_kernel(tc, tab_words, tab_scales, offs, w, e,
         for t in range(PACK):
             units = slice(t * P, (t + 1) * P)
             quantize(enc_w[1][:, units], enc_s[1][:, units], enc_in[1][:, t * K_PASS : (t + 1) * K_PASS])
+        quantize_turned(0)
 
         def encode(j, places, alone):
             entries = slice(j * PIECE, (j + 1) * PIECE)
@@ -330,7 +340,7 @@ def tile_list_tied_vessel_residual_kernel(tc, tab_words, tab_scales, offs, w, e,
                 )
             return y
 
-        steps = [held(f"steps{z}", [P, 2 * S], F32, on={0: "w_raw0", 3: "w_raw1"}.get(z)) for z in range(TILES // 2)]
+        steps = [held(f"steps{z}", [P, 2 * S], F32, on={0: "w_raw0", 3: "tab_w0"}.get(z)) for z in range(TILES // 2)]
         late = sum(AHEAD[:2])
 
         def picked(m, first, count):
@@ -362,6 +372,8 @@ def tile_list_tied_vessel_residual_kernel(tc, tab_words, tab_scales, offs, w, e,
                 scale = heads[:, behind[0], behind[1] : behind[1] + 1] if behind else minus_d[:, m : m + 1]
                 if m == 0 and j < END:
                     tag = f"x{(j + 1) % 2}"
+                elif (m, j) == (2, 0):
+                    tag = f"a{(len(turns) - 1) % 2}"
                 else:
                     tag = f"a{len(turns) % 2}"
                     turns.append((m, j))
@@ -376,10 +388,6 @@ def tile_list_tied_vessel_residual_kernel(tc, tab_words, tab_scales, offs, w, e,
         gather(0, 0, AHEAD[0])
         first_col = bank([P, P], "vec")
         nc.tensor.transpose(first_col[:], first_row[:], ident[:])
-        negate(first_d[:], first_col[:, 0:1])
-        negate(minus_d[:, 1:2], first_col[:, 1:2])
-        for m in range(2):
-            lay_heads(m, first_col[:, m : m + 1], negate)
         h_in[0] = placed("h_in0", [P, PIECE * PACK], BF16, 4 * P)
         mid_picks = placed("mid_picks", [P, AHEAD[1]], F32, 0)
         nc.vector.tensor_copy(
@@ -399,17 +407,19 @@ def tile_list_tied_vessel_residual_kernel(tc, tab_words, tab_scales, offs, w, e,
                 negate(minus_rows[0:2, :], second_row[0:2, :])
                 homes[(1, 0)] = placed("step1_0", [P, PIECE], F32, 39 * STEP // 4)[:]
             if (m, j) == (1, 1):
-                negate(minus_rows[QUAD : QUAD + 4, :], later_rows[QUAD : QUAD + 4, :])
+                negate(minus_rows[QUAD : QUAD + 2, :], later_rows[QUAD : QUAD + 2, :])
                 homes[(1, 1)] = placed("step1_1", [P, PIECE], F32, 65 * STEP // 4)[:]
             if m == 1 and j < END:
                 weave(j + 1)
+            if (m, j) == (2, 0):
+                negate(minus_d[:, 2:4], first_col[:, 0:2])
             if (m, j) == (LEAD, 0):
                 turn_w(1)
-            if (m, j) == (2, 0):
+                quantize_turned(1)
                 later_cols = bank([P, P], "vec")
                 nc.tensor.transpose(later_cols[:], minus_rows[:], ident[:])
-                nc.scalar.copy(out=minus_d[:, 2:4], in_=later_cols[:, 0:2])
-                nc.scalar.copy(out=minus_d[:, 4:TILES], in_=later_cols[:, QUAD : QUAD + 4])
+                nc.scalar.copy(out=minus_d[:, 4:6], in_=later_cols[:, 0:2])
+                nc.scalar.copy(out=minus_d[:, 6:TILES], in_=later_cols[:, QUAD : QUAD + 2])
             if m >= 2 and j == 0:
                 lay_heads(m, minus_d[:, m : m + 1], nc.scalar.copy)
             beat(m, j)

@@ -36,6 +36,7 @@ LEAD = 3
 LAST = TILES - 1
 END = PIECES - 1
 STEP = 4 * PIECE
+EARLY = 3 * PIECE
 SHARE = (3, 2)
 AHEAD = (384, 128, 384)
 
@@ -69,19 +70,18 @@ def tile_list_tied_vessel_residual_kernel(tc, tab_words, tab_scales, offs, w, e,
         vec_rows = held("vec_rows", [P, H], F32)
         ident = held("ident", [P, P], F32)
         v_w = [held(f"v_w{a}", [P, S], U32) for a in range(PASSES)]
-        v_rows = held("v_rows", [P, S], U8)
+        v_rows = placed("v_rows", [P, S], U8, STEP // 2)
         v_s = [held(f"v_s{a}", [P, S], U8) for a in range(PASSES)]
         enc_in = [held(f"enc_in{a}", [P, H * PACK], BF16) for a in range(PASSES)]
         enc_s = [held(f"enc_s{a}", [P, H], U8) for a in range(PASSES)]
         enc_w = [held(f"enc_w{a}", [P, H], U32) for a in range(PASSES)]
-        dec_in = [held(f"dec_in{a}", [P, K_PASS * PACK], BF16) for a in range(PASSES)]
+        dec_in = {}
         dec_s = {}
         dec_w = [held(f"dec_w{a}", [P, K_PASS], U32) for a in range(PASSES)]
         h_w = {}
         h_s = {}
         minus_d = held("minus_d", [P, TILES], F32)
         first_d = held("first_d", [P, 1], F32, on="h_in1")
-        first_row = placed("first_row", [P, P], F32, 2 * P)
         later_rows = placed("later_rows", [P, P], F32, 63 * STEP // 4)
         second_row = placed("second_row", [P, P], F32, 21 * STEP // 2)
         minus_rows = held("minus_rows", [P, P], F32)
@@ -89,7 +89,6 @@ def tile_list_tied_vessel_residual_kernel(tc, tab_words, tab_scales, offs, w, e,
         warm = held("warm", [P, 1], F32)
 
         nc.vector.memset(vec_rows[:], 0.0)
-        nc.vector.memset(first_row[:], 0.0)
         nc.vector.memset(minus_rows[:], 0.0)
         nc.vector.memset(tab_s[QUAD : 2 * QUAD, :].bitcast(I32), 0)
         nc.vector.memset(tab_s[2 * QUAD : P, :].bitcast(I32), 0)
@@ -120,13 +119,16 @@ def tile_list_tied_vessel_residual_kernel(tc, tab_words, tab_scales, offs, w, e,
             rows = w4_words.rearrange("a p c -> p a c")
             nc.sync.dma_start(out=w4_w[part][:].bitcast(I32), in_=rows[:, :, 2 * first * P : 2 * last * P].bitcast(I32))
 
+        def move_rows(a, q, first, last):
+            row = LIVE * (QUADS * a + q)
+            nc.sync.dma_start(
+                out=v_s[a][QUAD * q : QUAD * q + LIVE, first:last].bitcast(I32),
+                in_=v_rows[row : row + LIVE, first:last].bitcast(I32),
+            )
+
         def move_plane(a):
             for q in range(QUADS):
-                row = LIVE * (QUADS * a + q)
-                nc.sync.dma_start(
-                    out=v_s[a][QUAD * q : QUAD * q + LIVE, :].bitcast(I32),
-                    in_=v_rows[row : row + LIVE, :].bitcast(I32),
-                )
+                move_rows(a, q, 0, EARLY if (a, q) == (1, QUADS - 1) else S)
 
         def quantize(codes, scales, grouped):
             nc.vector.quantize_mx(out=codes.bitcast(FP8X4), scales=scales, in_=grouped)
@@ -142,7 +144,14 @@ def tile_list_tied_vessel_residual_kernel(tc, tab_words, tab_scales, offs, w, e,
             source = w_raw[a][:].rearrange("p (i g t z x) -> p t g z i x", i=PACK, t=PACK, z=RUN // LINE, x=LINE)
             nc.scalar.copy(out=target[:, t], in_=source[:, t])
 
+        def room(j):
+            return (5 * j + 1 + 2 * (j >= LEAD)) * STEP
+
         def turn_w(a):
+            if a == 0:
+                dec_in[a] = held(f"dec_in{a}", [P, K_PASS * PACK], BF16)
+            else:
+                dec_in[a] = placed(f"dec_in{a}", [P, K_PASS * PACK], BF16, room(END) + 3 * STEP // 2)
             words = enc_in[a][:].bitcast(F32).rearrange("p (t c u) -> p t c u", t=PACK, u=2)
             target = dec_in[a][:].rearrange("c (p u x t) -> c p u x t", u=2, x=2, t=PACK)
             for u in range(2):
@@ -162,14 +171,14 @@ def tile_list_tied_vessel_residual_kernel(tc, tab_words, tab_scales, offs, w, e,
         load_table(0)
         nc.sync.dma_start(out=e_line[:], in_=e.rearrange("(o r) -> o r", o=1))
         d_rows = d.rearrange("(m p) -> m p", p=P)
-        nc.sync.dma_start(out=vec_rows[1:3, 0:P], in_=d_rows[0:2])
+        nc.sync.dma_start(out=vec_rows[1:5, 0:P], in_=d_rows[0:4])
         load_w(0)
         load_table(1)
         move_plane(0)
         load_w(1)
         move_plane(1)
         load_state(0)
-        nc.sync.dma_start(out=first_row[0:2, :], in_=d_rows[2:4])
+        move_rows(1, QUADS - 1, EARLY, S)
         load_w4(0)
         load_state(1)
         nc.sync.dma_start(out=second_row[0:2, :], in_=d_rows[4:6])
@@ -222,8 +231,8 @@ def tile_list_tied_vessel_residual_kernel(tc, tab_words, tab_scales, offs, w, e,
                     write(heads[:, tile, first:last], column.to_broadcast([P, last - first]))
 
         negate(first_d[:], vec_cols[:, 0, 1:2])
-        negate(minus_d[:, 0:2], vec_cols[:, 0, 1:3])
-        for m in range(2):
+        negate(minus_d[:, 0:4], vec_cols[:, 0, 1:5])
+        for m in range(4):
             lay_heads(m, vec_cols[:, 0, 1 + m : 2 + m], negate)
 
         nc.vector.tensor_copy(v_w[0][:], tab_w[0][:].bitcast(U32).indirect(offsets[:]))
@@ -257,9 +266,6 @@ def tile_list_tied_vessel_residual_kernel(tc, tab_words, tab_scales, offs, w, e,
                         start=(a == 0 and (alone or t == 0)),
                         stop=(a == PASSES - 1 and (alone or t == PACK - 1)),
                     )
-
-        def room(j):
-            return (5 * j + 1 + 2 * (j >= LEAD)) * STEP
 
         acts = {}
         h_rows = {}
@@ -298,9 +304,9 @@ def tile_list_tied_vessel_residual_kernel(tc, tab_words, tab_scales, offs, w, e,
                 in_=h_rows[j][:].rearrange("p (t c x) -> p c t x", t=PACK, x=LINE),
             )
             if j >= LEAD - 1:
-                homes[(LEAD - 1, j - 2)] = placed(f"step2_{j}", [P, PIECE], F32, room(j))[:]
+                homes[(LEAD - 1, j - 2)] = placed(f"step2_{j}", [P, PIECE], F32, room(j) - (j == END) * STEP // 2)[:]
                 if j == END:
-                    homes[(0, j)] = placed(f"step0_{j}", [P, PIECE], F32, room(j) + STEP)[:]
+                    homes[(0, j)] = placed(f"step0_{j}", [P, PIECE], F32, room(j) + STEP // 2)[:]
             h_w[j] = held(f"h_w{j}", [P, PIECE], U32)
             if j == 1:
                 h_s[j] = placed(f"h_s{j}", [P, PIECE], U8, 43 * STEP // 4)
@@ -386,8 +392,6 @@ def tile_list_tied_vessel_residual_kernel(tc, tab_words, tab_scales, offs, w, e,
         gelu(0)
         scale_h(0)
         gather(0, 0, AHEAD[0])
-        first_col = bank([P, P], "vec")
-        nc.tensor.transpose(first_col[:], first_row[:], ident[:])
         h_in[0] = placed("h_in0", [P, PIECE * PACK], BF16, 4 * P)
         mid_picks = placed("mid_picks", [P, AHEAD[1]], F32, 0)
         nc.vector.tensor_copy(
@@ -411,16 +415,15 @@ def tile_list_tied_vessel_residual_kernel(tc, tab_words, tab_scales, offs, w, e,
                 homes[(1, 1)] = placed("step1_1", [P, PIECE], F32, 65 * STEP // 4)[:]
             if m == 1 and j < END:
                 weave(j + 1)
-            if (m, j) == (2, 0):
-                negate(minus_d[:, 2:4], first_col[:, 0:2])
-            if (m, j) == (LEAD, 0):
+            if (m, j) == (1, END):
                 turn_w(1)
                 quantize_turned(1)
+            if (m, j) == (LEAD, 0):
                 later_cols = bank([P, P], "vec")
                 nc.tensor.transpose(later_cols[:], minus_rows[:], ident[:])
                 nc.scalar.copy(out=minus_d[:, 4:6], in_=later_cols[:, 0:2])
                 nc.scalar.copy(out=minus_d[:, 6:TILES], in_=later_cols[:, QUAD : QUAD + 2])
-            if m >= 2 and j == 0:
+            if m >= 4 and j == 0:
                 lay_heads(m, minus_d[:, m : m + 1], nc.scalar.copy)
             beat(m, j)
         for half in range(S // BANK):

from contextlib import ExitStack

import concourse.mybir as mybir
from concourse.masks import make_identity

K, H, T, S = 1024, 512, 2048, 1024
FLOPS = 2 * S * (K * H + H * K + K * K)

F32 = mybir.dt.float32
BF16 = mybir.dt.bfloat16
I32 = mybir.dt.int32
U32 = mybir.dt.uint32
U16 = mybir.dt.uint16
U8 = mybir.dt.uint8
FP8X4 = mybir.dt.float8_e4m3fn_x4
FP4X4 = mybir.dt.float4_e2m1fn_x4
ACT = mybir.ActivationFunctionType
ADD = mybir.AluOpType.add

P = 128
PACK = 4
K_PASS = P * PACK
PASSES = K // K_PASS
BANK = 512
TILES = K // P
TILES_A_PASS = K_PASS // P
GROUP = 16
QUADS = 4
QUAD = P // QUADS
LIVE = 4
RUN = 8
LINE = 4
PIECE = 128
PIECES = S // PIECE
LEAD = 3
LAST = TILES - 1
END = PIECES - 1
STEP = 4 * PIECE
EARLY = 3 * PIECE
SHARE = (3, 2)
AHEAD = (384, 128, 384)


def tile_list_tied_vessel_residual_kernel(tc, tab_words, tab_scales, offs, w, e, w4_words, w4_scales, gT, d, out):
    nc = tc.nc
    with ExitStack() as ctx:
        keep = ctx.enter_context(tc.tile_pool(name="keep", bufs=1))
        lane = ctx.enter_context(tc.tile_pool(name="lane", bufs=1))
        psum = ctx.enter_context(tc.psum_pool(name="psum", bufs=1))

        def held(name, shape, dtype, on=None):
            return keep.tile(shape, dtype, name=name, tag=on or name, align_bytes=64)

        def placed(name, shape, dtype, offset):
            return lane.tile(shape, dtype, name=name, tag=name, align_bytes=64, offset=offset)

        def bank(shape, tag):
            return psum.tile(shape, F32, name="sums", tag=tag, bufs=1)

        offsets = held("offsets", [P, S // GROUP], U16)
        tab_s = held("tab_s", [P, T], U8)
        tab_w = [held(f"tab_w{a}", [P, T], I32) for a in range(PASSES)]
        w_raw = [held(f"w_raw{a}", [P, PACK * H], F32) for a in range(PASSES)]
        state = [held(f"state{m}", [P, T], F32) for m in range(TILES)]
        picks = held("picks", [P, TILES * S], F32)
        w4_parts = [(0, LEAD), (LEAD, TILES)]
        w4_w = [held(f"w4_w{first}", [P, PASSES, 2 * (last - first) * P], U8) for first, last in w4_parts]
        w4_s = [held(f"w4_s{first}", [P, PASSES, (last - first) * P], U8) for first, last in w4_parts]
        e_line = held("e_line", [1, H], F32)
        vec_rows = held("vec_rows", [P, H], F32)
        ident = held("ident", [P, P], F32)
        v_w = [held(f"v_w{a}", [P, S], U32) for a in range(PASSES)]
        v_rows = placed("v_rows", [P, S], U8, STEP // 2)
        v_s = [held(f"v_s{a}", [P, S], U8) for a in range(PASSES)]
        enc_in = [held(f"enc_in{a}", [P, H * PACK], BF16) for a in range(PASSES)]
        enc_s = [held(f"enc_s{a}", [P, H], U8) for a in range(PASSES)]
        enc_w = [held(f"enc_w{a}", [P, H], U32) for a in range(PASSES)]
        dec_in = {}
        dec_s = {}
        dec_w = [held(f"dec_w{a}", [P, K_PASS], U32) for a in range(PASSES)]
        h_w = {}
        h_s = {}
        minus_d = held("minus_d", [P, TILES], F32)
        first_d = held("first_d", [P, 1], F32, on="h_in1")
        later_rows = placed("later_rows", [P, P], F32, 63 * STEP // 4)
        second_row = placed("second_row", [P, P], F32, 21 * STEP // 2)
        minus_rows = held("minus_rows", [P, P], F32)
        e_cols = held("e_cols", [P, PACK], F32)
        warm = held("warm", [P, 1], F32)

        nc.vector.memset(vec_rows[:], 0.0)
        nc.vector.memset(minus_rows[:], 0.0)
        nc.vector.memset(tab_s[QUAD : 2 * QUAD, :].bitcast(I32), 0)
        nc.vector.memset(tab_s[2 * QUAD : P, :].bitcast(I32), 0)
        make_identity(nc, ident[:])

        nc.scalar.activation(out=warm[:], in_=vec_rows[:, H - 1 : H], func=ACT.Gelu_apprx_tanh)

        def listed(window, first, count):
            return window.indirect(offsets[:, first // GROUP : (first + count) // GROUP])

        def load_table(a):
            nc.sync.dma_start(out=tab_w[a][:], in_=tab_words[a].rearrange("p t i -> p (t i)").bitcast(I32))

        def load_w(a):
            rows = w[a * K_PASS : (a + 1) * K_PASS, :]
            nc.sync.dma_start(out=w_raw[a][:], in_=rows.rearrange("(p i) r -> p (i r)", i=PACK))

        def load_state(m):
            nc.sync.dma_start(out=state[m][:], in_=gT[m * P : (m + 1) * P, :])

        def load_w4(part):
            first, last = w4_parts[part]
            for q in range(QUADS):
                nc.sync.dma_start(
                    out=w4_s[part][QUAD * q : QUAD * q + LIVE, :, :].bitcast(I32),
                    in_=w4_scales[:, LIVE * q : LIVE * (q + 1), first * P : last * P].rearrange("a j n -> j a n").bitcast(I32),
                )
            rows = w4_words.rearrange("a p c -> p a c")
            nc.sync.dma_start(out=w4_w[part][:].bitcast(I32), in_=rows[:, :, 2 * first * P : 2 * last * P].bitcast(I32))

        def move_rows(a, q, first, last):
            row = LIVE * (QUADS * a + q)
            nc.sync.dma_start(
                out=v_s[a][QUAD * q : QUAD * q + LIVE, first:last].bitcast(I32),
                in_=v_rows[row : row + LIVE, first:last].bitcast(I32),
            )

        def move_plane(a):
            for q in range(QUADS):
                move_rows(a, q, 0, EARLY if (a, q) == (1, QUADS - 1) else S)

        def quantize(codes, scales, grouped):
            nc.vector.quantize_mx(out=codes.bitcast(FP8X4), scales=scales, in_=grouped)

        def cast_on_vector(a, first, last):
            nc.vector.tensor_copy(
                enc_in[a][:].rearrange("p (t g s i) -> p g t s i", t=PACK, s=RUN, i=PACK)[:, :, first:last],
                w_raw[a][:].rearrange("p (i g t s) -> p g t s i", i=PACK, t=PACK, s=RUN)[:, :, first:last],
            )

        def cast_on_scalar(a, t):
            target = enc_in[a][:].rearrange("p (t g z x i) -> p t g z i x", t=PACK, z=RUN // LINE, x=LINE, i=PACK)
            source = w_raw[a][:].rearrange("p (i g t z x) -> p t g z i x", i=PACK, t=PACK, z=RUN // LINE, x=LINE)
            nc.scalar.copy(out=target[:, t], in_=source[:, t])

        def room(j):
            return (5 * j + 1 + 2 * (j >= LEAD)) * STEP

        def turn_w(a):
            if a == 0:
                dec_in[a] = held(f"dec_in{a}", [P, K_PASS * PACK], BF16)
            else:
                dec_in[a] = placed(f"dec_in{a}", [P, K_PASS * PACK], BF16, room(END) + 3 * STEP // 2)
            words = enc_in[a][:].bitcast(F32).rearrange("p (t c u) -> p t c u", t=PACK, u=2)
            target = dec_in[a][:].rearrange("c (p u x t) -> c p u x t", u=2, x=2, t=PACK)
            for u in range(2):
                turned = bank([P, PACK, P], f"x{u}")
                for t in range(PACK):
                    nc.tensor.transpose(turned[:, t, :], words[:, t, :, u], ident[:])
                pairs = turned[:].rearrange("c t p -> c (t p)").bitcast(BF16)
                nc.scalar.copy(out=target[:, :, u, :, :], in_=pairs.rearrange("c (t p x) -> c p x t", t=PACK, x=2))

        def quantize_turned(a):
            dec_s[a] = held(f"dec_s{a}", [P, K_PASS], U8, on="w_raw1" if a == 0 else None)
            quantize(dec_w[a][:], dec_s[a][:], dec_in[a][:])

        nc.sync.dma_start(offsets[:], offs)
        nc.sync.dma_start(out=tab_s[0:QUAD, :].bitcast(I32), in_=tab_scales.rearrange("a j t -> (a j) t").bitcast(I32))
        nc.vector.tensor_copy(v_rows[:], tab_s[:].indirect(offsets[:]))
        load_table(0)
        nc.sync.dma_start(out=e_line[:], in_=e.rearrange("(o r) -> o r", o=1))
        d_rows = d.rearrange("(m p) -> m p", p=P)
        nc.sync.dma_start(out=vec_rows[1:5, 0:P], in_=d_rows[0:4])
        load_w(0)
        load_table(1)
        move_plane(0)
        load_w(1)
        move_plane(1)
        load_state(0)
        move_rows(1, QUADS - 1, EARLY, S)
        load_w4(0)
        load_state(1)
        nc.sync.dma_start(out=second_row[0:2, :], in_=d_rows[4:6])
        load_state(2)
        nc.sync.dma_start(out=later_rows[QUAD : QUAD + 2, :], in_=d_rows[6:TILES])
        load_state(3)
        load_w4(1)
        for m in range(LEAD + 1, TILES):
            load_state(m)

        first_wave = [(m, j - m // 2) for j in range(PIECES) for m in range(LEAD) if j >= m // 2]
        later = sorted((m + j, -m, j) for m, j in [(LEAD - 1, 2)] + [(m, j) for m in range(LEAD, LAST) for j in range(PIECES)])
        beats = first_wave + [(-back, END if -back < LEAD else j) for turn, back, j in later]
        spare = [(1, 0, 2), None, (2, 0, 1), (0, END, 1)] + [(3, j, 1) for j in range(6)]
        spare += [(4, 0, 1), (5, 0, 1), (3, 6, 1), (6, 0, 1), (3, 7, 1)] + [(LAST, j, 1) for j in range(6)] + [(LAST, 6, 2)]
        follower = {}
        for b, (m, j) in enumerate(beats[:-1]):
            before = beats[b - 1] if b > 0 else (0, 0)
            if before == (LAST - 1, END - 2):
                follower[(m, j)] = (before[0], before[1] + 1, 2)
            elif before[0] not in (0, LEAD) and before[1] < END and before not in ((1, 0), (LAST - 1, END - 1)):
                follower[(m, j)] = (before[0], before[1] + 1, 1)
            else:
                follower[(m, j)] = spare.pop(0)
        assert not spare

        nc.scalar.copy(
            out=vec_rows[0:1, :].rearrange("o (t g s) -> o t g s", t=PACK, s=RUN),
            in_=e_line[:].rearrange("o (g t s) -> o t g s", t=PACK, s=RUN),
        )
        vec_cols = bank([P, PACK, P], "vec")
        for t in range(PACK):
            nc.tensor.transpose(vec_cols[:, t, :], vec_rows[:, t * P : (t + 1) * P], ident[:])
        nc.scalar.copy(out=e_cols[:], in_=vec_cols[:, :, 0])
        heads = picks[:].rearrange("p (m j x) -> p m j x", m=TILES, x=PIECE)[:, :, :, 0]

        def negate(target, source):
            nc.scalar.activation(out=target, in_=source, func=ACT.Copy, scale=-1.0)

        runs = []
        for host, tile, piece in sorted((m, one[0], one[1]) for (m, j), one in follower.items() if one and (m, j) != (0, 0)):
            if runs and runs[-1][:2] == [host, tile] and runs[-1][3] == piece:
                runs[-1][3] = piece + 1
            else:
                runs.append([host, tile, piece, piece + 1])

        def lay_heads(m, column, write):
            for host, tile, first, last in runs:
                if host == m:
                    write(heads[:, tile, first:last], column.to_broadcast([P, last - first]))

        negate(first_d[:], vec_cols[:, 0, 1:2])
        negate(minus_d[:, 0:4], vec_cols[:, 0, 1:5])
        for m in range(4):
            lay_heads(m, vec_cols[:, 0, 1 + m : 2 + m], negate)

        nc.vector.tensor_copy(v_w[0][:], tab_w[0][:].bitcast(U32).indirect(offsets[:]))
        cast_on_vector(0, 0, SHARE[0])
        for t in range(SHARE[0], PACK):
            cast_on_scalar(0, t)
        quantize(enc_w[0][:], enc_s[0][:], enc_in[0][:])
        nc.vector.tensor_copy(v_w[1][:], tab_w[1][:].bitcast(U32).indirect(offsets[:]))
        turn_w(0)
        for t in range(PACK):
            if t < SHARE[1]:
                cast_on_vector(1, t, t + 1)
            else:
                cast_on_scalar(1, t)
        for t in range(PACK):
            units = slice(t * P, (t + 1) * P)
            quantize(enc_w[1][:, units], enc_s[1][:, units], enc_in[1][:, t * K_PASS : (t + 1) * K_PASS])
        quantize_turned(0)

        def encode(j, places, alone):
            entries = slice(j * PIECE, (j + 1) * PIECE)
            for a in range(PASSES):
                for t in range(PACK):
                    units = slice(t * P, (t + 1) * P)
                    nc.tensor.matmul_mx(
                        out=places[t],
                        lhsT=enc_w[a][:, units].bitcast(FP8X4),
                        lhsT_scale=enc_s[a][:, units],
                        rhs=v_w[a][:, entries].bitcast(FP8X4),
                        rhs_scale=v_s[a][:, entries],
                        start=(a == 0 and (alone or t == 0)),
                        stop=(a == PASSES - 1 and (alone or t == PACK - 1)),
                    )

        acts = {}
        h_rows = {}
        h_in = {}
        homes = {}

        def gelu(j):
            if j == 0:
                places = [bank([P, PIECE], f"a{t}")[:] for t in range(PACK)]
            else:
                shared = bank([P, PACK, PIECE], f"x{j % 2}")
                places = [shared[:, t, :] for t in range(PACK)]
            encode(j, places, j == 0)
            if j < LEAD:
                acts[j] = held(f"acts{j}", [P, PACK * PIECE], F32)
            else:
                acts[j] = placed(f"acts{j}", [P, PACK * PIECE], F32, room(j - 1) + STEP)
            for t in range(PACK):
                nc.scalar.activation(out=acts[j][:, t * PIECE : (t + 1) * PIECE], in_=places[t], func=ACT.Gelu_apprx_tanh, scale=e_cols[:, t : t + 1])

        def scale_h(j):
            if j < LEAD - 1:
                h_rows[j] = held(f"h_rows{j}", [P, PACK * PIECE], BF16)
            else:
                h_rows[j] = placed(f"h_rows{j}", [P, PACK * PIECE], BF16, room(j))
            for t in range(PACK):
                own = slice(t * PIECE, (t + 1) * PIECE)
                nc.scalar.activation(out=h_rows[j][:, own], in_=acts[j][:, own], func=ACT.Copy, scale=e_cols[:, t : t + 1])
            if j >= LEAD:
                homes[(1, j - 1)] = placed(f"step1_{j}", [P, PIECE], F32, room(j - 1) + 2 * STEP)[:]

        def weave(j):
            h_in[j] = held(f"h_in{j}", [P, PIECE * PACK], BF16)
            nc.scalar.copy(
                out=h_in[j][:].rearrange("p (c x t) -> p c t x", x=LINE, t=PACK),
                in_=h_rows[j][:].rearrange("p (t c x) -> p c t x", t=PACK, x=LINE),
            )
            if j >= LEAD - 1:
                homes[(LEAD - 1, j - 2)] = placed(f"step2_{j}", [P, PIECE], F32, room(j) - (j == END) * STEP // 2)[:]
                if j == END:
                    homes[(0, j)] = placed(f"step0_{j}", [P, PIECE], F32, room(j) + STEP // 2)[:]
            h_w[j] = held(f"h_w{j}", [P, PIECE], U32)
            if j == 1:
                h_s[j] = placed(f"h_s{j}", [P, PIECE], U8, 43 * STEP // 4)
            elif j == 2:
                h_s[j] = placed(f"h_s{j}", [P, PIECE], U8, 16 * STEP)
            else:
                h_s[j] = held(f"h_s{j}", [P, PIECE], U8)
            quantize(h_w[j][:], h_s[j][:], h_in[j][:])

        def decode(m, first, count, tag):
            half, place = divmod(m, TILES_A_PASS)
            own = slice(place * P, (place + 1) * P)
            part = 0 if m < LEAD else 1
            col = (m - w4_parts[part][0]) * P
            y = bank([P, count], tag)
            entries = slice(first, first + count)
            for a in range(PASSES):
                nc.tensor.matmul_mx(
                    out=y[:],
                    lhsT=w4_w[part][:, a, 2 * col : 2 * (col + P)].bitcast(FP4X4),
                    lhsT_scale=w4_s[part][:, a, col : col + P],
                    rhs=v_w[a][:, entries].bitcast(FP8X4),
                    rhs_scale=v_s[a][:, entries],
                    start=(a == 0),
                    stop=False,
                )
            for at in range(0, count, PIECE):
                j = (first + at) // PIECE
                nc.tensor.matmul_mx(
                    out=y[:, at : at + PIECE],
                    lhsT=dec_w[half][:, own].bitcast(FP8X4),
                    lhsT_scale=dec_s[half][:, own],
                    rhs=h_w[j][:].bitcast(FP8X4),
                    rhs_scale=h_s[j][:],
                    start=False,
                    stop=(at + PIECE == count),
                )
            return y

        steps = [held(f"steps{z}", [P, 2 * S], F32, on={0: "w_raw0", 3: "tab_w0"}.get(z)) for z in range(TILES // 2)]
        late = sum(AHEAD[:2])

        def picked(m, first, count):
            if m == 0 and late <= first < sum(AHEAD):
                return late_picks[:, first - late : first - late + count]
            if m == 0 and AHEAD[0] <= first < late:
                return mid_picks[:, first - AHEAD[0] : first - AHEAD[0] + count]
            return picks[:, m * S + first : m * S + first + count]

        def step_of(m, first, count):
            at = (m % 2) * S + first
            return homes.get((m, first // PIECE), steps[m // 2][:, at : at + count])

        def gather(m, first, count):
            nc.vector.tensor_copy(picked(m, first, count), listed(state[m][:], first, count))

        def scatter(m, first, count):
            nc.vector.tensor_tensor(listed(state[m][:], first, count), picked(m, first, count), step_of(m, first, count), ADD)
            if first + count == S:
                nc.sync.dma_start(out=out[m * P : (m + 1) * P, :], in_=state[m][:])

        turns = []

        def beat(m, j):
            behind = follower.get((m, j))
            if (m, j) == (0, 0):
                scale, tag = first_d[:], "x1"
            else:
                scale = heads[:, behind[0], behind[1] : behind[1] + 1] if behind else minus_d[:, m : m + 1]
                if m == 0 and j < END:
                    tag = f"x{(j + 1) % 2}"
                elif (m, j) == (2, 0):
                    tag = f"a{(len(turns) - 1) % 2}"
                else:
                    tag = f"a{len(turns) % 2}"
                    turns.append((m, j))
            y = decode(m, j * PIECE, PIECE, tag)
            nc.scalar.activation(out=step_of(m, j * PIECE, PIECE), in_=y[:], func=ACT.Copy, scale=scale)
            scatter(m, j * PIECE, PIECE)
            if behind:
                gather(behind[0], behind[1] * PIECE, behind[2] * PIECE)

        gelu(0)
        scale_h(0)
        gather(0, 0, AHEAD[0])
        h_in[0] = placed("h_in0", [P, PIECE * PACK], BF16, 4 * P)
        mid_picks = placed("mid_picks", [P, AHEAD[1]], F32, 0)
        nc.vector.tensor_copy(
            h_in[0][:].rearrange("p (c t) -> p c t", t=PACK), h_rows[0][:].rearrange("p (t c) -> p c t", t=PACK)
        )
        gather(0, AHEAD[0], AHEAD[1])
        h_w[0] = held("h_w0", [P, PIECE], U32)
        h_s[0] = held("h_s0", [P, PIECE], U8)
        quantize(h_w[0][:], h_s[0][:], h_in[0][:])
        late_picks = held("late_picks", [P, AHEAD[2]], F32, on="h_rows0")
        gather(0, late, AHEAD[2])
        for m, j in beats:
            if m == 0 and j < END:
                gelu(j + 1)
                scale_h(j + 1)
            if (m, j) == (1, 0):
                negate(minus_rows[0:2, :], second_row[0:2, :])
                homes[(1, 0)] = placed("step1_0", [P, PIECE], F32, 39 * STEP // 4)[:]
            if (m, j) == (1, 1):
                negate(minus_rows[QUAD : QUAD + 2, :], later_rows[QUAD : QUAD + 2, :])
                homes[(1, 1)] = placed("step1_1", [P, PIECE], F32, 65 * STEP // 4)[:]
            if m == 1 and j < END:
                weave(j + 1)
            if (m, j) == (1, END):
                turn_w(1)
                quantize_turned(1)
            if (m, j) == (LEAD, 0):
                later_cols = bank([P, P], "vec")
                nc.tensor.transpose(later_cols[:], minus_rows[:], ident[:])
                nc.scalar.copy(out=minus_d[:, 4:6], in_=later_cols[:, 0:2])
                nc.scalar.copy(out=minus_d[:, 6:TILES], in_=later_cols[:, QUAD : QUAD + 2])
            if m >= 4 and j == 0:
                lay_heads(m, minus_d[:, m : m + 1], nc.scalar.copy)
            beat(m, j)
        for half in range(S // BANK):
            y = decode(LAST, half * BANK, BANK, f"a{half}")
            nc.scalar.activation(out=step_of(LAST, half * BANK, BANK), in_=y[:], func=ACT.Copy, scale=minus_d[:, LAST:TILES])
        scatter(LAST, 0, S)
